import numpy as np, ml_dtypes
CORES = [9,25,41,57]
N = 4
import mx_ref
BF = ml_dtypes.bfloat16
def entries(a):
    return np.ascontiguousarray(a.T).reshape(-1)
def table(e):
    return np.ascontiguousarray(np.reshape(e, (-1, 16)).T).astype(np.int32)
def gcols(t, e):
    v = np.concatenate([t.reshape(8, 16, -1, 4), np.zeros((8, 16, 1, 4), BF)], axis=2)
    return np.ascontiguousarray(np.stack([v[g][:, e[g]] for g in range(8)])).reshape(128, -1)
def cols(t, e):
    v = np.concatenate([t.reshape(128, -1, 4), np.zeros((128, 1, 4), BF)], axis=1)
    return np.ascontiguousarray(v[:, e]).reshape(128, -1)
def tile(rs):
    return np.stack(rs, axis=2).reshape(128, -1).astype(BF)
def cut(t, i, w=512):
    return t[:, w * i:w * i + w]
def pick(q, e):
    c = np.concatenate([q[0].reshape(128, -1, 4), np.zeros((128, 1, 4), np.uint8)], axis=1); s = np.concatenate([q[1], np.ones((16, 1), np.uint8)], axis=1)
    return (np.ascontiguousarray(c[:, e].reshape(128, -1)), np.ascontiguousarray(s[:, e]))
def join(*qs):
    return (np.concatenate([q[0] for q in qs], axis=1), np.concatenate([q[1] for q in qs], axis=1))
def put(q, e, v):
    c, s = q[0].reshape(128, -1, 4).copy(), q[1].copy(); c[:, e] = v[0].reshape(128, -1, 4); s[:, e] = v[1]
    return (c.reshape(128, -1), s)
def pk(c, s):
    return (np.ascontiguousarray(c), mx_ref.live(s))
def emit(q):
    return q[0], q[1]
def packed(v, rng):
    q = [mx_ref.quantize(np.ascontiguousarray(v[r])) for r in range(N)]
    return np.stack([a for a, b in q]), np.stack([mx_ref.plane(b, rng) for a, b in q])
def values_of_codes():
    e, c = np.zeros((128, 128, 4), np.float32), np.zeros((128, 2, 4), np.uint8)
    e[np.arange(128), np.arange(128), 0] = 1
    c[:127, :, 0] = np.arange(256).reshape(2, 128).T[:127]
    return mx_ref.matmul(mx_ref.quantize(e.reshape(128, 512).astype(BF)), (c.reshape(128, 8), np.full((16, 2), 127, np.uint8))).T.reshape(-1).astype(np.float64)
CODE_VALUE, SCALE_VALUE = values_of_codes(), 2.0 ** (np.arange(256) - 127.0)
def decode(q):
    return (CODE_VALUE[q[0]].reshape(16, 8, -1, 4) * SCALE_VALUE[q[1]][:, None, :, None] + 0.0).reshape(128, -1).astype(np.float32)
def f(rng, *shape):
    return mx_ref.flush((rng.standard_normal(shape, dtype=np.float32) * np.exp2(rng.integers(-2, 3, shape[:-1] + (1,)))).astype(BF))
def wide(rng, *shape, cols=0):
    v = rng.standard_normal(shape, dtype=np.float32) * np.exp2(rng.integers(-12, 13, shape)).astype(np.float32)
    if cols: v *= np.repeat(np.exp2(rng.integers(-cols, cols + 1, shape[:-2] + (1, shape[-1] // 4))) * (rng.random(shape[:-2] + (1, shape[-1] // 4)) > 0.0625), 4, axis=-1).astype(np.float32)
    return mx_ref.flush(v.astype(BF))
C, M, F, R = 320, 128, 4, 3
def order(p):
    return np.argsort(-(p[::16] + np.float32(0.0)), axis=1, kind="stable")
def rewrite(t, e, h):
    a, b = t.reshape(8, 16, -1, 4).copy(), h.reshape(8, 16, -1, 4)
    for g in range(8):
        c, j = np.unique(e[g], return_index=True)
        a[g][:, c] = b[g][:, j]
    return a.reshape(128, -1)
def big(v):
    v = v.astype(np.float32)
    v[np.abs(v) < np.float32(2.0 ** -16)] = 0
    return v.astype(BF)
def offsets(a):
    return np.stack([table(np.concatenate([k, np.full(16 - F, -1)])) for k in a])
def numbers_of(rng):
    return {"x": big(f(rng, N, 128, 4 * C)), "m": big(f(rng, N, 128, 4 * M)), "kap": offsets(rng.integers(0, C, (N, F))), "u": np.array(f(rng, N, 128, 512)), "v": np.array(f(rng, N, 128, 512))}
def layers(rng):
    return big(f(rng, N, 128, 2048)).reshape(N, 8, 16, 4, 8, 16, 4)
def weights(rng, w):
    c, p = packed(np.ascontiguousarray(w).reshape(N, 128, 2048), rng)
    return {"wc": c, "ws": p}
def setup_inputs(rng):
    return {**numbers_of(rng), **weights(rng, layers(rng))}
def setup_inputs_ties(rng):
    d = numbers_of(rng)
    e = rng.permutation(N)
    x, m = d["x"].reshape(N, 8, 16, C, 4), d["m"].reshape(N, 8, 16, M, 4)
    for r in range(N):
        k = np.zeros(C, int) if r == e[0] else rng.permutation(C) % 3
        i = np.zeros(M, int) if r == e[0] else rng.permutation(M) % 3
        a = x[r][:, :8, :3].copy()
        a[:, :, 2] = 0
        x[r][:, :8] = a[:, :, k]
        m[r][:, :8] = a[:, :, i]
    x[e[1]] = 0
    u = d["u"].reshape(N, 8, 16, 128, 4)
    u[:, :, 8:, ::16] = 0
    u[:, :, 8:, 1] = 0
    w = layers(rng)
    w[:, :, 8:, :, :, :8] = 0
    kap = offsets(rng.integers(0, C, (N, 2))[:, rng.permutation(4) % 2])
    return {"x": x.reshape(N, 128, 4 * C), "m": m.reshape(N, 128, 4 * M), "kap": kap, "u": u.reshape(N, 128, 512), "v": d["v"], **weights(rng, w)}
def near_part(rng, s, b, size):
    p = np.zeros((16, s.size, 4))
    p[0, :, 0] = b
    g = ((s[:, None] >> np.arange(8)) & 1) * np.exp2(np.arange(8) - 23.0) * size
    p[8], p[9] = g[:, :4], g[:, 4:]
    p[10:] = rng.integers(4, 8, (6, s.size, 4)) * 2.0 ** -20 * size
    return p
def setup_inputs_near(rng):
    d = numbers_of(rng)
    kind = rng.permutation(8)
    c = np.where(kind < 6, kind % 2 * 2.0 - 1.0, 0.0)
    x, m = np.zeros((N, 8, 16, C, 4), np.float32), np.zeros((N, 8, 16, M, 4), np.float32)
    upper = np.arange(C) // (C // 2)
    for r in range(N):
        for g in range(8):
            i = (np.arange(C) + rng.integers(C)) % C
            b, a = np.full(C, c[g]), np.full(M, c[g])
            if kind[g] < 4: b[rng.integers(C)] *= 2.0 ** 30
            if kind[g] == 7:
                i = i % (C // 2) * 2 + upper
                b, a = (8 + upper) * 2.0 ** -33, (8 + rng.integers(0, 2, M)) * 2.0 ** -33
            size = 1.0 if kind[g] < 6 else 2.0 ** -4
            x[r, g] = near_part(rng, (i + 1) // 2, b, size)
            m[r, g] = near_part(rng, rng.integers(0, C // 2 + 1, M), a, size)
            if kind[g] == 7:
                x[r, g, 1, :, 0] = 17 * 2.0 ** -33 - b
                m[r, g, 1, :, 0] = 17 * 2.0 ** -33 - a
    u = d["u"].reshape(N, 128, 128, 4)
    k = np.where(rng.permutation(N) < N // 2, 2.0 ** -30, 1.0).astype(np.float32).astype(BF)
    u[:, :, ::16] = 0
    u[:, :, 1] = 0
    for h in range(0, 128, 16):
        u[:, h, h, 0] = k
        u[:, h + 8:h + 10, h] = k[:, None, None]
    h = 16 * int(np.argmax(kind))
    u[:, h, h, 0] = (k.astype(np.float32) * np.float32(1.125)).astype(BF)
    u[:, h + 1, h, 0] = k
    sort = rng.permutation(np.array([0, 5, 6, 7, 1, 2, 3, 4])[:N])
    one = np.argsort(kind)[sort]
    a = rng.integers(0, C, (N, F))
    for r in range(N):
        h = 16 * int(one[r])
        u[r, h:h + 16, 1] = u[r, h:h + 16, h]
        if sort[r] in (0, 5, 6, 7): a[r] = np.insert(rng.permutation(3), int(rng.integers(1, 4)), C - 1)
    w = layers(rng)
    w[:, :, :10] = 0
    w[:, :, :, :, :, :10] = 0
    w[:, :, :, :, np.flatnonzero(kind > 5)] = 0
    return {"x": x.reshape(N, 128, 4 * C).astype(BF), "m": m.reshape(N, 128, 4 * M).astype(BF), "kap": offsets(a), "u": u.reshape(N, 128, 512), "v": d["v"], **weights(rng, w)}
def setup_inputs_huge(rng):
    d = numbers_of(rng)
    o = rng.permutation(N)
    t = {}
    for key, n in (("x", C), ("m", M)):
        c = np.stack([rng.permutation(n) % 2 * 2.0 - 1.0 for r in range(N)])
        c[o < N // 2] = -1
        z = rng.random((N, 128, n, 4))
        z[:, ::8, :, 0] = 0
        t[key] = np.where(c[:, None, :, None] < 0, -2.0 ** 30 * (1 - 0.125 * z), 2.0 ** 28 * (0.8 - 0.2 * z)).astype(np.float32).reshape(N, 128, 4 * n).astype(BF)
    u = d["u"].reshape(N, 128, 128, 4)
    s = np.stack([np.append(rng.permutation(8) % 2 * 2.0 - 1.0, o[r] % 2 * 2.0 - 1.0) for r in range(N)])
    a = (2.0 ** 30 * (1 - 0.0625 * rng.integers(0, 2, (N, 128, 9, 4))) * s[:, None, :, None]).astype(np.float32).astype(BF)
    u[:, :, ::16] = a[:, :, :8]
    u[:, :, 1] = a[:, :, 8]
    w = np.zeros((N, 128, 4, 128, 4), np.float32)
    i = np.arange(128)
    for b in range(4): w[:, i, b, i, b] = 16
    return {"x": t["x"], "m": t["m"], "kap": d["kap"], "u": u.reshape(N, 128, 512), "v": d["v"], **weights(rng, w.astype(BF))}
def setup_inputs_wrap(rng):
    d = numbers_of(rng)
    x, m = d["x"].astype(np.float32).reshape(N, 8, 16, C, 4), d["m"].astype(np.float32).reshape(N, 8, 16, M, 4)
    u = d["u"].reshape(N, 128, 128, 4)
    x[:, :, :11] = 0
    m[:, :, :11] = 0
    u[:, :, ::16] = 0
    u[:, :, 1] = 0
    a = np.stack([rng.permutation(np.array([0, 1, C // 2, C - 1])) for r in range(N)])
    a[rng.integers(N)] = C - 1
    q = rng.integers(0, C + 1, (N, 8, M))
    o = rng.permutation(N)
    for r in range(N):
        g = rng.permutation(8)
        q[r, g[0]] = 0
        q[r, g[1]] = C
        q[r, g[2]] = rng.permutation(C)[:M]
        q[r, g[3]] = rng.integers(C - 2, C + 1, M)
        q[r, g[4]] = (rng.integers(C) - a[r][rng.integers(0, F, M)]) % C
        x[r, g[2], 0, :, 0] = rng.integers(1, 8, C)
        m[r, g[2], 0, :, 0] = rng.integers(1, 8, M)
        u[r, 16 * g[2], 1, 0] = -1 if o[r] < N // 2 else 1
    for h in range(0, 128, 16): u[:, h + 8:h + 11, h] = 1
    for t, key in ((x, 2 * (C - np.argsort(rng.random((N, 8, C)), axis=2))), (m, 2 * (C - q) + rng.integers(0, 2, q.shape))):
        z = ((key[:, :, :, None] >> np.arange(12)) & 1) * np.exp2(np.arange(12.0))
        for i in range(3): t[:, :, 8 + i] = z[:, :, :, 4 * i:4 * i + 4]
    w = layers(rng)
    w[:, :, :11] = 0
    w[:, :, :, :, :, :11] = 0
    return {"x": x.reshape(N, 128, 4 * C).astype(BF), "m": m.reshape(N, 128, 4 * M).astype(BF), "kap": offsets(a), "u": u.reshape(N, 128, 512), "v": d["v"], **weights(rng, w)}
def setup_inputs_spread(rng):
    d = setup_inputs(rng)
    d["x"] = big(wide(rng, N, 128, 4 * C, cols=6))
    d["m"] = big(wide(rng, N, 128, 4 * M, cols=6))
    return d
def check_inputs(d):
    b = []
    for k in ("x", "m", "u", "v"):
        a = np.abs(d[k].astype(np.float32))
        if not (np.isfinite(a).all() and ((a == 0) | (a >= 2.0 ** -30) & (a <= 2.0 ** 30)).all()): b.append("a value of " + k)
    none, least, most = [emit(mx_ref.quantize(np.full((128, 16), k, np.float32).astype(BF)))[1][0, 0] for k in (0.0, 2.0 ** -30, 2.0 ** 30)]
    for r in range(N):
        k = entries(d["kap"][r])
        if ((k[:F] < 0) | (k[:F] >= C)).any(): b.append("an offset of kap")
        if (k[F:] != -1).any(): b.append("kap: an entry that means nothing isn't -1")
        if ((d["wc"][r] == 0x7F) | (d["wc"][r] == 0xFF)).any(): b.append("wc: a code that is no number")
        s = mx_ref.live(d["ws"][r])
        if ((s != none) & ((s < least) | (s > most))).any(): b.append("ws: a scale out of range")
    return b
def reference(x, m, kap, u, v, wc, ws):
    qu = [mx_ref.quantize(u[r]) for r in range(N)]
    lay = [pk(wc[r], ws[r]) for r in range(N)]
    disc, msg = [x[r] for r in range(N)], [m[r] for r in range(N)]
    ok = np.zeros((N, R, M), np.float32)
    for t in range(R):
        won = []
        for r in range(N):
            p = mx_ref.matmul(qu[r], mx_ref.quantize(disc[r]))
            s = mx_ref.matmul(qu[r], mx_ref.quantize(msg[r]))
            n = np.sum(p[::16][:, :, None] > s[::16][:, None, :], axis=1)
            c = (n[:, None, :] + entries(kap[r])[:F][None, :, None]) % C
            e = np.take_along_axis(order(p), c.reshape(8, F * M), axis=1)
            z = ((gcols(disc[r], e).astype(np.float32) + np.tile(msg[r], (1, F)).astype(np.float32)) * np.float32(0.5)).astype(BF)
            best = np.argmax(mx_ref.matmul(qu[r], mx_ref.quantize(z))[1].reshape(F, M) + np.float32(0.0), axis=0)
            i = best * M + np.arange(M)
            h = cols(z, i)
            disc[r] = rewrite(disc[r], e[:, i], h)
            ok[r, t] = best
            won.append(mx_ref.quantize(h))
        came = decode(join(*won))
        for r in range(N):
            o = (r - 1) % N
            n = cut(came, o, 4 * M)
            msg[r] = tile([np.maximum(mx_ref.matmul(pick(lay[r], np.arange(128 * b, 128 * b + 128)), won[o]), np.float32(0.0)) * np.float32(0.03125) + n[:, b::4] for b in range(4)])
    y = np.zeros((N, 128, C + M), np.float32)
    oc, osc = np.zeros((N, 128, 4 * C + 4 * M), np.uint8), np.zeros((N, 16, C + M), np.uint8)
    for r in range(N):
        q = mx_ref.quantize(np.concatenate([disc[r], msg[r]], axis=1))
        y[r] = mx_ref.matmul(mx_ref.quantize(v[r]), q)
        oc[r], osc[r] = emit(q)
    return {"y": y, "ok": ok, "oc": oc, "osc": osc}

@@ -1,0 +1,489 @@
+from concourse.mybir import dt, AluOpType, AxisListType, ActivationFunctionType
+
+C, M, F, R = 320, 128, 4, 3
+NI = C // 16
+BIG = 2.0 ** 96
+SEG = [8 * i * (i + 1) for i in range(9)]
+
+TILES = [(("d", 19, 18, 17), 320, 0), ((16, 15, 14, 13), 256, 320), ((12, 11, 10, 9), 192, 576),
+         ((8, 7, 6, 5), 128, 768), ((4, 3, 2, 1), 128, 896)]
+PAR = {
+    "pe": [0, 4, 3, 2, 1],
+    "srows": (16, 15, 14, 13, 12, 11),
+    "vsums": (1, 2, 3, 4),
+    "vmsg": (0, 2),
+    "cyc": 1.04, "fix": 55.0, "wake": 70.0, "ga": 1.56, "sca": 3.8,
+    "off": {'VZ00': 35, 'SsgWm': -35, 'Vpre': 44, 'SHp': 33, 'VRS3': 31, 'Vrk': -10, 'VQC1': 59, 'VX0': 34, 'GEt': 60,
+            'VL': 40, 'SRS19': -45, 'GsentQ2': 58, 'SRS9': 57, 'VQG': 5, 'VcI3': 54, 'Vd5': 42, 'VCT10': 60, 'VposA': 40,
+            'Vews': 31, 'Sn2': 10, 'VQC0': -26, 'VRS4': 22, 'Vrd': 10, 'GuI': 26, 'Gi16': 24, 'Vroff': -31, 'GkI': 5,
+            'VWm': -21, 'VQC2': -20, 'SA': 3, 'SK4': 54, 'VCT7': 28, 'VCT4': 36, 'PB2': -9, 'VY1': 37, 'VW2': -6,
+            'VCT5': 43, 'Vhf': 32, 'SysbQX': 16, 'VQC3': -47},
+}
+
+Q4, U8, BF, F32, I32, U16 = "float8_e4m3fn_x4", "uint8", "bfloat16", "float32", "int32", "uint16"
+SCRATCH = {"ps": ("psum", [128, 4096], F32)}
+for _d, _l in (
+        (BF, "Xt:1792 Xh:1280 Yt:512 Yh:512 Z:2048 ut:512 vt:512 CT:4096 FT:512 Et:2048 Gi:512 Gt:512 Ri:512 Rt:512 j16:320 Mk:320 "
+             "K16:320 keep:320 j4:256 Mk4:256 K4:256 Ai:576 A:576 iO:320 sg0:320 sg1:320 vg0:320 vg1:320 junk:3072 rd:320 o2:640 "
+             "d4:256 e4:256 erep:512 Hp:512 ew:128 d5:128 ews:128 EQ:576 st:576"),
+        (F32, "cF:8 cG:16 Lf:16 i16:32 RC:20 jc:8 dum:32 ti:32 tq:32 tc:32 nb:4 kF:16 dk:16 D16:16 D32:32 d1:320 W:320 d2:320 "
+              "W2:320 d3:128 Wm:128 RS:20 tr:60 n:8 pos:64 pre:16 okc:4 zi:8 hf:32 e1:32 e2:32 e3:32 Rr:512 ysb:448"),
+        (I32, "pI:16 cI:8 kI:16"),
+        (U16, "uL:8 L:16 roff:20 pof:64 zof0:64 zof1:64 ziu:8 hof:32 xof:32")):
+    for _e in _l.split():
+        SCRATCH[_e.split(":")[0]] = ("sbuf", [128, int(_e.split(":")[1])], _d)
+for _e in ("A:448 u:128 v:128 g:128 W:512 C:1024 F:128 E:512 G:128 R:128 Z0:512 Z1:512 Z2:512 H0:128 H1:128 H2:128 "
+           "L0:128 L1:128 L2:128").split():
+    SCRATCH["Q" + _e.split(":")[0]] = ("sbuf", [128, int(_e.split(":")[1])], Q4)
+    SCRATCH["S" + _e.split(":")[0]] = ("sbuf", [128, int(_e.split(":")[1])], U8)
+
+SEMAPHORES = ["cV", "cS", "cP", "cG", "lu", "lx0", "lx1", "lm", "lv", "lwc", "lws", "lk", "outh", "outg", "sent",
+              "arr0", "arr1", "arr2"]
+
+
+def build(g, core, T, topo):
+    Alu, Act = AluOpType, ActivationFunctionType
+    CYC, FIX, GA, SCA = PAR["cyc"], PAR["fix"], PAR["ga"], PAR["sca"]
+    rank = T.rank_of(core)
+    nxt = T.cores[(rank + 1) % len(T.cores)]
+    rid, pid = topo.addr(nxt)[0], topo.addr(nxt)[1]
+    mask = topo.mask(core, nxt)
+    ne = len(topo.engines(core, nxt))
+    ops = []
+    V, S, P, G, Y = g.vector, g.scalar, g.tensor, g, g.sync
+
+    def add(eng, fn, r, w, busy, lat=None, sem=None, n=16):
+        ops.append({"e": eng, "f": fn, "r": list(r), "w": list(w), "busy": busy, "lat": busy if lat is None else lat,
+                    "sem": sem, "n": n})
+
+    def cyc(n):
+        return FIX + n * CYC
+
+    def ps(b, a, z):
+        return T.ps[:, 512 * b + a:512 * b + z]
+
+    def ts(out, in0, s1, s2, op0, op1, r, w, n):
+        if op1 is None:
+            add("V", lambda: V.tensor_scalar(out, in0, s1, None, op0), r, w, cyc(n))
+        else:
+            add("V", lambda: V.tensor_scalar(out, in0, s1, s2, op0, op1), r, w, cyc(n))
+
+    def tt(out, in0, in1, op, r, w, n):
+        add("V", lambda: V.tensor_tensor(out, in0, in1, op), r, w, cyc(n))
+
+    def cp(out, in_, r, w, n):
+        add("V", lambda: V.tensor_copy(out, in_), r, w, cyc(n))
+
+    def scan(out, a, b, init, op0, op1, r, w, n):
+        add("V", lambda: V.tensor_tensor_scan(out, a, b, init, op0, op1), r, w, cyc(n))
+
+    def mset(ap, val, w, n):
+        add("V", lambda: V.memset(ap, val), [], w, cyc(n))
+
+    def quant(q, s, t, r, w, n):
+        add("V", lambda: V.quantize_mx(q, s, t), r, w, 20 + 0.27 * 4 * n)
+
+    def act(out, in_, fn, r, w, n, **kw):
+        add("S", lambda: S.activation(out, in_, fn, **kw), r, w, cyc(n) + (25 if "accum_out" in kw else 0))
+
+    def mm(out, a, sa, b, sb, r, w, n, start=True, stop=True):
+        add("P", lambda: P.matmul_mx(out, a, sa, b, sb, start, stop), r, w, (n + 16) * 1.25)
+
+    def iota(out, pat, base, cm, w, n, flt=True):
+        if flt:
+            add("G", lambda: G.iota(out, pat, base, cm, allow_small_or_imprecise_dtypes=True), [], w, 160 + 2 * n * CYC)
+        else:
+            add("G", lambda: G.iota(out, pat, base, cm), [], w, 160 + 2 * n * CYC)
+
+    def dma(q, out, in_, r, w, sem, lat=2200.0):
+        e = {"Y": Y, "S": S, "G": G}[q]
+        add(q, lambda: e.dma_start(out, in_), r, w, 100.0 if q != "G" else 700.0, lat, sem)
+
+    ID = Act.Identity
+
+    dma("Y", T.ut[:], T.u[:], [], ["ut"], "lu", 1900.0)
+    dma("S", T.Xt[:, 0:640], T.x[:, 0:640], [], ["X0"], "lx0", 2300.0)
+    dma("Y", T.Xt[:, 640:1280], T.x[:, 640:1280], [], ["X1"], "lx1", 2300.0)
+    dma("S", T.Yt[:], T.m[:], [], ["Y0", "Y1", "Y2", "Y3"], "lm", 2600.0)
+    quant(T.Qu[:], T.Su[:], T.ut[:], ["ut"], ["Qu"], 128)
+    dma("Y", T.QW[:].bitcast(dt.uint8), T.wc[:], ["Qu"], ["QW"], "lwc", 3500.0)
+    dma("Y", T.SW[:], T.ws[:], ["Qu"], ["SW"], "lws", 3500.0)
+    dma("Y", T.vt[:], T.v[:], ["Qu"], ["vt"], "lv", 3000.0)
+
+    iota(T.pI[:, 8:16], [[16, 8]], 0, 0, ["uI"], 8, flt=False)
+    cp(T.uL[:], T.pI[:, 8:16], ["uI"], ["uL"], 8)
+    iota(T.pI[:, 0:8], [[0, 8]], 0, 1, ["pI"], 8, flt=False)
+    for a, z, sh, an in [(0, 1, 0, 15), (1, 2, 4, 7), (2, 3, 2, 3), (3, 4, 0, 3), (4, 6, 0, 7), (6, 8, 3, 1)]:
+        ts(T.cI[:, a:z], T.pI[:, a:z], sh, an, Alu.logical_shift_right, Alu.bitwise_and, ["pI"], ["cI%d" % a], 1)
+    cp(T.cF[:], T.cI[:], ["cI%d" % c for c in (0, 1, 2, 3, 4, 6)], ["cF"], 8)
+    rc, gc_, r4, t4 = [T.cF[:, c:c + 1] for c in range(4)]
+    act(T.cG[:, 0:2], T.cF[:, 0:2], Act.Copy, ["cF"], ["neg"], 2, scale=-1.0)
+    nr, ng = T.cG[:, 0:1], T.cG[:, 1:2]
+    iota(T.j16[:], [[0, NI], [1, 16]], 0, 0, ["j16"], C)
+    ts(T.Mk[:], T.j16[:], rc, 0.5, Alu.is_equal, Alu.subtract, ["j16", "cF"], ["Mk"], C / 2)
+    ts(T.Mk[:], T.Mk[:], 2 * BIG, None, Alu.mult, None, ["Mk"], ["Mk"], C / 2)
+    act(T.keep[:], T.j16[:], Act.Sign, ["j16"], ["keep"], C)
+    act(T.K16[:], T.keep[:], ID, ["keep"], ["K16"], C, scale=2 * BIG, bias=-BIG)
+    for rows, width, first in TILES:
+        a, z = 4 * (first + 16 * rows[3]), 4 * (first + width)
+        mset(T.CT[:, a:z], 0.0, ["CT%s" % str(i) for i in rows], (z - a) / 2)
+    iota(T.Gi[:], [[1, 8], [0, 64]], 0, 0, ["Gi"], 512)
+    add("G", lambda: G.dma_start(T.kI[0:1, :], T.kap[:], allow_slow_non_contiguous=True), ["Gi"], ["kI"], 1500.0, 3000.0, "lk")
+    act(T.Gt[:], T.Gi[:], Act.Abs, ["Gi", "neg"], ["Gt"], 512, bias=ng)
+    act(T.Gt[:], T.Gt[:], Act.Relu, ["Gt"], ["Gt"], 512, bias=1.0, scale=-1.0)
+    quant(T.QG[:], T.SG[:], T.Gt[:], ["Gt"], ["QG"], 128)
+    iota(T.i16[:], [[16, 32]], 0, 0, ["i16"], 32)
+    act(T.cG[:, 2:3], rc, ID, ["cF"], ["cG2"], 1, scale=-1.0, bias=15.0)
+    act(T.RC[:], T.i16[:, 0:NI], ID, ["i16", "cG2"], ["RC"], NI, bias=T.cG[:, 2:3])
+    act(T.jc[:], T.i16[:, 0:8], ID, ["i16", "cF"], ["jc"], 8, bias=rc)
+    act(T.cG[:, 3:4], rc, ID, ["cF"], ["cG3"], 1, bias=float(4 * C))
+    act(T.dum[:], T.i16[:], ID, ["i16", "cG3"], ["dum"], 32, bias=T.cG[:, 3:4])
+    mset(T.RS[:, 0:1], 0.0, ["RS0"], 1)
+    iota(T.iO[:], [[4, C]], -2 * C, 0, ["iO"], C)
+    n4 = 256
+    iota(T.j4[:], [[0, n4 // 4], [1, 4]], 0, 0, ["j4"], n4)
+    ts(T.Mk4[:], T.j4[:], r4, 0.5, Alu.is_equal, Alu.subtract, ["j4", "cF"], ["Mk4"], n4 / 2)
+    ts(T.Mk4[:], T.Mk4[:], 2 * BIG, None, Alu.mult, None, ["Mk4"], ["Mk4"], n4 / 2)
+    act(T.K4[:], T.j4[:], Act.Sign, ["j4"], ["K4"], n4)
+    act(T.K4[:], T.K4[:], ID, ["K4"], ["K4"], n4, scale=2 * BIG, bias=-BIG)
+    L16a, L16b, L32, L32e, LEND, LF, LD16, LD32 = (T.L[:, 0:1], T.L[:, 2:3], T.L[:, 4:6], T.L[:, 6:8], T.L[:, 8:10],
+                                                   T.L[:, 10:12], T.L[:, 12:13], T.L[:, 14:16])
+    act(T.Lf[:, 0:2], T.cF[:, 3:5], Act.Copy, ["cF"], ["Lf0"], 2)
+    act(T.Lf[:, 2:4], T.cF[:, 3:5], ID, ["cF"], ["Lf2"], 2, bias=4.0)
+    act(T.Lf[:, 4:6], T.cF[:, 4:6], Act.Copy, ["cF"], ["Lf4"], 2)
+    act(T.Lf[:, 6:8], T.cF[:, 4:6], ID, ["cF"], ["Lf6"], 2, scale=16.0, bias=15.0)
+    act(T.cG[:, 4:6], T.cF[:, 4:6], Act.Square, ["cF"], ["cG4"], 2, bias=1.5)
+    act(T.Lf[:, 8:10], T.cG[:, 4:6], ID, ["cG4"], ["Lf8"], 2, scale=8.0, bias=-3.0)
+    ts(T.cG[:, 10:11], t4, 3.0, None, Alu.is_lt, None, ["cF"], ["cG10"], 1)
+    ts(T.cG[:, 6:7], t4, 5.0, T.cG[:, 10:11], Alu.add, Alu.mult, ["cF", "cG10"], ["cG6"], 1)
+    for c in range(2):
+        ts(T.cG[:, 8 + c:9 + c], r4, 4.0 * c, gc_, Alu.add, Alu.is_equal, ["cF"], ["cG8%d" % c], 1)
+        act(T.Lf[:, 14 + c:15 + c], T.cF[:, 6:7], ID, ["cF"], ["Lf14%d" % c], 1, bias=2.0 * c)
+    ts(T.Lf[:, 10:12], T.cG[:, 8:10], T.cG[:, 6:7], None, Alu.mult, None, ["cG80", "cG81", "cG6"], ["Lf10"], 2)
+    act(T.Lf[:, 12:14], T.cF[:, 2:4], Act.Copy, ["cF"], ["Lf12"], 2)
+    cp(T.L[:], T.Lf[:], ["Lf0", "Lf2", "Lf4", "Lf6", "Lf8", "Lf10", "Lf12", "Lf140", "Lf141"], ["L"], 16)
+    act(T.cG[:, 7:8], t4, ID, ["cF"], ["t640"], 1, bias=float(2 * C))
+    t640 = T.cG[:, 7:8]
+    cp(T.kF[0:1, :], T.kI[0:1, :], ["kI"], ["kF"], 16)
+    add("G", lambda: G.partition_broadcast(T.dk[:], T.kF[0:1, :], 128), ["kF"], ["dk"], 260.0)
+    act(T.D16[:], T.dk[:].indirect(LD16), Act.Copy, ["dk", "L"], ["D16"], 16 * GA)
+    act(T.D32[:], T.dk[:].indirect(LD32), Act.Copy, ["dk", "L"], ["D32"], 32 * GA)
+    iota(T.ti[:], [[1, 4], [0, 8]], 0, 0, ["ti"], 32)
+    act(T.tq[:], T.ti[:], Act.Copy, ["ti"], ["tq"], 32, scale=0.25)
+    act(T.tc[:], T.ti[:], ID, ["ti"], ["tc"], 32, bias=float(2 * C - 1))
+    mset(T.nb[:], -BIG, ["nb"], 4)
+    mset(T.pre[:], BIG, ["pre"], 8)
+    mset(T.FT[:], 0.0, ["FT"], 256)
+    iota(T.Ri[:], [[0, 8], [1, 16], [0, 4]], 0, 0, ["Ri"], 512)
+    act(T.Rt[:], T.Ri[:], Act.Abs, ["Ri", "neg"], ["Rt"], 512, bias=nr)
+    act(T.Rt[:], T.Rt[:], Act.Relu, ["Rt"], ["Rt"], 512, bias=float(M), scale=-float(M))
+    quant(T.QR[:], T.SR[:], T.Rt[:], ["Rt"], ["QR"], 128)
+    for i in range(8):
+        iota(T.Ai[:, SEG[i]:SEG[i + 1]], [[1, 16 * (i + 1)]], -16 * i, 0, ["Ai%d" % i], 16 * (i + 1))
+    act(T.A[:], T.Ai[:], Act.Abs, ["Ai%d" % i for i in range(8)] + ["neg"], ["A"], 576, bias=nr)
+    act(T.A[:], T.A[:], Act.Relu, ["A"], ["A"], 576, bias=4096.0, scale=-4096.0)
+    act(T.A[:], T.A[:], ID, ["A"], ["A"], 576, bias=1.0)
+    for i in range(1, 8):
+        iota(T.A[:, SEG[i]:SEG[i] + 1], [[0, 1]], 0, 0, ["A"], 1)
+    iota(T.Et[:], [[0, 2048]], 1, 0, ["Et"], 2048)
+    add("G", lambda: G.affine_select(T.Et[:], T.Et[:], [[-1, 4], [-16, 128], [1, 4]], Alu.is_equal, 0.0, 0, 16),
+        ["Et"], ["Et"], 210 + 4096 * CYC)
+    quant(T.QE[:], T.SE[:], T.Et[:], ["Et"], ["QE"], 512)
+
+    cp(T.Qg[:].bitcast(dt.uint32), T.Qu[:].bitcast(dt.uint32).indirect(T.uL[:]), ["Qu", "uL"], ["Qg"], 128 * GA)
+    act(T.Sg[:], T.Su[:].indirect(T.uL[:]), Act.Copy, ["Qu", "uL"], ["Sg"], 128 * GA)
+    quant(T.Qv[:], T.Sv[:], T.vt[:], ["vt"], ["Qv"], 128)
+
+    kX, kY = ["X0", "X1"], ["Y0", "Y1", "Y2", "Y3"]
+    kG = ["Qg", "Sg"]
+    t1, t2, rk = T.tr[:, 0:NI], T.tr[:, NI:2 * NI], T.tr[:, 2 * NI:3 * NI]
+
+    def quant_x():
+        quant(T.QA[:, 0:C], T.SA[:, 0:C], T.Xt[:, 0:4 * C], kX, ["QX"], C)
+
+    def quant_y():
+        quant(T.QA[:, C:C + M], T.SA[:, C:C + M], T.Yt[:], kY, ["QY"], M)
+
+    def new_y(t, rb, db):
+        q, s, k = T["QL%d" % t][:], T["SL%d" % t][:], "land%d" % t
+        for b in range(4):
+            mm(ps(rb[b], 0, M), T.QW[:, M * b:M * b + M], T.SW[:, M * b:M * b + M], q, s, ["QW", "SW", k], ["B%d" % rb[b]], M)
+            mm(ps(db[b], 0, M), T.QE[:, M * b:M * b + M], T.SE[:, M * b:M * b + M], q, s, ["QE", k], ["B%d" % db[b]], M)
+            act(T.Rr[:, M * b:M * b + M], ps(rb[b], 0, M), Act.Relu, ["B%d" % rb[b]], ["Rr%d" % b], M, scale=0.03125)
+            tt(T.Yt[:, b:512:4], T.Rr[:, M * b:M * b + M], ps(db[b], 0, M), Alu.add, ["Rr%d" % b, "B%d" % db[b]], ["Y%d" % b], M)
+
+    for t in range(R):
+        QZ, SZ, QH, SH = T["QZ%d" % t], T["SZ%d" % t], T["QH%d" % t], T["SH%d" % t]
+        quant_x()
+        mm(ps(0, 0, C), T.Qg[:], T.Sg[:], T.QA[:, 0:C], T.SA[:, 0:C], kG + ["QX"], ["B0"], C)
+        mm(ps(1, 0, C), T.Qg[:], T.Sg[:], T.QA[:, 0:C], T.SA[:, 0:C], kG + ["QX"], ["B1"], C)
+        act(T.Xh[:], T.Xt[:, 0:4 * C], Act.Copy, kX, ["Xh"], 4 * C, scale=0.5)
+        tt(T.d1[:], ps(0, 0, C), T.Mk[:], Alu.min, ["B0", "Mk"], ["d1"], C)
+        scan(T.W[:], T.K16[:], T.d1[:], -BIG, Alu.min, Alu.max, ["K16", "d1"], ["W"], C)
+        flip = [0, 0]
+        for rows, width, first in TILES:
+            for slot, i in enumerate(rows):
+                w = C if i == "d" else 16 * i
+                out = T.CT[:, 4 * first + slot:4 * (first + w):4]
+                key = "CT%s" % str(i)
+                if i == "d":
+                    tt(out, T.W[:], ps(0, 0, C), Alu.is_ge, ["W", "B0"], [key], C)
+                    scan(T.rd[:], T.keep[:], out, 0.0, Alu.mult, Alu.add, ["keep", key], ["rd"], C / 2)
+                    continue
+                own = T.W[:, 16 * i + 15:16 * i + 16]
+                if i in PAR["srows"]:
+                    sk = "sg%d" % flip[0]
+                    flip[0] ^= 1
+                    act(T[sk][:, 0:w], ps(1, 0, w), Act.Sign, ["B1", "W"], [sk], w, bias=own, scale=-1.0)
+                    act(out, T[sk][:, 0:w], Act.Relu, [sk], [key, "RS%d" % i], w, accum_out=T.RS[:, i:i + 1])
+                else:
+                    ts(out, ps(0, 0, w), own, None, Alu.is_lt, None, ["B0", "W"], [key], w)
+                    if i in PAR["vsums"]:
+                        add("V", lambda o=T.RS[:, i:i + 1], a=out: V.tensor_reduce(o, a, AxisListType.X, Alu.add),
+                            [key], ["RS%d" % i], cyc(w))
+                    else:
+                        a = 8 * i * (i - 1)
+                        act(T.junk[:, a:a + w], out, Act.Copy, [key], ["RS%d" % i], w, accum_out=T.RS[:, i:i + 1])
+        for z, u in enumerate(PAR["pe"]):
+            rows, width, first = TILES[u]
+            quant(T.QC[:, first:first + width], T.SC[:, first:first + width], T.CT[:, 4 * first:4 * (first + width)],
+                  ["CT%s" % str(i) for i in rows], ["QC%d" % u], width)
+            mm(ps(2, 0, width), T.QG[:], T.SG[:], T.QC[:, first:first + width], T.SC[:, first:first + width],
+               ["QG", "QC%d" % u], ["B2"], width, start=(z == 0), stop=(z == 4))
+        if t > 0:
+            new_y(t - 1, [4, 6, 4, 6], [5, 7, 5, 7])
+        quant_y()
+        act(T.Yh[:], T.Yt[:], Act.Copy, kY, ["Yh"], 512, scale=0.5)
+        mm(ps(3, 0, M), T.Qg[:], T.Sg[:], T.QA[:, C:C + M], T.SA[:, C:C + M], kG + ["QY"], ["B3"], M)
+        tt(T.d3[:], ps(3, 0, M), T.Mk[:, 0:M], Alu.min, ["B3", "Mk"], ["d3"], M)
+        scan(T.Wm[:], T.K16[:, 0:M], T.d3[:], -BIG, Alu.min, Alu.max, ["K16", "d3"], ["Wm"], M)
+        tt(t1, T.RC[:], T.rd[:, 15:C:16], Alu.subtract, ["RC", "rd"], ["t1"], 2 * NI)
+        tt(t2, t1, T.RS[:], Alu.subtract, ["t1"] + ["RS%d" % i for i in range(NI)], ["t2"], 2 * NI)
+        tt(T.d2[:], ps(2, 0, C), T.Mk[:], Alu.min, ["B2", "Mk"], ["d2"], C)
+        scan(T.W2[:], T.K16[:], T.d2[:], -BIG, Alu.min, Alu.max, ["K16", "d2"], ["W2"], C)
+        tt(rk, T.W2[:, 15:C:16], t2, Alu.add, ["W2", "t2"], ["rk"], 2 * NI)
+        cp(T.roff[:], rk, ["rk"], ["roff"], NI)
+        cp(T.o2[:, 0:C].indirect(T.roff[:]), T.iO[:], ["roff", "iO"], ["o2a"], C * SCA)
+        cp(T.o2[:, C:2 * C], T.o2[:, 0:C], ["o2a"], ["o2b"], C / 2)
+        for i in range(8):
+            own = T.Wm[:, 16 * i + 15:16 * i + 16]
+            if i in PAR["vmsg"]:
+                sk = "vg%d" % flip[1]
+                flip[1] ^= 1
+                ts(T[sk][:], ps(0, 0, C), own, None, Alu.is_gt, None, ["B0", "Wm"], [sk], C)
+                act(T[sk][:], T[sk][:], Act.Copy, [sk], ["n%d" % i, sk], C, accum_out=T.n[:, i:i + 1])
+            else:
+                sk = "sg%d" % flip[0]
+                flip[0] ^= 1
+                act(T[sk][:], ps(1, 0, C), Act.Sign, ["B1", "Wm"], [sk], C, bias=own, scale=-1.0)
+                act(T[sk][:], T[sk][:], Act.Relu, [sk], ["n%d" % i, sk], C, scale=-1.0, accum_out=T.n[:, i:i + 1])
+        for h in range(2):
+            zof, pos, pk = T["zof%d" % h], T.pos[:, 16 * h:16 * h + 16], "pof%d" % h
+            pof = T.pof[:, 16 * h:16 * h + 16]
+            tt(pos, T.n[:, 0:4 * h + 4].indirect(L16b if h else L16a), T.D16[:], Alu.add,
+               ["n%d" % i for i in range(4 * h + 4)] + ["L", "D16"], ["pos%d" % h], 16 * GA)
+            cp(pof, pos, ["pos%d" % h], [pk], 16)
+            tt(T.d4[:], T.o2[:].indirect(pof), T.Mk4[:], Alu.min, ["o2a", "o2b", pk, "Mk4"], ["d4"], n4 * GA)
+            scan(T.e4[:], T.K4[:], T.d4[:], -BIG, Alu.min, Alu.max, ["K4", "d4"], ["e4"], n4 / 2)
+            ts(zof[:], T.e4[:, 3:n4:4], t640, None, Alu.add, None, ["e4", "t640"], ["zof%d" % h], n4 / 4)
+            if h == 1:
+                tt(T.pos[:, 32:64], T.n[:].indirect(L32), T.D32[:], Alu.add, ["n%d" % i for i in range(8)] + ["L", "D32"], ["posA"], 32 * GA)
+                cp(T.pof[:, 32:64], T.pos[:, 32:64], ["posA"], ["pofA"], 32)
+                act(T.erep[:], T.o2[:].indirect(T.pof[:, 32:64]), Act.Copy, ["o2a", "o2b", "pofA"], ["erep"], 512 * GA)
+            for k in range(F):
+                a = 512 * k + n4 * h
+                tt(T.Z[:, a:a + n4], T.Xh[:].indirect(zof[:, 16 * k:16 * k + 16]), T.Yh[:, n4 * h:n4 * h + n4], Alu.add,
+                   ["Xh", "Yh", "zof%d" % h], ["Z%d%d" % (k, h)], n4 * GA)
+        for k in range(F):
+            quant(QZ[:, M * k:M * k + M], SZ[:, M * k:M * k + M], T.Z[:, 512 * k:512 * k + 512],
+                  ["Z%d0" % k, "Z%d1" % k], ["QZ%d_%d" % (t, k)], M)
+            mm(ps(4 + k, 0, M), QZ[:, M * k:M * k + M], SZ[:, M * k:M * k + M], T.Qu[:], T.Su[:],
+               ["QZ%d_%d" % (t, k), "Qu"], ["B%d" % (4 + k)], M)
+        kQZ = ["QZ%d_%d" % (t, k) for k in range(F)]
+        kZ = ["Z%d%d" % (k, h) for k in range(F) for h in range(2)]
+        scan(T.pre[:, 5:9], T.ps[:, 2049:4096:512], T.nb[:], -BIG, Alu.max, Alu.max, ["B4", "B5", "B6", "B7", "nb"], ["pre"], 4)
+        ts(T.FT[:, 0:32], T.pre[:, 0:8].indirect(LF), T.pre[:, 8:9], None, Alu.is_lt, None, ["pre", "L"], ["FT"], 32 * GA)
+        quant(T.QF[:], T.SF[:], T.FT[:], ["FT"], ["QF"], M)
+        mm(ps(3, 0, M), T.QR[:], T.SR[:], T.QF[:], T.SF[:], ["QR", "QF"], ["B3"], M)
+        tt(T.zi[:], ps(3, 0, 8), T.jc[:], Alu.add, ["B3", "jc"], ["zi"], 8)
+        cp(T.ziu[:], T.zi[:], ["zi"], ["ziu"], 8)
+        cp(QH[:].bitcast(dt.uint32), QZ[:].bitcast(dt.uint32).indirect(T.ziu[:]), kQZ + ["ziu"], ["QH%d" % t], M * GA)
+        act(SH[:], SZ[:].indirect(T.ziu[:]), Act.Copy, kQZ + ["ziu"], ["SH%d" % t], M * GA)
+        arr = T.sem["arr%d" % t]
+        add("G", lambda a=T["SL%d" % t][:], b=SH[:], s=arr: G.remote_dma(a, b, s, T.sem.sent, pid, rid, mask),
+            ["SH%d" % t], ["sentS%d" % t], 600.0, 2000.0, "remote")
+        add("G", lambda a=T["QL%d" % t][:].bitcast(dt.uint8), b=QH[:].bitcast(dt.uint8), s=arr:
+            G.remote_dma(a, b, s, T.sem.sent, pid, rid, mask), ["QH%d" % t], ["sentQ%d" % t], 600.0, 2600.0, "remote")
+        add("A", None, ["sentS%d" % t, "sentQ%d" % t], ["land%d" % t], 0.0, 0.0, "arr%d" % t, 2 * ne)
+        act(T.junk[:, 3040:3072], T.FT[:, 0:32], Act.Copy, ["FT"], ["okc%d" % t, "jk"], 32, accum_out=T.okc[:, t:t + 1])
+        dma("Y", T.ok[t], T.okc[:, t:t + 1], ["okc%d" % t], [], "outh")
+        act(T.ew[:], T.erep[:].indirect(T.ziu[:]), Act.Copy, ["erep", "ziu"], ["ew"], M * GA)
+        tt(T.hf[:], T.zi[:].indirect(L32), T.tq[:], Alu.add, ["zi", "tq", "L"], ["hf"], 32 * GA)
+        ts(T.hof[:], T.hf[:], 4.0, None, Alu.mult, None, ["hf"], ["hof"], 32)
+        act(T.Hp[:], T.Z[:].indirect(T.hof[:]), Act.Copy, kZ + ["hof"], ["Hp"], 512 * GA)
+        tt(T.d5[:], T.erep[:].indirect(T.ziu[:]), T.Mk[:, 0:M], Alu.min, ["erep", "ziu", "Mk"], ["d5"], M * GA)
+        scan(T.ews[:], T.K16[:, 0:M], T.d5[:], -BIG, Alu.min, Alu.max, ["K16", "d5"], ["ews"], M / 2)
+        for i in range(8):
+            w = 16 * (i + 1)
+            ts(T.EQ[:, SEG[i]:SEG[i + 1]], T.ew[:, 0:w], T.ews[:, w - 1:w], None, Alu.is_equal, None, ["ew", "ews"], ["EQ%d" % i], w / 2)
+        tt(T.e1[:], T.ews[:].indirect(L32e), T.tc[:], Alu.add, ["ews", "tc", "L"], ["e1"], 32 * GA)
+        scan(T.st[:], T.A[:], T.EQ[:], 0.0, Alu.mult, Alu.max, ["A"] + ["EQ%d" % i for i in range(8)], ["st"], 288)
+        tt(T.e2[:], T.st[:].indirect(LEND), T.e1[:], Alu.add, ["st", "e1", "L"], ["e2"], 32 * GA)
+        tt(T.e3[:], T.e2[:], T.dum[:], Alu.min, ["e2", "dum"], ["e3"], 64)
+        cp(T.xof[:], T.e3[:], ["e3"], ["xof"], 32)
+        cp(T.Xt[:].indirect(T.xof[:]), T.Hp[:], ["xof", "Hp"] + kX, kX, 512 * SCA)
+
+    new_y(R - 1, [4, 5, 6, 7], [0, 1, 2, 3])
+    quant_y()
+    quant_x()
+    for key, a, z, b in (("QY", C, C + M, 4), ("QX", 0, C, 5)):
+        mm(ps(b, 0, z - a), T.Qv[:], T.Sv[:], T.QA[:, a:z], T.SA[:, a:z], ["Qv", key], ["B%d" % b], z - a)
+        dma("Y", T.oc[:, 4 * a:4 * z], T.QA[:, a:z].bitcast(dt.uint8), [key], [], "outh")
+        act(T.ysb[:, a:z], ps(b, 0, z - a), Act.Copy, ["B%d" % b], ["ysb" + key], z - a)
+        dma("S", T.y[:, a:z], T.ysb[:, a:z], ["ysb" + key], [], "outh")
+    for k in range(4):
+        dma("G" if k == 3 else "Y", T.osc[4 * k:4 * k + 4, :], T.SA[32 * k:32 * k + 4, :], ["QX", "QY"], [],
+            "outg" if k == 3 else "outh")
+    return ops, ne
+
+
+def depend(ops):
+    writer, readers = {}, {}
+    for i, o in enumerate(ops):
+        d = set()
+        for k in o["r"]:
+            if k in writer:
+                d.add(writer[k])
+            if k[0] == "B" and len(k) == 2:
+                d.update(j for j in readers.get(k, []) if ops[j]["e"] != o["e"])
+        for k in o["w"]:
+            if k in writer:
+                d.add(writer[k])
+            d.update(readers.get(k, []))
+        d.discard(i)
+        o["d"] = sorted(d)
+        for k in o["r"]:
+            readers.setdefault(k, []).append(i)
+        for k in o["w"]:
+            writer[k] = i
+            readers[k] = []
+
+
+def name(o):
+    k = (o["w"] or o["r"])[0]
+    if k.startswith("sg") or k.startswith("vg"):
+        k = k[:2] + o["r"][1]
+    if k[:2] in ("QZ", "QH", "SH"):
+        k = k[:2] + k[3:]
+    return o["e"] + k
+
+
+def plan(ops):
+    n, WAKE, off = len(ops), PAR["wake"], PAR["off"]
+    level = [o["lat"] for o in ops]
+    key = [0.0] * n
+    low = [0.0] * n
+    for i in range(n - 1, -1, -1):
+        o = ops[i]
+        key[i] = max(level[i] + 100.0 * off.get(name(o), 0), low[i])
+        for j in o["d"]:
+            level[j] = max(level[j], level[i] + WAKE + ops[j]["lat"])
+            low[j] = max(low[j], key[i] + 1e-3)
+    line = {e: [] for e in "VSPGYA"}
+    for i in sorted(range(n), key=lambda i: (-key[i], i)):
+        o = ops[i]
+        t = 0.0
+        for j in o["d"]:
+            p = ops[j]
+            t = max(t, p["t0"] + p["lat"] + (0.0 if p["e"] == "P" and o["e"] == "P" else WAKE))
+        ln, d = line[o["e"]], o["busy"]
+        k = len(ln)
+        while k > 0 and ln[k - 1][1] > t:
+            k -= 1
+        while k < len(ln) and t + d > ln[k][0]:
+            t = max(t, ln[k][1])
+            k += 1
+        ln.insert(k, (t, t + d))
+        o["t0"] = t
+    return sorted(range(n), key=lambda i: (ops[i]["t0"], i))
+
+
+def emit(g, T, ops, order, ne):
+    queue = {"V": g.vector, "S": g.scalar, "P": g.tensor, "G": g, "Y": g.sync}
+    seq, cnt = {}, {}
+    for i in order:
+        o = ops[i]
+        if o["sem"] is None:
+            cnt[o["e"]] = cnt.get(o["e"], 0) + 1
+            seq[i] = cnt[o["e"]]
+    known = {e: {} for e in queue}
+    clock, waits, wanted = {}, {}, set()
+    for i in order:
+        o = ops[i]
+        e = o["e"]
+        if e == "A":
+            clock[i] = {o["sem"]: 1}
+            continue
+        kn, ws = known[e], []
+        for j in sorted(o["d"], key=lambda j: -ops[j]["t0"]):
+            p = ops[j]
+            if p["e"] == "P" and e == "P":
+                continue
+            key, val = (p["e"], seq[j]) if p["sem"] is None else (p["sem"], 1)
+            if kn.get(key, 0) >= val:
+                continue
+            ws.append(j)
+            wanted.add(j)
+            for k, v in clock[j].items():
+                if kn.get(k, 0) < v:
+                    kn[k] = v
+        waits[i] = ws
+        c = dict(kn)
+        if o["sem"] is None:
+            c[e] = seq[i]
+        else:
+            c[o["sem"]] = 1
+        clock[i] = c
+    last = {}
+    for i in order:
+        if ops[i]["sem"] is None:
+            last[ops[i]["e"]] = i
+    wanted.update(last.values())
+    num, cnt, total = {}, {}, {}
+    for i in order:
+        if ops[i]["sem"] is None and i in wanted:
+            cnt[ops[i]["e"]] = cnt.get(ops[i]["e"], 0) + 1
+            num[i] = cnt[ops[i]["e"]]
+    for i in order:
+        o = ops[i]
+        if o["e"] == "A":
+            total[o["sem"]] = o["n"]
+            continue
+        q = queue[o["e"]]
+        for j in waits[i]:
+            p = ops[j]
+            if p["sem"] is None:
+                q.wait_ge(T.sem["c" + p["e"]], num[j])
+            else:
+                q.wait_ge(T.sem[p["sem"]], p["n"])
+        ins = o["f"]()
+        if o["sem"] is None:
+            if i in wanted:
+                ins.then_inc(T.sem["c" + o["e"]], 1)
+        elif o["sem"] == "remote":
+            total["sent"] = total.get("sent", 0) + ne
+        else:
+            ins.then_inc(T.sem[o["sem"]], 16)
+            total[o["sem"]] = total.get(o["sem"], 0) + 16
+    for e, v in cnt.items():
+        total["c" + e] = v
+    for k in sorted(total, key=lambda k: k.startswith("out")):
+        g.wait_ge(T.sem[k], total[k])
+
+
+def rank_program(g, core, T, topo):
+    if T.rank_of(core) is None:
+        return
+    ops, ne = build(g, core, T, topo)
+    depend(ops)
+    emit(g, T, ops, plan(ops), ne)

@@ -1,35 +1,36 @@
-from concourse.mybir import dt, AluOpType, AxisListType, ActivationFunctionType
+from concourse.mybir import dt, AluOpType, ActivationFunctionType
 
 C, M, F, R = 320, 128, 4, 3
 NI = C // 16
 BIG = 2.0 ** 96
+K16W, K4W = 2.0 ** 30, 2.0 ** 13
 SEG = [8 * i * (i + 1) for i in range(9)]
+HI = 192
+GAP = 8
+XE = 4 * C + GAP
+MID = 4 * HI + 4
+SW = 384
 
-TILES = [(("d", 19, 18, 17), 320, 0), ((16, 15, 14, 13), 256, 320), ((12, 11, 10, 9), 192, 576),
-         ((8, 7, 6, 5), 128, 768), ((4, 3, 2, 1), 128, 896)]
+TILES = [(("d", 19, 18, 17), 320, 0), ((16, 15, 14, 13), 256, 320), ((9, 10, 11, 12), 192, 576),
+         ((5, 6, 7, 8), 128, 768), ((1, 2, 3, 4), 64, 896)]
 PAR = {
-    "pe": [0, 4, 3, 2, 1],
-    "srows": (16, 15, 14, 13, 12, 11),
-    "vsums": (1, 2, 3, 4),
-    "vmsg": (0, 2),
-    "cyc": 1.04, "fix": 55.0, "wake": 70.0, "ga": 1.56, "sca": 3.8,
-    "off": {'VZ00': 35, 'SsgWm': -35, 'Vpre': 44, 'SHp': 33, 'VRS3': 31, 'Vrk': -10, 'VQC1': 59, 'VX0': 34, 'GEt': 60,
-            'VL': 40, 'SRS19': -45, 'GsentQ2': 58, 'SRS9': 57, 'VQG': 5, 'VcI3': 54, 'Vd5': 42, 'VCT10': 60, 'VposA': 40,
-            'Vews': 31, 'Sn2': 10, 'VQC0': -26, 'VRS4': 22, 'Vrd': 10, 'GuI': 26, 'Gi16': 24, 'Vroff': -31, 'GkI': 5,
-            'VWm': -21, 'VQC2': -20, 'SA': 3, 'SK4': 54, 'VCT7': 28, 'VCT4': 36, 'PB2': -9, 'VY1': 37, 'VW2': -6,
-            'VCT5': 43, 'Vhf': 32, 'SysbQX': 16, 'VQC3': -47},
+    "vrows": 12,
+    "vmsg": (0, 4),
+    "chunks": (4, 4),
+    "eg": "VS",
+    "pe": (0, 3, 4, 2, 1),
 }
 
 Q4, U8, BF, F32, I32, U16 = "float8_e4m3fn_x4", "uint8", "bfloat16", "float32", "int32", "uint16"
 SCRATCH = {"ps": ("psum", [128, 4096], F32)}
 for _d, _l in (
-        (BF, "Xt:1792 Xh:1280 Yt:512 Yh:512 Z:2048 ut:512 vt:512 CT:4096 FT:512 Et:2048 Gi:512 Gt:512 Ri:512 Rt:512 j16:320 Mk:320 "
-             "K16:320 keep:320 j4:256 Mk4:256 K4:256 Ai:576 A:576 iO:320 sg0:320 sg1:320 vg0:320 vg1:320 junk:3072 rd:320 o2:640 "
-             "d4:256 e4:256 erep:512 Hp:512 ew:128 d5:128 ews:128 EQ:576 st:576"),
-        (F32, "cF:8 cG:16 Lf:16 i16:32 RC:20 jc:8 dum:32 ti:32 tq:32 tc:32 nb:4 kF:16 dk:16 D16:16 D32:32 d1:320 W:320 d2:320 "
-              "W2:320 d3:128 Wm:128 RS:20 tr:60 n:8 pos:64 pre:16 okc:4 zi:8 hf:32 e1:32 e2:32 e3:32 Rr:512 ysb:448"),
-        (I32, "pI:16 cI:8 kI:16"),
-        (U16, "uL:8 L:16 roff:20 pof:64 zof0:64 zof1:64 ziu:8 hof:32 xof:32")):
+        (BF, "Xt:1800 Xh:1288 Yt:512 Yh:512 Z:2048 ut:512 vt:512 CT:4096 FT:512 Et:2048 Gi:512 Gt:512 Ri:512 Rt:512 j16:320 Mk:320 "
+             "K16:320 keep:320 A16:320 a1:320 a2:320 big:320 j4:256 A4:256 w4:16 Ai:576 A:576 iO:320 iP:320 sg0:320 sg1:320 vg:320 "
+             "vb:2560 rs:1538 kq:384 rd:320 o2:640 er:512 e4:256 erep:512 Hp:512 ew:128 ews:128 EQ:576 st:576"),
+        (F32, "cF:8 cG:16 Lf:24 i16:32 RC:20 jc:8 dum:32 ti:32 tq:32 nb:4 kF:16 dk:16 D16:48 qf:16 d1:320 W:320 s4:16 "
+              "W2:320 d3:128 Wm:128 RS:20 tr:60 n:8 pos:48 pre:16 okc:4 zi:8 hf:32 e:96 Rr:512 ysb:448"),
+        (I32, "pI:16 cI:8 kI:16 qI:8"),
+        (U16, "uL:8 L:24 roff:20 pof:48 zof:128 ziu:8 hof:32 xof:32")):
     for _e in _l.split():
         SCRATCH[_e.split(":")[0]] = ("sbuf", [128, int(_e.split(":")[1])], _d)
 for _e in ("A:448 u:128 v:128 g:128 W:512 C:1024 F:128 E:512 G:128 R:128 Z0:512 Z1:512 Z2:512 H0:128 H1:128 H2:128 "
@@ -40,10 +41,34 @@ for _e in ("A:448 u:128 v:128 g:128 W:512 C:1024 F:128 E:512 G:128 R:128 Z0:512 
 SEMAPHORES = ["cV", "cS", "cP", "cG", "lu", "lx0", "lx1", "lm", "lv", "lwc", "lws", "lk", "outh", "outg", "sent",
               "arr0", "arr1", "arr2"]
 
+FIRST = {
+    "V": "kq0 CT4 cI4 cI2 CT3 cI3 uL kq1 CT1 cI1 cI6 pm cI0 CT0 cF big kq2 Mk0 dn16 qpad CT2 nb rs0 qu qx1 FT0 Qg qx0 Mk sz pma "
+         "Lf0 dH dL WH WL pmb cG81 qy c1 pmf c11 qI qv c7 c3 c2 cG10 c10 c9 c8 d3 c6 kF c12 dg cG6 q2 gap Wm w4b c5 Lq cG80 f0 "
+         "w4a rd Lf10 s1 a2 s2 Ls down s0 qG t1 L c4 q0 s3 q3 q1 A16 ua g0 W2 ub f4 rk n0 A4 pos0 roff g4 o2a pof0 o2b n4 pre0 "
+         "er0 pos1 wb e40 pof1 zof0 up up16 Z30 Z10 e41 Z20 zof1 Z00 Z21 Z31 Z01 qz2 Z11 qz3 qz1 qz0 qR qE2 pre FT qF zi ziu hf "
+         "QH qE3 ews qE1 EQ6 EQ7 EQ5 EQ1 EQ2 EQ4 EQ0 EQ3 hof st e2 qE0 e3 xof X",
+    "S": "lx1 lm keep neg t640 cG4 cG2 qf0 qg1 qf1 a0 K16 Sg Gt0 Yh Gt1 a19 Lf8 rc1 Gu2 jc Gu0 RC Gu1 b19 sq a18 a17 b18 b17 se "
+         "a16 a15 b16 Gu3 b15 Lf4 qg0 a13 sp Lr0 b13 Lr1 a14 f1 b14 n1 a1 f2 f3 n3 D0 n2 f5 iO n5 f6 f7 D1 n6 n7 Xh er1 Rt0 tq "
+         "Rt1 A0 ec31 ec10 A1 cG3 ec20 ec21 ec01 ec30 A2 ec00 ec11 ew SH e12 e10 okc e13 dum e11 Hp",
+    "P": "mH m0 m1 mS mC0 mC3 mC4 mC2 mC1 mZ2 mZ3 mZ1 mZ0 mF",
+    "G": "uI pI j16 i16 Gi kI Ai1 Ai6 iP0 Ai4 j4 iP1 Ri Ai2 Ai0 Ai3 dk Ai7 Ai5 Et0 ti Et1 Az1 Az2 Az3 Az4 Az5 Az6 Az7 sendQ sendS",
+    "Y": "lu lx0 lv lwc lws ok"}
+STEADY = {
+    "V": "qx1 qx0 dH WH dL c12 WL Y1 dg c7 c11 c9 Y0 rd c10 c3 c4 Y3 c1 Y2 s2 c2 t1 qy q2 c5 c8 d3 c6 Wm q0 q3 s1 s3 q1 s0 f0 W2 "
+         "ua g0 ub n0 rk f4 roff pos0 o2a pof0 o2b g4 er0 n4 e40 pos1 zof0 pof1 Z30 Z10 e41 Z00 zof1 Z20 Z01 Z11 Z31 Z21 qz0 qz1 "
+         "qz2 qz3 pre FT qF zi ziu hf QH ews hof EQ0 EQ4 EQ3 EQ7 EQ6 EQ1 EQ2 EQ5 st e2 e3 xof X",
+    "S": "Xh Rr1 a19 a18 b19 Rr0 a17 Rr3 b17 Rr2 b18 a15 a16 b15 b16 a13 a14 b13 b14 f1 f2 n1 n2 f3 n3 f6 f5 n6 n5 f7 n7 Yh er1 "
+         "ec10 ec30 ec11 ec31 ec01 ec00 okc ec20 ec21 ew SH e11 e10 e12 e13 Hp",
+    "P": "mH m0 m1 mW1 mE0 mE1 mW3 mW0 mW2 mE3 mE2 mS mC0 mC3 mC4 mC2 mC1 mZ0 mZ1 mZ2 mZ3 mF",
+    "G": "sendQ sendS", "Y": "ok", "A": "land<"}
+LAST = {
+    "V": "qx0 qx1 Y3 Y0 Y1 Y2 qy", "S": "Rr3 Rr0 Rr1 Rr2 ysx oyx ysy oyy", "P": "mE1 mW3 mW0 mE3 mW1 mE2 mE0 mW2 mvx mvy",
+    "G": "os3", "Y": "ocx os0 os1 os2 ocy", "A": "land<"}
+ORDER = [FIRST, STEADY, STEADY, LAST]
+
 
 def build(g, core, T, topo):
     Alu, Act = AluOpType, ActivationFunctionType
-    CYC, FIX, GA, SCA = PAR["cyc"], PAR["fix"], PAR["ga"], PAR["sca"]
     rank = T.rank_of(core)
     nxt = T.cores[(rank + 1) % len(T.cores)]
     rid, pid = topo.addr(nxt)[0], topo.addr(nxt)[1]
@@ -51,298 +76,340 @@ def build(g, core, T, topo):
     ne = len(topo.engines(core, nxt))
     ops = []
     V, S, P, G, Y = g.vector, g.scalar, g.tensor, g, g.sync
+    at = [0]
 
-    def add(eng, fn, r, w, busy, lat=None, sem=None, n=16):
-        ops.append({"e": eng, "f": fn, "r": list(r), "w": list(w), "busy": busy, "lat": busy if lat is None else lat,
-                    "sem": sem, "n": n})
-
-    def cyc(n):
-        return FIX + n * CYC
+    def add(name, eng, fn, r, w, sem=None, n=16, late=0):
+        ops.append({"name": name + "<" * late, "at": at[0] + late, "e": eng, "f": fn, "r": list(r), "w": list(w), "sem": sem, "n": n})
 
     def ps(b, a, z):
         return T.ps[:, 512 * b + a:512 * b + z]
 
-    def ts(out, in0, s1, s2, op0, op1, r, w, n):
+    def ts(name, out, in0, s1, s2, op0, op1, r, w):
         if op1 is None:
-            add("V", lambda: V.tensor_scalar(out, in0, s1, None, op0), r, w, cyc(n))
+            add(name, "V", lambda: V.tensor_scalar(out, in0, s1, None, op0), r, w)
         else:
-            add("V", lambda: V.tensor_scalar(out, in0, s1, s2, op0, op1), r, w, cyc(n))
+            add(name, "V", lambda: V.tensor_scalar(out, in0, s1, s2, op0, op1), r, w)
 
-    def tt(out, in0, in1, op, r, w, n):
-        add("V", lambda: V.tensor_tensor(out, in0, in1, op), r, w, cyc(n))
+    def tt(name, out, in0, in1, op, r, w):
+        add(name, "V", lambda: V.tensor_tensor(out, in0, in1, op), r, w)
 
-    def cp(out, in_, r, w, n):
-        add("V", lambda: V.tensor_copy(out, in_), r, w, cyc(n))
+    def cp(name, out, in_, r, w):
+        add(name, "V", lambda: V.tensor_copy(out, in_), r, w)
 
-    def scan(out, a, b, init, op0, op1, r, w, n):
-        add("V", lambda: V.tensor_tensor_scan(out, a, b, init, op0, op1), r, w, cyc(n))
+    def scan(name, out, a, b, init, op0, op1, r, w):
+        add(name, "V", lambda: V.tensor_tensor_scan(out, a, b, init, op0, op1), r, w)
 
-    def mset(ap, val, w, n):
-        add("V", lambda: V.memset(ap, val), [], w, cyc(n))
+    def mset(name, ap, val, w):
+        add(name, "V", lambda: V.memset(ap, val), [], w)
 
-    def quant(q, s, t, r, w, n):
-        add("V", lambda: V.quantize_mx(q, s, t), r, w, 20 + 0.27 * 4 * n)
+    def quant(name, q, s, t, r, w):
+        add(name, "V", lambda: V.quantize_mx(q, s, t), r, w)
 
-    def act(out, in_, fn, r, w, n, **kw):
-        add("S", lambda: S.activation(out, in_, fn, **kw), r, w, cyc(n) + (25 if "accum_out" in kw else 0))
+    def act(name, out, in_, fn, r, w, **kw):
+        add(name, "S", lambda: S.activation(out, in_, fn, **kw), r, w)
 
-    def mm(out, a, sa, b, sb, r, w, n, start=True, stop=True):
-        add("P", lambda: P.matmul_mx(out, a, sa, b, sb, start, stop), r, w, (n + 16) * 1.25)
+    def mm(name, out, a, sa, b, sb, r, w, start=True, stop=True):
+        add(name, "P", lambda: P.matmul_mx(out, a, sa, b, sb, start, stop), r, w)
 
-    def iota(out, pat, base, cm, w, n, flt=True):
+    def iota(name, out, pat, base, cm, w, flt=True):
         if flt:
-            add("G", lambda: G.iota(out, pat, base, cm, allow_small_or_imprecise_dtypes=True), [], w, 160 + 2 * n * CYC)
+            add(name, "G", lambda: G.iota(out, pat, base, cm, allow_small_or_imprecise_dtypes=True), [], w)
         else:
-            add("G", lambda: G.iota(out, pat, base, cm), [], w, 160 + 2 * n * CYC)
+            add(name, "G", lambda: G.iota(out, pat, base, cm), [], w)
 
-    def dma(q, out, in_, r, w, sem, lat=2200.0):
+    def dma(name, q, out, in_, r, w, sem):
         e = {"Y": Y, "S": S, "G": G}[q]
-        add(q, lambda: e.dma_start(out, in_), r, w, 100.0 if q != "G" else 700.0, lat, sem)
+        add(name, q, lambda: e.dma_start(out, in_), r, w, sem)
 
     ID = Act.Identity
+    VR = PAR["vrows"]
 
-    dma("Y", T.ut[:], T.u[:], [], ["ut"], "lu", 1900.0)
-    dma("S", T.Xt[:, 0:640], T.x[:, 0:640], [], ["X0"], "lx0", 2300.0)
-    dma("Y", T.Xt[:, 640:1280], T.x[:, 640:1280], [], ["X1"], "lx1", 2300.0)
-    dma("S", T.Yt[:], T.m[:], [], ["Y0", "Y1", "Y2", "Y3"], "lm", 2600.0)
-    quant(T.Qu[:], T.Su[:], T.ut[:], ["ut"], ["Qu"], 128)
-    dma("Y", T.QW[:].bitcast(dt.uint8), T.wc[:], ["Qu"], ["QW"], "lwc", 3500.0)
-    dma("Y", T.SW[:], T.ws[:], ["Qu"], ["SW"], "lws", 3500.0)
-    dma("Y", T.vt[:], T.v[:], ["Qu"], ["vt"], "lv", 3000.0)
+    dma("lu", "Y", T.ut[:], T.u[:], [], ["ut"], "lu")
+    dma("lx1", "S", T.Xt[:, 4 * HI + GAP:XE], T.x[:, 4 * HI:4 * C], [], ["X1"], "lx1")
+    dma("lx0", "Y", T.Xt[:, 0:4 * HI], T.x[:, 0:4 * HI], [], ["X0"], "lx0")
+    dma("lm", "S", T.Yt[:], T.m[:], [], ["Y0", "Y1", "Y2", "Y3"], "lm")
+    quant("qu", T.Qu[:], T.Su[:], T.ut[:], ["ut"], ["Qu"])
+    dma("lwc", "Y", T.QW[:].bitcast(dt.uint8), T.wc[:], ["Qu"], ["QW"], "lwc")
+    dma("lws", "Y", T.SW[:], T.ws[:], ["Qu"], ["SW"], "lws")
+    dma("lv", "Y", T.vt[:], T.v[:], ["Qu"], ["vt"], "lv")
 
-    iota(T.pI[:, 8:16], [[16, 8]], 0, 0, ["uI"], 8, flt=False)
-    cp(T.uL[:], T.pI[:, 8:16], ["uI"], ["uL"], 8)
-    iota(T.pI[:, 0:8], [[0, 8]], 0, 1, ["pI"], 8, flt=False)
+    iota("uI", T.pI[:, 8:16], [[16, 8]], 0, 0, ["uI"], flt=False)
+    cp("uL", T.uL[:], T.pI[:, 8:16], ["uI"], ["uL"])
+    iota("pI", T.pI[:, 0:8], [[0, 8]], 0, 1, ["pI"], flt=False)
     for a, z, sh, an in [(0, 1, 0, 15), (1, 2, 4, 7), (2, 3, 2, 3), (3, 4, 0, 3), (4, 6, 0, 7), (6, 8, 3, 1)]:
-        ts(T.cI[:, a:z], T.pI[:, a:z], sh, an, Alu.logical_shift_right, Alu.bitwise_and, ["pI"], ["cI%d" % a], 1)
-    cp(T.cF[:], T.cI[:], ["cI%d" % c for c in (0, 1, 2, 3, 4, 6)], ["cF"], 8)
+        ts("cI%d" % a, T.cI[:, a:z], T.pI[:, a:z], sh, an, Alu.logical_shift_right, Alu.bitwise_and, ["pI"], ["cI%d" % a])
+    cp("cF", T.cF[:], T.cI[:], ["cI%d" % c for c in (0, 1, 2, 3, 4, 6)], ["cF"])
     rc, gc_, r4, t4 = [T.cF[:, c:c + 1] for c in range(4)]
-    act(T.cG[:, 0:2], T.cF[:, 0:2], Act.Copy, ["cF"], ["neg"], 2, scale=-1.0)
+    act("neg", T.cG[:, 0:2], T.cF[:, 0:2], Act.Copy, ["cF"], ["neg"], scale=-1.0)
     nr, ng = T.cG[:, 0:1], T.cG[:, 1:2]
-    iota(T.j16[:], [[0, NI], [1, 16]], 0, 0, ["j16"], C)
-    ts(T.Mk[:], T.j16[:], rc, 0.5, Alu.is_equal, Alu.subtract, ["j16", "cF"], ["Mk"], C / 2)
-    ts(T.Mk[:], T.Mk[:], 2 * BIG, None, Alu.mult, None, ["Mk"], ["Mk"], C / 2)
-    act(T.keep[:], T.j16[:], Act.Sign, ["j16"], ["keep"], C)
-    act(T.K16[:], T.keep[:], ID, ["keep"], ["K16"], C, scale=2 * BIG, bias=-BIG)
-    for rows, width, first in TILES:
-        a, z = 4 * (first + 16 * rows[3]), 4 * (first + width)
-        mset(T.CT[:, a:z], 0.0, ["CT%s" % str(i) for i in rows], (z - a) / 2)
-    iota(T.Gi[:], [[1, 8], [0, 64]], 0, 0, ["Gi"], 512)
-    add("G", lambda: G.dma_start(T.kI[0:1, :], T.kap[:], allow_slow_non_contiguous=True), ["Gi"], ["kI"], 1500.0, 3000.0, "lk")
-    act(T.Gt[:], T.Gi[:], Act.Abs, ["Gi", "neg"], ["Gt"], 512, bias=ng)
-    act(T.Gt[:], T.Gt[:], Act.Relu, ["Gt"], ["Gt"], 512, bias=1.0, scale=-1.0)
-    quant(T.QG[:], T.SG[:], T.Gt[:], ["Gt"], ["QG"], 128)
-    iota(T.i16[:], [[16, 32]], 0, 0, ["i16"], 32)
-    act(T.cG[:, 2:3], rc, ID, ["cF"], ["cG2"], 1, scale=-1.0, bias=15.0)
-    act(T.RC[:], T.i16[:, 0:NI], ID, ["i16", "cG2"], ["RC"], NI, bias=T.cG[:, 2:3])
-    act(T.jc[:], T.i16[:, 0:8], ID, ["i16", "cF"], ["jc"], 8, bias=rc)
-    act(T.cG[:, 3:4], rc, ID, ["cF"], ["cG3"], 1, bias=float(4 * C))
-    act(T.dum[:], T.i16[:], ID, ["i16", "cG3"], ["dum"], 32, bias=T.cG[:, 3:4])
-    mset(T.RS[:, 0:1], 0.0, ["RS0"], 1)
-    iota(T.iO[:], [[4, C]], -2 * C, 0, ["iO"], C)
+    iota("j16", T.j16[:], [[0, NI], [1, 16]], 0, 0, ["j16"])
+    ts("Mk0", T.Mk[:], T.j16[:], rc, 0.5, Alu.is_equal, Alu.subtract, ["j16", "cF"], ["Mk"])
+    ts("Mk", T.Mk[:], T.Mk[:], 2 * BIG, None, Alu.mult, None, ["Mk"], ["Mk"])
+    act("keep", T.keep[:], T.j16[:], Act.Sign, ["j16"], ["keep"])
+    act("K16", T.K16[:], T.keep[:], ID, ["keep"], ["K16"], scale=2 * BIG, bias=-BIG)
+    act("a0", T.a1[:], T.j16[:], Act.Abs, ["j16", "neg"], ["a1"], bias=nr)
+    act("a1", T.a1[:], T.a1[:], Act.Sign, ["a1"], ["a1"])
+    act("rc1", T.cG[:, 11:12], rc, ID, ["cF"], ["rc1"], bias=1.0)
+    ts("a2", T.a2[:], T.j16[:], T.cG[:, 11:12], K16W, Alu.is_equal, Alu.mult, ["j16", "rc1"], ["a2"])
+    tt("A16", T.A16[:], T.a1[:], T.a2[:], Alu.max, ["a1", "a2"], ["A16"])
+    up16 = T.w4[:, 14:15]
+    ts("wb", up16, rc, 15.0, K16W, Alu.is_lt, Alu.mult, ["cF"], ["wb"])
+    ts("up16", up16, up16, 1.0, None, Alu.max, None, ["wb"], ["wb"])
+    ts("dn16", T.cG[:, 12:13], rc, 15.0, 1.0 / K16W, Alu.is_equal, Alu.max, ["cF"], ["dn16"])
+    mset("gap", T.Xt[:, 4 * HI:4 * HI + GAP], 0.0, ["gap"])
+    mset("big", T.big[:], 512.0, ["big"])
+    for u, (rows, width, first) in enumerate(TILES):
+        a, z = (4 * (first + 16 * min(i for i in rows if i != "d")), 4 * (first + width)) if u < 4 else (4 * first, 4096)
+        mset("CT%d" % u, T.CT[:, a:z], 0.0, ["CT%s" % str(i) for i in rows])
+    quant("qpad", T.QC[:, 896:1024], T.SC[:, 896:1024], T.CT[:, 4 * 896:4096], ["CT1", "CT2", "CT3", "CT4"], ["QC4"])
+    iota("Gi", T.Gi[:], [[1, 8], [0, 64]], 0, 0, ["Gi"])
+    add("kI", "G", lambda: G.dma_start(T.kI[0:1, :], T.kap[:], allow_slow_non_contiguous=True), ["Gi"], ["kI"], "lk")
+    act("Gt0", T.Gt[:], T.Gi[:], Act.Abs, ["Gi", "neg"], ["Gt"], bias=ng)
+    act("Gt1", T.Gt[:], T.Gt[:], Act.Relu, ["Gt"], ["Gt"], bias=1.0 / K16W, scale=-1.0)
+    for c in range(4):
+        act("Gu%d" % c, T.Gt[:, 60 + c:512:64], T.Gt[:, 60 + c:512:64], Act.Copy, ["Gt"], ["Gu%d" % c], scale=K16W)
+    quant("qG", T.QG[:], T.SG[:], T.Gt[:], ["Gt"] + ["Gu%d" % c for c in range(4)], ["QG"])
+    iota("i16", T.i16[:], [[16, 32]], 0, 0, ["i16"])
+    act("cG2", T.cG[:, 2:3], rc, ID, ["cF"], ["cG2"], scale=-1.0, bias=15.0)
+    act("RC", T.RC[:], T.i16[:, 0:NI], ID, ["i16", "cG2"], ["RC"], bias=T.cG[:, 2:3])
+    act("jc", T.jc[:], T.i16[:, 0:8], ID, ["i16", "cF"], ["jc"], bias=rc)
+    act("cG3", T.cG[:, 3:4], rc, ID, ["cF"], ["cG3"], bias=float(XE))
+    act("dum", T.dum[:], T.i16[:], ID, ["i16", "cG3"], ["dum"], bias=T.cG[:, 3:4])
     n4 = 256
-    iota(T.j4[:], [[0, n4 // 4], [1, 4]], 0, 0, ["j4"], n4)
-    ts(T.Mk4[:], T.j4[:], r4, 0.5, Alu.is_equal, Alu.subtract, ["j4", "cF"], ["Mk4"], n4 / 2)
-    ts(T.Mk4[:], T.Mk4[:], 2 * BIG, None, Alu.mult, None, ["Mk4"], ["Mk4"], n4 / 2)
-    act(T.K4[:], T.j4[:], Act.Sign, ["j4"], ["K4"], n4)
-    act(T.K4[:], T.K4[:], ID, ["K4"], ["K4"], n4, scale=2 * BIG, bias=-BIG)
-    L16a, L16b, L32, L32e, LEND, LF, LD16, LD32 = (T.L[:, 0:1], T.L[:, 2:3], T.L[:, 4:6], T.L[:, 6:8], T.L[:, 8:10],
-                                                   T.L[:, 10:12], T.L[:, 12:13], T.L[:, 14:16])
-    act(T.Lf[:, 0:2], T.cF[:, 3:5], Act.Copy, ["cF"], ["Lf0"], 2)
-    act(T.Lf[:, 2:4], T.cF[:, 3:5], ID, ["cF"], ["Lf2"], 2, bias=4.0)
-    act(T.Lf[:, 4:6], T.cF[:, 4:6], Act.Copy, ["cF"], ["Lf4"], 2)
-    act(T.Lf[:, 6:8], T.cF[:, 4:6], ID, ["cF"], ["Lf6"], 2, scale=16.0, bias=15.0)
-    act(T.cG[:, 4:6], T.cF[:, 4:6], Act.Square, ["cF"], ["cG4"], 2, bias=1.5)
-    act(T.Lf[:, 8:10], T.cG[:, 4:6], ID, ["cG4"], ["Lf8"], 2, scale=8.0, bias=-3.0)
-    ts(T.cG[:, 10:11], t4, 3.0, None, Alu.is_lt, None, ["cF"], ["cG10"], 1)
-    ts(T.cG[:, 6:7], t4, 5.0, T.cG[:, 10:11], Alu.add, Alu.mult, ["cF", "cG10"], ["cG6"], 1)
+    iota("j4", T.j4[:], [[0, n4 // 4], [1, 4]], 0, 0, ["j4"])
+    ts("A4", T.A4[:], T.j4[:], r4, K4W, Alu.not_equal, Alu.mult, ["j4", "cF"], ["A4"])
+    ts("w4a", T.w4[:, 0:4], T.j4[:, 0:4], r4, 1.0 / K4W, Alu.not_equal, Alu.mult, ["j4", "cF"], ["w4a"])
+    ts("w4b", T.w4[:, 8:12], T.j4[:, 0:4], r4, None, Alu.is_equal, None, ["j4", "cF"], ["w4b"])
+    scan("up", T.s4[:, 0:4], T.A4[:, 0:4], T.w4[:, 8:12], 0.0, Alu.mult, Alu.add, ["A4", "w4b"], ["up"])
+    scan("down", T.s4[:, 8:12], T.w4[:, 0:4], T.w4[:, 8:12], 0.0, Alu.mult, Alu.add, ["w4a", "w4b"], ["down"])
+    up, down = T.s4[:, 3:4], T.s4[:, 11:12]
+    iota("iP0", T.iP[:, 0:HI], [[4, HI]], -MID, 0, ["iP0"])
+    iota("iP1", T.iP[:, HI:C], [[4, C - HI]], 4 * HI + GAP - MID, 0, ["iP1"])
+    act("iO", T.iO[:], T.iP[:], ID, ["iP0", "iP1", "down"], ["iO"], scale=down)
+    LS, L32, LEND, LF = T.L[:, 0:1], T.L[:, 4:6], T.L[:, 8:10], T.L[:, 10:12]
+    mset("Lf0", T.Lf[:], 0.0, ["Lf"])
+    mset("kq0", T.kq[:], 1.0, ["kq"])
+    mset("kq1", T.kq[:, 0:SW:192], 0.0, ["kq"])
+    mset("kq2", T.kq[:, 320:321], 0.0, ["kq"])
+    mset("rs0", T.rs[:, 4 * SW:4 * SW + 2], 0.0, ["rsz"])
+    ts("pm", T.qI[:, 4:6], T.pI[:, 0:2], 15.0, None, Alu.add, None, ["pI"], ["pm"])
+    ts("pma", T.qI[:, 6:7], T.qI[:, 4:5], 0, 3, Alu.logical_shift_right, Alu.bitwise_and, ["pm"], ["pma"])
+    ts("pmb", T.qI[:, 7:8], T.qI[:, 5:6], 2, 3, Alu.logical_shift_right, Alu.bitwise_and, ["pm"], ["pmb"])
+    cp("pmf", T.qf[:, 8:10], T.qI[:, 6:8], ["pma", "pmb"], ["pmf"])
+    act("sq", T.qf[:, 10:11], T.qf[:, 9:10], Act.Square, ["pmf"], ["sq"], bias=0.5)
+    act("se", T.qf[:, 11:12], T.qf[:, 10:11], ID, ["sq"], ["se"], scale=-32.0, bias=SW + 7.0)
+    act("sp", T.qf[:, 12:13], T.qf[:, 8:9], ID, ["pmf", "se"], ["sp"], scale=float(SW), bias=T.qf[:, 11:12])
+    ts("sz", T.qf[:, 13:14], rc, 0.0, 4.0 * SW, Alu.is_equal, Alu.mult, ["cF"], ["sz"])
+    ts("Ls", T.Lf[:, 0:1], T.qf[:, 12:13], T.qf[:, 13:14], None, Alu.max, None, ["sp", "sz", "Lf"], ["Ls"])
+    CH = PAR["chunks"]
+    NC = len(CH)
+    for c, r in enumerate(CH):
+        act("qf%d" % c, T.qf[:, c:c + 1], rc, ID, ["cF"], ["qf%d" % c], scale=1.0 / r, bias=-(r - 1) / (2.0 * r))
+        act("qg%d" % c, T.qf[:, 4 + c:5 + c], rc, ID, ["cF"], ["qg%d" % c], bias=float(sum(CH[:c])))
+    cp("qI", T.qI[:, 0:NC], T.qf[:, 0:NC], ["qf%d" % c for c in range(NC)], ["qI"])
+    cp("Lq", T.Lf[:, 12:12 + 4 * NC:4], T.qI[:, 0:NC], ["qI", "Lf"], ["Lq"])
+    for c, r in enumerate(CH):
+        act("Lr%d" % c, T.Lf[:, 14 + 4 * c:15 + 4 * c], T.Lf[:, 12 + 4 * c:13 + 4 * c], ID, ["Lq", "qg%d" % c], ["Lr%d" % c],
+            scale=-float(r), bias=T.qf[:, 4 + c:5 + c])
+    act("Lf4", T.Lf[:, 4:6], T.cF[:, 4:6], Act.Copy, ["cF", "Lf"], ["Lf4"])
+    act("cG4", T.cG[:, 4:6], T.cF[:, 4:6], Act.Square, ["cF"], ["cG4"], bias=1.5)
+    act("Lf8", T.Lf[:, 8:10], T.cG[:, 4:6], ID, ["cG4", "Lf"], ["Lf8"], scale=8.0, bias=-3.0)
+    ts("cG10", T.cG[:, 10:11], t4, 3.0, None, Alu.is_lt, None, ["cF"], ["cG10"])
+    ts("cG6", T.cG[:, 6:7], t4, 5.0, T.cG[:, 10:11], Alu.add, Alu.mult, ["cF", "cG10"], ["cG6"])
     for c in range(2):
-        ts(T.cG[:, 8 + c:9 + c], r4, 4.0 * c, gc_, Alu.add, Alu.is_equal, ["cF"], ["cG8%d" % c], 1)
-        act(T.Lf[:, 14 + c:15 + c], T.cF[:, 6:7], ID, ["cF"], ["Lf14%d" % c], 1, bias=2.0 * c)
-    ts(T.Lf[:, 10:12], T.cG[:, 8:10], T.cG[:, 6:7], None, Alu.mult, None, ["cG80", "cG81", "cG6"], ["Lf10"], 2)
-    act(T.Lf[:, 12:14], T.cF[:, 2:4], Act.Copy, ["cF"], ["Lf12"], 2)
-    cp(T.L[:], T.Lf[:], ["Lf0", "Lf2", "Lf4", "Lf6", "Lf8", "Lf10", "Lf12", "Lf140", "Lf141"], ["L"], 16)
-    act(T.cG[:, 7:8], t4, ID, ["cF"], ["t640"], 1, bias=float(2 * C))
+        ts("cG8%d" % c, T.cG[:, 8 + c:9 + c], r4, 4.0 * c, gc_, Alu.add, Alu.is_equal, ["cF"], ["cG8%d" % c])
+    ts("Lf10", T.Lf[:, 10:12], T.cG[:, 8:10], T.cG[:, 6:7], None, Alu.mult, None, ["cG80", "cG81", "cG6", "Lf"], ["Lf10"])
+    cp("L", T.L[:], T.Lf[:], ["Ls", "Lf4", "Lf8", "Lf10", "Lq"] + ["Lr%d" % c for c in range(NC)], ["L"])
+    act("t640", T.cG[:, 7:8], t4, ID, ["cF"], ["t640"], bias=MID + 0.25)
     t640 = T.cG[:, 7:8]
-    cp(T.kF[0:1, :], T.kI[0:1, :], ["kI"], ["kF"], 16)
-    add("G", lambda: G.partition_broadcast(T.dk[:], T.kF[0:1, :], 128), ["kF"], ["dk"], 260.0)
-    act(T.D16[:], T.dk[:].indirect(LD16), Act.Copy, ["dk", "L"], ["D16"], 16 * GA)
-    act(T.D32[:], T.dk[:].indirect(LD32), Act.Copy, ["dk", "L"], ["D32"], 32 * GA)
-    iota(T.ti[:], [[1, 4], [0, 8]], 0, 0, ["ti"], 32)
-    act(T.tq[:], T.ti[:], Act.Copy, ["ti"], ["tq"], 32, scale=0.25)
-    act(T.tc[:], T.ti[:], ID, ["ti"], ["tc"], 32, bias=float(2 * C - 1))
-    mset(T.nb[:], -BIG, ["nb"], 4)
-    mset(T.pre[:], BIG, ["pre"], 8)
-    mset(T.FT[:], 0.0, ["FT"], 256)
-    iota(T.Ri[:], [[0, 8], [1, 16], [0, 4]], 0, 0, ["Ri"], 512)
-    act(T.Rt[:], T.Ri[:], Act.Abs, ["Ri", "neg"], ["Rt"], 512, bias=nr)
-    act(T.Rt[:], T.Rt[:], Act.Relu, ["Rt"], ["Rt"], 512, bias=float(M), scale=-float(M))
-    quant(T.QR[:], T.SR[:], T.Rt[:], ["Rt"], ["QR"], 128)
+    cp("kF", T.kF[0:1, :], T.kI[0:1, :], ["kI"], ["kF"])
+    add("dk", "G", lambda: G.partition_broadcast(T.dk[:], T.kF[0:1, :], 128), ["kF"], ["dk"])
+    for c in range(NC):
+        act("D%d" % c, T.D16[:, 16 * c:16 * c + 16], T.dk[:].indirect(T.L[:, 12 + 4 * c:13 + 4 * c]), Act.Copy, ["dk", "L"], ["D%d" % c])
+    iota("ti", T.ti[:], [[1, 4], [0, 8]], 0, 0, ["ti"])
+    act("tq", T.tq[:], T.ti[:], Act.Copy, ["ti"], ["tq"], scale=0.25)
+    mset("nb", T.nb[:], -BIG, ["nb"])
+    mset("pre0", T.pre[:], BIG, ["pre"])
+    mset("FT0", T.FT[:], 0.0, ["FT"])
+    iota("Ri", T.Ri[:], [[0, 8], [1, 16], [0, 4]], 0, 0, ["Ri"])
+    act("Rt0", T.Rt[:], T.Ri[:], Act.Abs, ["Ri", "neg"], ["Rt"], bias=nr)
+    act("Rt1", T.Rt[:], T.Rt[:], Act.Relu, ["Rt"], ["Rt"], bias=float(M), scale=-float(M))
+    quant("qR", T.QR[:], T.SR[:], T.Rt[:], ["Rt"], ["QR"])
     for i in range(8):
-        iota(T.Ai[:, SEG[i]:SEG[i + 1]], [[1, 16 * (i + 1)]], -16 * i, 0, ["Ai%d" % i], 16 * (i + 1))
-    act(T.A[:], T.Ai[:], Act.Abs, ["Ai%d" % i for i in range(8)] + ["neg"], ["A"], 576, bias=nr)
-    act(T.A[:], T.A[:], Act.Relu, ["A"], ["A"], 576, bias=4096.0, scale=-4096.0)
-    act(T.A[:], T.A[:], ID, ["A"], ["A"], 576, bias=1.0)
+        iota("Ai%d" % i, T.Ai[:, SEG[i]:SEG[i + 1]], [[1, 16 * (i + 1)]], -16 * i, 0, ["Ai%d" % i])
+    act("A0", T.A[:], T.Ai[:], Act.Abs, ["Ai%d" % i for i in range(8)] + ["neg"], ["A"], bias=nr)
+    act("A1", T.A[:], T.A[:], Act.Relu, ["A"], ["A"], bias=4096.0, scale=-4096.0)
+    act("A2", T.A[:], T.A[:], ID, ["A"], ["A"], bias=1.0)
     for i in range(1, 8):
-        iota(T.A[:, SEG[i]:SEG[i] + 1], [[0, 1]], 0, 0, ["A"], 1)
-    iota(T.Et[:], [[0, 2048]], 1, 0, ["Et"], 2048)
-    add("G", lambda: G.affine_select(T.Et[:], T.Et[:], [[-1, 4], [-16, 128], [1, 4]], Alu.is_equal, 0.0, 0, 16),
-        ["Et"], ["Et"], 210 + 4096 * CYC)
-    quant(T.QE[:], T.SE[:], T.Et[:], ["Et"], ["QE"], 512)
+        iota("Az%d" % i, T.A[:, SEG[i]:SEG[i] + 1], [[0, 1]], 0, 0, ["A"])
+    iota("Et0", T.Et[:], [[0, 2048]], 1, 0, ["Et"])
+    add("Et1", "G", lambda: G.affine_select(T.Et[:], T.Et[:], [[-1, 4], [-16, 128], [1, 4]], Alu.is_equal, 0.0, 0, 16),
+        ["Et"], ["Et"])
+    for b in range(4):
+        quant("qE%d" % b, T.QE[:, M * b:M * b + M], T.SE[:, M * b:M * b + M], T.Et[:, 512 * b:512 * b + 512], ["Et"], ["QE%d" % b])
 
-    cp(T.Qg[:].bitcast(dt.uint32), T.Qu[:].bitcast(dt.uint32).indirect(T.uL[:]), ["Qu", "uL"], ["Qg"], 128 * GA)
-    act(T.Sg[:], T.Su[:].indirect(T.uL[:]), Act.Copy, ["Qu", "uL"], ["Sg"], 128 * GA)
-    quant(T.Qv[:], T.Sv[:], T.vt[:], ["vt"], ["Qv"], 128)
+    cp("Qg", T.Qg[:].bitcast(dt.uint32), T.Qu[:].bitcast(dt.uint32).indirect(T.uL[:]), ["Qu", "uL"], ["Qg"])
+    act("Sg", T.Sg[:], T.Su[:].indirect(T.uL[:]), Act.Copy, ["Qu", "uL"], ["Sg"])
+    quant("qv", T.Qv[:], T.Sv[:], T.vt[:], ["vt"], ["Qv"])
 
     kX, kY = ["X0", "X1"], ["Y0", "Y1", "Y2", "Y3"]
     kG = ["Qg", "Sg"]
-    t1, t2, rk = T.tr[:, 0:NI], T.tr[:, NI:2 * NI], T.tr[:, 2 * NI:3 * NI]
+    t1, rk, uu = T.tr[:, 0:NI], T.tr[:, NI:2 * NI], T.tr[:, 2 * NI:3 * NI]
 
     def quant_x():
-        quant(T.QA[:, 0:C], T.SA[:, 0:C], T.Xt[:, 0:4 * C], kX, ["QX"], C)
+        quant("qx1", T.QA[:, HI:C], T.SA[:, HI:C], T.Xt[:, 4 * HI + GAP:XE], ["X1"], ["QX1"])
+        quant("qx0", T.QA[:, 0:HI], T.SA[:, 0:HI], T.Xt[:, 0:4 * HI], ["X0"], ["QX0"])
 
     def quant_y():
-        quant(T.QA[:, C:C + M], T.SA[:, C:C + M], T.Yt[:], kY, ["QY"], M)
+        quant("qy", T.QA[:, C:C + M], T.SA[:, C:C + M], T.Yt[:], kY, ["QY"])
 
     def new_y(t, rb, db):
         q, s, k = T["QL%d" % t][:], T["SL%d" % t][:], "land%d" % t
         for b in range(4):
-            mm(ps(rb[b], 0, M), T.QW[:, M * b:M * b + M], T.SW[:, M * b:M * b + M], q, s, ["QW", "SW", k], ["B%d" % rb[b]], M)
-            mm(ps(db[b], 0, M), T.QE[:, M * b:M * b + M], T.SE[:, M * b:M * b + M], q, s, ["QE", k], ["B%d" % db[b]], M)
-            act(T.Rr[:, M * b:M * b + M], ps(rb[b], 0, M), Act.Relu, ["B%d" % rb[b]], ["Rr%d" % b], M, scale=0.03125)
-            tt(T.Yt[:, b:512:4], T.Rr[:, M * b:M * b + M], ps(db[b], 0, M), Alu.add, ["Rr%d" % b, "B%d" % db[b]], ["Y%d" % b], M)
+            mm("mW%d" % b, ps(rb[b], 0, M), T.QW[:, M * b:M * b + M], T.SW[:, M * b:M * b + M], q, s, ["QW", "SW", k], ["B%d" % rb[b]])
+            mm("mE%d" % b, ps(db[b], 0, M), T.QE[:, M * b:M * b + M], T.SE[:, M * b:M * b + M], q, s, ["QE%d" % b, k], ["B%d" % db[b]])
+            act("Rr%d" % b, T.Rr[:, M * b:M * b + M], ps(rb[b], 0, M), Act.Relu, ["B%d" % rb[b]], ["Rr%d" % b], scale=0.03125)
+            tt("Y%d" % b, T.Yt[:, b:512:4], T.Rr[:, M * b:M * b + M], ps(db[b], 0, M), Alu.add, ["Rr%d" % b, "B%d" % db[b]], ["Y%d" % b])
 
     for t in range(R):
+        at[0] = t
         QZ, SZ, QH, SH = T["QZ%d" % t], T["SZ%d" % t], T["QH%d" % t], T["SH%d" % t]
         quant_x()
-        mm(ps(0, 0, C), T.Qg[:], T.Sg[:], T.QA[:, 0:C], T.SA[:, 0:C], kG + ["QX"], ["B0"], C)
-        mm(ps(1, 0, C), T.Qg[:], T.Sg[:], T.QA[:, 0:C], T.SA[:, 0:C], kG + ["QX"], ["B1"], C)
-        act(T.Xh[:], T.Xt[:, 0:4 * C], Act.Copy, kX, ["Xh"], 4 * C, scale=0.5)
-        tt(T.d1[:], ps(0, 0, C), T.Mk[:], Alu.min, ["B0", "Mk"], ["d1"], C)
-        scan(T.W[:], T.K16[:], T.d1[:], -BIG, Alu.min, Alu.max, ["K16", "d1"], ["W"], C)
-        flip = [0, 0]
+        mm("mH", ps(3, 0, C - HI), T.Qg[:], T.Sg[:], T.QA[:, HI:C], T.SA[:, HI:C], kG + ["QX1"], ["B3"])
+        mm("m1", ps(1, 0, C), T.Qg[:], T.Sg[:], T.QA[:, 0:C], T.SA[:, 0:C], kG + ["QX0", "QX1"], ["B1"])
+        mm("m0", ps(0, 0, C), T.Qg[:], T.Sg[:], T.QA[:, 0:C], T.SA[:, 0:C], kG + ["QX0", "QX1"], ["B0"])
+        act("Xh", T.Xh[:], T.Xt[:, 0:XE], Act.Copy, kX + ["gap"], ["Xh"], scale=0.5)
+        tt("dH", T.d1[:, HI:C], ps(3, 0, C - HI), T.Mk[:, HI:C], Alu.min, ["B3", "Mk"], ["dH"])
+        scan("WH", T.W[:, HI:C], T.K16[:, HI:C], T.d1[:, HI:C], -BIG, Alu.min, Alu.max, ["K16", "dH"], ["WH"])
+        tt("dL", T.d1[:, 0:HI], ps(0, 0, HI), T.Mk[:, 0:HI], Alu.min, ["B0", "Mk"], ["dL"])
+        scan("WL", T.W[:, 0:HI], T.K16[:, 0:HI], T.d1[:, 0:HI], -BIG, Alu.min, Alu.max, ["K16", "dL"], ["WL"])
+        diag = T.CT[:, 0:4 * C:4]
+        tt("dg", diag, T.W[:], ps(0, 0, C), Alu.is_ge, ["WH", "WL", "B0"], ["CTd"])
+        scan("rd", T.rd[:], T.keep[:], diag, 0.0, Alu.mult, Alu.add, ["keep", "CTd"], ["rd"])
+        tt("t1", t1, T.rd[:, 15:C:16], T.RC[:], Alu.subtract, ["RC", "rd"], ["t1"])
         for rows, width, first in TILES:
             for slot, i in enumerate(rows):
-                w = C if i == "d" else 16 * i
-                out = T.CT[:, 4 * first + slot:4 * (first + w):4]
-                key = "CT%s" % str(i)
                 if i == "d":
-                    tt(out, T.W[:], ps(0, 0, C), Alu.is_ge, ["W", "B0"], [key], C)
-                    scan(T.rd[:], T.keep[:], out, 0.0, Alu.mult, Alu.add, ["keep", key], ["rd"], C / 2)
                     continue
-                own = T.W[:, 16 * i + 15:16 * i + 16]
-                if i in PAR["srows"]:
-                    sk = "sg%d" % flip[0]
-                    flip[0] ^= 1
-                    act(T[sk][:, 0:w], ps(1, 0, w), Act.Sign, ["B1", "W"], [sk], w, bias=own, scale=-1.0)
-                    act(out, T[sk][:, 0:w], Act.Relu, [sk], [key, "RS%d" % i], w, accum_out=T.RS[:, i:i + 1])
+                w = 16 * i
+                out = T.CT[:, 4 * first + slot:4 * (first + w):4]
+                key, kw = "CT%d" % i, "WH" if w >= HI else "WL"
+                own = T.W[:, w + 15:w + 16]
+                if i > VR:
+                    sk = "sg%d" % (i % 2)
+                    act("a%d" % i, T[sk][:, 0:w], ps(1, 0, w), Act.Sign, ["B1", kw], [sk], bias=own, scale=-1.0)
+                    act("b%d" % i, out, T[sk][:, 0:w], Act.Relu, [sk], [key, "RS%d" % i], accum_out=T.RS[:, i:i + 1])
                 else:
-                    ts(out, ps(0, 0, w), own, None, Alu.is_lt, None, ["B0", "W"], [key], w)
-                    if i in PAR["vsums"]:
-                        add("V", lambda o=T.RS[:, i:i + 1], a=out: V.tensor_reduce(o, a, AxisListType.X, Alu.add),
-                            [key], ["RS%d" % i], cyc(w))
-                    else:
-                        a = 8 * i * (i - 1)
-                        act(T.junk[:, a:a + w], out, Act.Copy, [key], ["RS%d" % i], w, accum_out=T.RS[:, i:i + 1])
-        for z, u in enumerate(PAR["pe"]):
+                    ts("c%d" % i, out, ps(0, 0, w), own, None, Alu.is_lt, None, ["B0", kw], [key])
+        for c in range(4):
+            scan("s%d" % c, T.rs[:, SW * c:SW * c + SW], T.kq[:], T.CT[:, 4 * 576 + c:4 * 960:4], 0.0, Alu.mult, Alu.add,
+                 ["kq"] + ["CT%d" % (c + 1 + 4 * a) for a in range(3)], ["rs%d" % c])
+        tt("ua", T.tr[:, 2 * NI:2 * NI + 16], T.rs[:].indirect(LS), T.tr[:, 0:16], Alu.add,
+           ["t1", "L", "rsz"] + ["rs%d" % c for c in range(4)], ["uu"])
+        tt("ub", T.tr[:, 2 * NI + VR + 1:3 * NI], T.tr[:, VR + 1:NI], T.RS[:, VR + 1:NI], Alu.add,
+           ["t1"] + ["RS%d" % i for i in range(VR + 1, NI)], ["uu"])
+        for u in range(3):
             rows, width, first = TILES[u]
-            quant(T.QC[:, first:first + width], T.SC[:, first:first + width], T.CT[:, 4 * first:4 * (first + width)],
-                  ["CT%s" % str(i) for i in rows], ["QC%d" % u], width)
-            mm(ps(2, 0, width), T.QG[:], T.SG[:], T.QC[:, first:first + width], T.SC[:, first:first + width],
-               ["QG", "QC%d" % u], ["B2"], width, start=(z == 0), stop=(z == 4))
+            quant("q%d" % u, T.QC[:, first:first + width], T.SC[:, first:first + width], T.CT[:, 4 * first:4 * (first + width)],
+                  ["CT%s" % str(i) for i in rows], ["QC%d" % u])
+        quant("q3", T.QC[:, 768:960], T.SC[:, 768:960], T.CT[:, 4 * 768:4 * 960], ["CT%d" % i for i in range(1, 9)], ["QC3", "QC4"])
+        for z, u in enumerate(PAR["pe"]):
+            first, width = TILES[u][2], max(TILES[u][1], M)
+            mm("mC%d" % u, ps(2, 0, width), T.QG[:], T.SG[:], T.QC[:, first:first + width], T.SC[:, first:first + width],
+               ["QG", "QC%d" % u], ["B2"], start=(z == 0), stop=(z == 4))
         if t > 0:
             new_y(t - 1, [4, 6, 4, 6], [5, 7, 5, 7])
         quant_y()
-        act(T.Yh[:], T.Yt[:], Act.Copy, kY, ["Yh"], 512, scale=0.5)
-        mm(ps(3, 0, M), T.Qg[:], T.Sg[:], T.QA[:, C:C + M], T.SA[:, C:C + M], kG + ["QY"], ["B3"], M)
-        tt(T.d3[:], ps(3, 0, M), T.Mk[:, 0:M], Alu.min, ["B3", "Mk"], ["d3"], M)
-        scan(T.Wm[:], T.K16[:, 0:M], T.d3[:], -BIG, Alu.min, Alu.max, ["K16", "d3"], ["Wm"], M)
-        tt(t1, T.RC[:], T.rd[:, 15:C:16], Alu.subtract, ["RC", "rd"], ["t1"], 2 * NI)
-        tt(t2, t1, T.RS[:], Alu.subtract, ["t1"] + ["RS%d" % i for i in range(NI)], ["t2"], 2 * NI)
-        tt(T.d2[:], ps(2, 0, C), T.Mk[:], Alu.min, ["B2", "Mk"], ["d2"], C)
-        scan(T.W2[:], T.K16[:], T.d2[:], -BIG, Alu.min, Alu.max, ["K16", "d2"], ["W2"], C)
-        tt(rk, T.W2[:, 15:C:16], t2, Alu.add, ["W2", "t2"], ["rk"], 2 * NI)
-        cp(T.roff[:], rk, ["rk"], ["roff"], NI)
-        cp(T.o2[:, 0:C].indirect(T.roff[:]), T.iO[:], ["roff", "iO"], ["o2a"], C * SCA)
-        cp(T.o2[:, C:2 * C], T.o2[:, 0:C], ["o2a"], ["o2b"], C / 2)
+        act("Yh", T.Yh[:], T.Yt[:], Act.Copy, kY, ["Yh"], scale=0.5)
+        mm("mS", ps(3, 0, M), T.Qg[:], T.Sg[:], T.QA[:, C:C + M], T.SA[:, C:C + M], kG + ["QY"], ["B3"])
+        tt("d3", T.d3[:], ps(3, 0, M), T.Mk[:, 0:M], Alu.min, ["B3", "Mk"], ["d3"])
+        scan("Wm", T.Wm[:], T.K16[:, 0:M], T.d3[:], -BIG, Alu.min, Alu.max, ["K16", "d3"], ["Wm"])
+        scan("W2", T.W2[:], T.A16[:], ps(2, 0, C), 0.0, Alu.mult, Alu.add, ["A16", "B2"], ["W2"])
+        tt("rk", rk, T.W2[:, 15:C:16], uu, Alu.subtract, ["W2", "uu"], ["rk"])
+        ts("roff", T.roff[:], rk, 0.25, None, Alu.add, None, ["rk"], ["roff"])
+        cp("o2a", T.o2[:, 0:C].indirect(T.roff[:]), T.iO[:], ["roff", "iO"], ["o2a"])
+        cp("o2b", T.o2[:, C:2 * C], T.o2[:, 0:C], ["o2a"], ["o2b"])
         for i in range(8):
             own = T.Wm[:, 16 * i + 15:16 * i + 16]
             if i in PAR["vmsg"]:
-                sk = "vg%d" % flip[1]
-                flip[1] ^= 1
-                ts(T[sk][:], ps(0, 0, C), own, None, Alu.is_gt, None, ["B0", "Wm"], [sk], C)
-                act(T[sk][:], T[sk][:], Act.Copy, [sk], ["n%d" % i, sk], C, accum_out=T.n[:, i:i + 1])
+                ts("f%d" % i, T.vg[:], ps(0, 0, C), own, None, Alu.is_gt, None, ["B0", "Wm"], ["vg"])
+                scan("g%d" % i, T.vb[:, C * i:C * i + C], T.vg[:], T.big[:], -128.0, Alu.add, Alu.min, ["vg", "big"], ["vb%d" % i])
+                ts("n%d" % i, T.n[:, i:i + 1], T.vb[:, C * i + C - 1:C * i + C], 128.0, None, Alu.add, None, ["vb%d" % i], ["n%d" % i])
             else:
-                sk = "sg%d" % flip[0]
-                flip[0] ^= 1
-                act(T[sk][:], ps(1, 0, C), Act.Sign, ["B1", "Wm"], [sk], C, bias=own, scale=-1.0)
-                act(T[sk][:], T[sk][:], Act.Relu, [sk], ["n%d" % i, sk], C, scale=-1.0, accum_out=T.n[:, i:i + 1])
-        for h in range(2):
-            zof, pos, pk = T["zof%d" % h], T.pos[:, 16 * h:16 * h + 16], "pof%d" % h
-            pof = T.pof[:, 16 * h:16 * h + 16]
-            tt(pos, T.n[:, 0:4 * h + 4].indirect(L16b if h else L16a), T.D16[:], Alu.add,
-               ["n%d" % i for i in range(4 * h + 4)] + ["L", "D16"], ["pos%d" % h], 16 * GA)
-            cp(pof, pos, ["pos%d" % h], [pk], 16)
-            tt(T.d4[:], T.o2[:].indirect(pof), T.Mk4[:], Alu.min, ["o2a", "o2b", pk, "Mk4"], ["d4"], n4 * GA)
-            scan(T.e4[:], T.K4[:], T.d4[:], -BIG, Alu.min, Alu.max, ["K4", "d4"], ["e4"], n4 / 2)
-            ts(zof[:], T.e4[:, 3:n4:4], t640, None, Alu.add, None, ["e4", "t640"], ["zof%d" % h], n4 / 4)
-            if h == 1:
-                tt(T.pos[:, 32:64], T.n[:].indirect(L32), T.D32[:], Alu.add, ["n%d" % i for i in range(8)] + ["L", "D32"], ["posA"], 32 * GA)
-                cp(T.pof[:, 32:64], T.pos[:, 32:64], ["posA"], ["pofA"], 32)
-                act(T.erep[:], T.o2[:].indirect(T.pof[:, 32:64]), Act.Copy, ["o2a", "o2b", "pofA"], ["erep"], 512 * GA)
+                sk = "sg%d" % (i % 2)
+                act("f%d" % i, T[sk][:], ps(1, 0, C), Act.Sign, ["B1", "Wm"], [sk], bias=own, scale=-1.0)
+                act("n%d" % i, T[sk][:], T[sk][:], Act.Relu, [sk], ["n%d" % i, sk], scale=-1.0, accum_out=T.n[:, i:i + 1])
+        for h, r in enumerate(CH):
+            i0, n = sum(CH[:h]), 64 * r
+            z0, pos, pk = 16 * i0, T.pos[:, 16 * h:16 * h + 16], "pof%d" % h
+            pof, er = T.pof[:, 16 * h:16 * h + 4 * r], T.er[:, 64 * i0:64 * i0 + n]
+            tt("pos%d" % h, pos, T.n[:, 0:i0 + r].indirect(T.L[:, 14 + 4 * h:15 + 4 * h]), T.D16[:, 16 * h:16 * h + 16], Alu.add,
+               ["n%d" % i for i in range(i0 + r)] + ["L", "D%d" % h], ["pos%d" % h])
+            cp(pk, pof, T.pos[:, 16 * h:16 * h + 4 * r], ["pos%d" % h], [pk])
+            if PAR["eg"][h] == "V":
+                cp("er%d" % h, er, T.o2[:].indirect(pof), ["o2a", "o2b", pk], ["er%d" % h])
+            else:
+                act("er%d" % h, er, T.o2[:].indirect(pof), Act.Copy, ["o2a", "o2b", pk], ["er%d" % h])
+            scan("e4%d" % h, T.e4[:, 0:n], T.A4[:, 0:n], er, 0.0, Alu.mult, Alu.add, ["A4", "er%d" % h], ["e4"])
+            ts("zof%d" % h, T.zof[:, z0:z0 + n // 4], T.e4[:, 3:n:4], t640, None, Alu.add, None, ["e4", "t640"], ["zof%d" % h])
             for k in range(F):
-                a = 512 * k + n4 * h
-                tt(T.Z[:, a:a + n4], T.Xh[:].indirect(zof[:, 16 * k:16 * k + 16]), T.Yh[:, n4 * h:n4 * h + n4], Alu.add,
-                   ["Xh", "Yh", "zof%d" % h], ["Z%d%d" % (k, h)], n4 * GA)
+                a, b = 512 * k + 64 * i0, 64 * i0 + 16 * r * k
+                tt("Z%d%d" % (k, h), T.Z[:, a:a + n], T.Xh[:].indirect(T.zof[:, z0 + 4 * r * k:z0 + 4 * r * (k + 1)]), T.Yh[:, 64 * i0:64 * i0 + n],
+                   Alu.add, ["Xh", "Yh", "zof%d" % h], ["Z%d%d" % (k, h)])
+                act("ec%d%d" % (k, h), T.erep[:, M * k + 16 * i0:M * k + 16 * (i0 + r)], T.er[:, b:b + 16 * r], ID,
+                    ["er%d" % h, "up"], ["ec%d%d" % (k, h)], scale=up)
         for k in range(F):
-            quant(QZ[:, M * k:M * k + M], SZ[:, M * k:M * k + M], T.Z[:, 512 * k:512 * k + 512],
-                  ["Z%d0" % k, "Z%d1" % k], ["QZ%d_%d" % (t, k)], M)
-            mm(ps(4 + k, 0, M), QZ[:, M * k:M * k + M], SZ[:, M * k:M * k + M], T.Qu[:], T.Su[:],
-               ["QZ%d_%d" % (t, k), "Qu"], ["B%d" % (4 + k)], M)
+            quant("qz%d" % k, QZ[:, M * k:M * k + M], SZ[:, M * k:M * k + M], T.Z[:, 512 * k:512 * k + 512],
+                  ["Z%d%d" % (k, h) for h in range(NC)], ["QZ%d_%d" % (t, k)])
+            mm("mZ%d" % k, ps(4 + k, 0, M), QZ[:, M * k:M * k + M], SZ[:, M * k:M * k + M], T.Qu[:], T.Su[:],
+               ["QZ%d_%d" % (t, k), "Qu"], ["B%d" % (4 + k)])
         kQZ = ["QZ%d_%d" % (t, k) for k in range(F)]
-        kZ = ["Z%d%d" % (k, h) for k in range(F) for h in range(2)]
-        scan(T.pre[:, 5:9], T.ps[:, 2049:4096:512], T.nb[:], -BIG, Alu.max, Alu.max, ["B4", "B5", "B6", "B7", "nb"], ["pre"], 4)
-        ts(T.FT[:, 0:32], T.pre[:, 0:8].indirect(LF), T.pre[:, 8:9], None, Alu.is_lt, None, ["pre", "L"], ["FT"], 32 * GA)
-        quant(T.QF[:], T.SF[:], T.FT[:], ["FT"], ["QF"], M)
-        mm(ps(3, 0, M), T.QR[:], T.SR[:], T.QF[:], T.SF[:], ["QR", "QF"], ["B3"], M)
-        tt(T.zi[:], ps(3, 0, 8), T.jc[:], Alu.add, ["B3", "jc"], ["zi"], 8)
-        cp(T.ziu[:], T.zi[:], ["zi"], ["ziu"], 8)
-        cp(QH[:].bitcast(dt.uint32), QZ[:].bitcast(dt.uint32).indirect(T.ziu[:]), kQZ + ["ziu"], ["QH%d" % t], M * GA)
-        act(SH[:], SZ[:].indirect(T.ziu[:]), Act.Copy, kQZ + ["ziu"], ["SH%d" % t], M * GA)
+        kZ = ["Z%d%d" % (k, h) for k in range(F) for h in range(NC)]
+        kE = ["ec%d%d" % (k, h) for k in range(F) for h in range(NC)]
+        scan("pre", T.pre[:, 5:9], T.ps[:, 2049:4096:512], T.nb[:], -BIG, Alu.max, Alu.max, ["B4", "B5", "B6", "B7", "nb"], ["pre"])
+        ts("FT", T.FT[:, 0:32], T.pre[:, 0:8].indirect(LF), T.pre[:, 8:9], None, Alu.is_lt, None, ["pre", "L"], ["FT"])
+        quant("qF", T.QF[:], T.SF[:], T.FT[:], ["FT"], ["QF"])
+        mm("mF", ps(3, 0, M), T.QR[:], T.SR[:], T.QF[:], T.SF[:], ["QR", "QF"], ["B3"])
+        tt("zi", T.zi[:], ps(3, 0, 8), T.jc[:], Alu.add, ["B3", "jc"], ["zi"])
+        cp("ziu", T.ziu[:], T.zi[:], ["zi"], ["ziu"])
+        cp("QH", QH[:].bitcast(dt.uint32), QZ[:].bitcast(dt.uint32).indirect(T.ziu[:]), kQZ + ["ziu"], ["QH%d" % t])
+        act("SH", SH[:], SZ[:].indirect(T.ziu[:]), Act.Copy, kQZ + ["ziu"], ["SH%d" % t])
         arr = T.sem["arr%d" % t]
-        add("G", lambda a=T["SL%d" % t][:], b=SH[:], s=arr: G.remote_dma(a, b, s, T.sem.sent, pid, rid, mask),
-            ["SH%d" % t], ["sentS%d" % t], 600.0, 2000.0, "remote")
-        add("G", lambda a=T["QL%d" % t][:].bitcast(dt.uint8), b=QH[:].bitcast(dt.uint8), s=arr:
-            G.remote_dma(a, b, s, T.sem.sent, pid, rid, mask), ["QH%d" % t], ["sentQ%d" % t], 600.0, 2600.0, "remote")
-        add("A", None, ["sentS%d" % t, "sentQ%d" % t], ["land%d" % t], 0.0, 0.0, "arr%d" % t, 2 * ne)
-        act(T.junk[:, 3040:3072], T.FT[:, 0:32], Act.Copy, ["FT"], ["okc%d" % t, "jk"], 32, accum_out=T.okc[:, t:t + 1])
-        dma("Y", T.ok[t], T.okc[:, t:t + 1], ["okc%d" % t], [], "outh")
-        act(T.ew[:], T.erep[:].indirect(T.ziu[:]), Act.Copy, ["erep", "ziu"], ["ew"], M * GA)
-        tt(T.hf[:], T.zi[:].indirect(L32), T.tq[:], Alu.add, ["zi", "tq", "L"], ["hf"], 32 * GA)
-        ts(T.hof[:], T.hf[:], 4.0, None, Alu.mult, None, ["hf"], ["hof"], 32)
-        act(T.Hp[:], T.Z[:].indirect(T.hof[:]), Act.Copy, kZ + ["hof"], ["Hp"], 512 * GA)
-        tt(T.d5[:], T.erep[:].indirect(T.ziu[:]), T.Mk[:, 0:M], Alu.min, ["erep", "ziu", "Mk"], ["d5"], M * GA)
-        scan(T.ews[:], T.K16[:, 0:M], T.d5[:], -BIG, Alu.min, Alu.max, ["K16", "d5"], ["ews"], M / 2)
+        add("sendS", "G", lambda a=T["SL%d" % t][:], b=SH[:], s=arr: G.remote_dma(a, b, s, T.sem.sent, pid, rid, mask),
+            ["SH%d" % t], ["sentS%d" % t], "remote")
+        add("sendQ", "G", lambda a=T["QL%d" % t][:].bitcast(dt.uint8), b=QH[:].bitcast(dt.uint8), s=arr:
+            G.remote_dma(a, b, s, T.sem.sent, pid, rid, mask), ["QH%d" % t], ["sentQ%d" % t], "remote")
+        add("land", "A", None, ["sentS%d" % t, "sentQ%d" % t], ["land%d" % t], "arr%d" % t, 2 * ne, late=1)
+        act("okc", T.a2[:, 0:32], T.FT[:, 0:32], Act.Copy, ["FT"], ["okc%d" % t, "a2"], accum_out=T.okc[:, t:t + 1])
+        dma("ok", "Y", T.ok[t], T.okc[:, t:t + 1], ["okc%d" % t], [], "outh")
+        act("ew", T.ew[:], T.erep[:].indirect(T.ziu[:]), ID, kE + ["ziu", "dn16"], ["ew"], scale=T.cG[:, 12:13])
+        tt("hf", T.hf[:], T.zi[:].indirect(L32), T.tq[:], Alu.add, ["zi", "tq", "L"], ["hf"])
+        ts("hof", T.hof[:], T.hf[:], 4.0, None, Alu.mult, None, ["hf"], ["hof"])
+        act("Hp", T.Hp[:], T.Z[:].indirect(T.hof[:]), Act.Copy, kZ + ["hof"], ["Hp"])
+        scan("ews", T.ews[:], T.A16[:, 0:M], T.ew[:], 0.0, Alu.mult, Alu.add, ["A16", "ew"], ["ews"])
         for i in range(8):
             w = 16 * (i + 1)
-            ts(T.EQ[:, SEG[i]:SEG[i + 1]], T.ew[:, 0:w], T.ews[:, w - 1:w], None, Alu.is_equal, None, ["ew", "ews"], ["EQ%d" % i], w / 2)
-        tt(T.e1[:], T.ews[:].indirect(L32e), T.tc[:], Alu.add, ["ews", "tc", "L"], ["e1"], 32 * GA)
-        scan(T.st[:], T.A[:], T.EQ[:], 0.0, Alu.mult, Alu.max, ["A"] + ["EQ%d" % i for i in range(8)], ["st"], 288)
-        tt(T.e2[:], T.st[:].indirect(LEND), T.e1[:], Alu.add, ["st", "e1", "L"], ["e2"], 32 * GA)
-        tt(T.e3[:], T.e2[:], T.dum[:], Alu.min, ["e2", "dum"], ["e3"], 64)
-        cp(T.xof[:], T.e3[:], ["e3"], ["xof"], 32)
-        cp(T.Xt[:].indirect(T.xof[:]), T.Hp[:], ["xof", "Hp"] + kX, kX, 512 * SCA)
+            ts("EQ%d" % i, T.EQ[:, SEG[i]:SEG[i + 1]], T.ew[:, 0:w], up16, T.ews[:, w - 1:w], Alu.mult, Alu.is_equal,
+               ["ew", "ews", "wb"], ["EQ%d" % i])
+        for c in range(4):
+            act("e1%d" % c, T.e[:, 8 * c:8 * c + 8], T.ews[:, 15:M:16], ID, ["ews"], ["e1%d" % c], bias=float(MID - 1 + c))
+        scan("st", T.st[:], T.A[:], T.EQ[:], 0.0, Alu.mult, Alu.max, ["A"] + ["EQ%d" % i for i in range(8)], ["st"])
+        tt("e2", T.e[:, 32:64], T.st[:].indirect(LEND), T.e[:, 0:32], Alu.add, ["st", "L"] + ["e1%d" % c for c in range(4)], ["e2"])
+        tt("e3", T.e[:, 64:96], T.e[:, 32:64], T.dum[:], Alu.min, ["e2", "dum"], ["e3"])
+        cp("xof", T.xof[:], T.e[:, 64:96], ["e3"], ["xof"])
+        cp("X", T.Xt[:].indirect(T.xof[:]), T.Hp[:], ["xof", "Hp", "gap"] + kX, kX)
 
+    at[0] = R
     new_y(R - 1, [4, 5, 6, 7], [0, 1, 2, 3])
     quant_y()
     quant_x()
-    for key, a, z, b in (("QY", C, C + M, 4), ("QX", 0, C, 5)):
-        mm(ps(b, 0, z - a), T.Qv[:], T.Sv[:], T.QA[:, a:z], T.SA[:, a:z], ["Qv", key], ["B%d" % b], z - a)
-        dma("Y", T.oc[:, 4 * a:4 * z], T.QA[:, a:z].bitcast(dt.uint8), [key], [], "outh")
-        act(T.ysb[:, a:z], ps(b, 0, z - a), Act.Copy, ["B%d" % b], ["ysb" + key], z - a)
-        dma("S", T.y[:, a:z], T.ysb[:, a:z], ["ysb" + key], [], "outh")
+    for key, a, z, b, k in (("y", C, C + M, 4, ["QY"]), ("x", 0, C, 5, ["QX0", "QX1"])):
+        mm("mv" + key, ps(b, 0, z - a), T.Qv[:], T.Sv[:], T.QA[:, a:z], T.SA[:, a:z], ["Qv"] + k, ["B%d" % b])
+        dma("oc" + key, "Y", T.oc[:, 4 * a:4 * z], T.QA[:, a:z].bitcast(dt.uint8), k, [], "outh")
+        act("ys" + key, T.ysb[:, a:z], ps(b, 0, z - a), Act.Copy, ["B%d" % b], ["ysb" + key])
+        dma("oy" + key, "S", T.y[:, a:z], T.ysb[:, a:z], ["ysb" + key], [], "outh")
     for k in range(4):
-        dma("G" if k == 3 else "Y", T.osc[4 * k:4 * k + 4, :], T.SA[32 * k:32 * k + 4, :], ["QX", "QY"], [],
+        dma("os%d" % k, "G" if k == 3 else "Y", T.osc[4 * k:4 * k + 4, :], T.SA[32 * k:32 * k + 4, :], ["QX0", "QX1", "QY"], [],
             "outg" if k == 3 else "outh")
     return ops, ne
 
@@ -369,48 +436,29 @@ def depend(ops):
             readers[k] = []
 
 
-def name(o):
-    k = (o["w"] or o["r"])[0]
-    if k.startswith("sg") or k.startswith("vg"):
-        k = k[:2] + o["r"][1]
-    if k[:2] in ("QZ", "QH", "SH"):
-        k = k[:2] + k[3:]
-    return o["e"] + k
-
-
-def plan(ops):
-    n, WAKE, off = len(ops), PAR["wake"], PAR["off"]
-    level = [o["lat"] for o in ops]
-    key = [0.0] * n
-    low = [0.0] * n
-    for i in range(n - 1, -1, -1):
-        o = ops[i]
-        key[i] = max(level[i] + 100.0 * off.get(name(o), 0), low[i])
-        for j in o["d"]:
-            level[j] = max(level[j], level[i] + WAKE + ops[j]["lat"])
-            low[j] = max(low[j], key[i] + 1e-3)
-    line = {e: [] for e in "VSPGYA"}
-    for i in sorted(range(n), key=lambda i: (-key[i], i)):
-        o = ops[i]
-        t = 0.0
-        for j in o["d"]:
-            p = ops[j]
-            t = max(t, p["t0"] + p["lat"] + (0.0 if p["e"] == "P" and o["e"] == "P" else WAKE))
-        ln, d = line[o["e"]], o["busy"]
-        k = len(ln)
-        while k > 0 and ln[k - 1][1] > t:
-            k -= 1
-        while k < len(ln) and t + d > ln[k][0]:
-            t = max(t, ln[k][1])
-            k += 1
-        ln.insert(k, (t, t + d))
-        o["t0"] = t
-    return sorted(range(n), key=lambda i: (ops[i]["t0"], i))
+def merge(ops):
+    q = {}
+    for i, o in enumerate(ops):
+        q.setdefault(o["e"], []).append(i)
+    for e in q:
+        q[e].sort(key=lambda i: (ops[i]["at"], ORDER[ops[i]["at"]][e].split().index(ops[i]["name"])))
+    head, done, order = {e: 0 for e in q}, set(), []
+    while len(order) < len(ops):
+        moved = False
+        for e in q:
+            while head[e] < len(q[e]) and all(j in done for j in ops[q[e][head[e]]]["d"]):
+                done.add(q[e][head[e]])
+                order.append(q[e][head[e]])
+                head[e] += 1
+                moved = True
+        assert moved
+    return order
 
 
 def emit(g, T, ops, order, ne):
     queue = {"V": g.vector, "S": g.scalar, "P": g.tensor, "G": g, "Y": g.sync}
     seq, cnt = {}, {}
+    place = {i: k for k, i in enumerate(order)}
     for i in order:
         o = ops[i]
         if o["sem"] is None:
@@ -425,7 +473,7 @@ def emit(g, T, ops, order, ne):
             clock[i] = {o["sem"]: 1}
             continue
         kn, ws = known[e], []
-        for j in sorted(o["d"], key=lambda j: -ops[j]["t0"]):
+        for j in sorted(o["d"], key=lambda j: -place[j]):
             p = ops[j]
             if p["e"] == "P" and e == "P":
                 continue
@@ -486,4 +534,4 @@ def rank_program(g, core, T, topo):
         return
     ops, ne = build(g, core, T, topo)
     depend(ops)
-    emit(g, T, ops, plan(ops), ne)
+    emit(g, T, ops, merge(ops), ne)

@@ -4,17 +4,19 @@ C, M, F, R = 320, 128, 4, 3
 NI = C // 16
 BIG = 2.0 ** 96
 K16W, K4W = 2.0 ** 30, 2.0 ** 13
-SEG = [8 * i * (i + 1) for i in range(9)]
+SEG = [160 * (i // 4) + 8 * (i % 4) * (i % 4 + 1) for i in range(9)]
 HI = 192
 GAP = 8
 XE = 4 * C + GAP
 MID = 4 * HI + 4
+HOLD = 1024.0
+SPARE = XE + 24
 SW = 384
+VR = 12
 
 TILES = [(("d", 19, 18, 17), 320, 0), ((16, 15, 14, 13), 256, 320), ((9, 10, 11, 12), 192, 576),
          ((5, 6, 7, 8), 128, 768), ((1, 2, 3, 4), 64, 896)]
 PAR = {
-    "vrows": 12,
     "vmsg": (0, 4),
     "chunks": (4, 4),
     "eg": "VS",
@@ -24,11 +26,11 @@ PAR = {
 Q4, U8, BF, F32, I32, U16 = "float8_e4m3fn_x4", "uint8", "bfloat16", "float32", "int32", "uint16"
 SCRATCH = {"ps": ("psum", [128, 4096], F32)}
 for _d, _l in (
-        (BF, "Xt:1800 Xh:1288 Yt:512 Yh:512 Z:2048 ut:512 vt:512 CT:4096 FT:512 Et:2048 Gi:512 Gt:512 Ri:512 Rt:512 j16:320 Mk:320 "
-             "K16:320 keep:320 A16:320 a1:320 a2:320 big:320 j4:256 A4:256 w4:16 Ai:576 A:576 iO:320 iP:320 sg0:320 sg1:320 vg:320 "
-             "vb:2560 rs:1538 kq:384 rd:320 o2:640 er:512 e4:256 erep:512 Hp:512 ew:128 ews:128 EQ:576 st:576"),
-        (F32, "cF:8 cG:16 Lf:24 i16:32 RC:20 jc:8 dum:32 ti:32 tq:32 nb:4 kF:16 dk:16 D16:48 qf:16 d1:320 W:320 s4:16 "
-              "W2:320 d3:128 Wm:128 RS:20 tr:60 n:8 pos:48 pre:16 okc:4 zi:8 hf:32 e:96 Rr:512 ysb:448"),
+        (BF, "Xt:3344 Xh:1288 Yt:512 Yh:512 Z:2048 ut:512 vt:512 CT:4096 FT:512 Et:2048 Gi:512 Gt:512 Ri:512 Rt:512 j16:320 Mk:320 "
+             "K16:320 keep:320 A16:128 a1:128 a2:128 mM:320 ab:16 big:320 j4:256 A4:256 w4:16 A:320 iO:320 iP:320 sg:2240 sm:2560 "
+             "vb:2560 rs:1538 kq:384 rd:320 o2:640 er:512 e4:512 jk:32 erep:512 Hp:512 ew:128 ews:128 EQ:320 st:320"),
+        (F32, "cF:8 cG:24 Lf:24 i16:32 RC:20 D1:320 Dc:16 h4:4 nb:4 kF:16 dk:16 D16:48 qf:16 d1:320 W:320 s4:16 "
+              "W2:320 d3:128 Wm:128 RS:20 tr:20 n:8 pos:48 pre:16 okc:8 e:64 Rr:512 ysb:448"),
         (I32, "pI:16 cI:8 kI:16 qI:8"),
         (U16, "uL:8 L:24 roff:20 pof:48 zof:128 ziu:8 hof:32 xof:32")):
     for _e in _l.split():
@@ -42,29 +44,39 @@ SEMAPHORES = ["cV", "cS", "cP", "cG", "lu", "lx0", "lx1", "lm", "lv", "lwc", "lw
               "arr0", "arr1", "arr2"]
 
 FIRST = {
-    "V": "kq0 CT4 cI4 cI2 CT3 cI3 uL kq1 CT1 cI1 cI6 pm cI0 CT0 cF big kq2 Mk0 dn16 qpad CT2 nb rs0 qu qx1 FT0 Qg qx0 Mk sz pma "
-         "Lf0 dH dL WH WL pmb cG81 qy c1 pmf c11 qI qv c7 c3 c2 cG10 c10 c9 c8 d3 c6 kF c12 dg cG6 q2 gap Wm w4b c5 Lq cG80 f0 "
-         "w4a rd Lf10 s1 a2 s2 Ls down s0 qG t1 L c4 q0 s3 q3 q1 A16 ua g0 W2 ub f4 rk n0 A4 pos0 roff g4 o2a pof0 o2b n4 pre0 "
-         "er0 pos1 wb e40 pof1 zof0 up up16 Z30 Z10 e41 Z20 zof1 Z00 Z21 Z31 Z01 qz2 Z11 qz3 qz1 qz0 qR qE2 pre FT qF zi ziu hf "
-         "QH qE3 ews qE1 EQ6 EQ7 EQ5 EQ1 EQ2 EQ4 EQ0 EQ3 hof st e2 qE0 e3 xof X",
-    "S": "lx1 lm keep neg t640 cG4 cG2 qf0 qg1 qf1 a0 K16 Sg Gt0 Yh Gt1 a19 Lf8 rc1 Gu2 jc Gu0 RC Gu1 b19 sq a18 a17 b18 b17 se "
-         "a16 a15 b16 Gu3 b15 Lf4 qg0 a13 sp Lr0 b13 Lr1 a14 f1 b14 n1 a1 f2 f3 n3 D0 n2 f5 iO n5 f6 f7 D1 n6 n7 Xh er1 Rt0 tq "
-         "Rt1 A0 ec31 ec10 A1 cG3 ec20 ec21 ec01 ec30 A2 ec00 ec11 ew SH e12 e10 okc e13 dum e11 Hp",
-    "P": "mH m0 m1 mS mC0 mC3 mC4 mC2 mC1 mZ2 mZ3 mZ1 mZ0 mF",
-    "G": "uI pI j16 i16 Gi kI Ai1 Ai6 iP0 Ai4 j4 iP1 Ri Ai2 Ai0 Ai3 dk Ai7 Ai5 Et0 ti Et1 Az1 Az2 Az3 Az4 Az5 Az6 Az7 sendQ sendS",
+    "V": "kq0 CT3 CT0 cI5 cI0 cI4 cI2 cI1 cI3 pm CT2 cF pmb kq1 dn16 pma CT1 pmf kq2 rs0 z1 z0 CT4 big uL qpad Lf0 Mk0 gap qu qI "
+         "Mk own qx1 Qg qy qx0 sz Lq dH FT0 WH wb w4b dL D1 WL c12 c6 c1 dg c2 d3 c8 qG c4 c10 c9 A4 w4a kF c3 Ls Wm s3 c5 qv c7 "
+         "c11 rd q0 t1 s1 La s0 s2 q3 down q2 L q1 ua f4 ub f0 W2 nb g0 roff a2 n0 o2a pos0 g4 o2b pof0 n4 er0 pos1 e40 pof1 up "
+         "zof0 Z20 Z30 e41 Z00 zof1 Z10 Z11 Z01 Z21 Z31 qz2 qz0 qz1 qz3 pre0 qR A16 pre Fa Fb qE0 qF ziu hof2 hof3 hof0 up16 QH "
+         "hof1 ews EQ7 EQ4 EQ6 EQ5 EQ1 EQ3 EQ2 EQ0 st1 st0 e21 qE3 e20 xo21 xo31 xo11 xo01 xo00 xo10 xo20 xo30 XA qE2 X qE1",
+    "S": "lm lx1 qg0 neg t640 qg1 qf0 cG4 b5 qf1 keep cG2 rc1 sq a0 z3 z2 se K16 Yh Sg Gt0 Lb mM sp Gt1 a19 cG3 a15 a18 a13 a14 "
+         "Le b18 a17 b19 RC b17 Lr0 Lr1 a16 f2 b13 b14 b16 f5 b15 f1 f3 f7 n2 iO D0 n1 n3 f6 n7 n6 D1 n5 Xh h41 p16 er1 h43 ec00 "
+         "h40 ec10 Dc ec20 Dn w2 ab Ad5 w3 Rt0 ec30 a1 Rt1 Ad0 Ad1 ec11 Ad4 Ru1 Ru3 Ad6 Ru2 ec01 h42 Ru0 ec31 Ad7 Ad2 Ad3 p256 "
+         "ec21 A2 oka ew okb SH e11 Hp0 e10 Hp1 okc",
+    "P": "mH m0 mS m1 mC0 mC3 mC4 mC2 mC1 mZ2 mZ0 mZ1 mZ3 mF",
+    "G": "pI j16 uI Gi j4 A0 kI i16 Ri iP1 iP0 dk Et0 Et1 Az1 Az2 Az3 Az5 Az6 Az7 sendQ sendS",
     "Y": "lu lx0 lv lwc lws ok"}
 STEADY = {
-    "V": "qx1 qx0 dH WH dL c12 WL Y1 dg c7 c11 c9 Y0 rd c10 c3 c4 Y3 c1 Y2 s2 c2 t1 qy q2 c5 c8 d3 c6 Wm q0 q3 s1 s3 q1 s0 f0 W2 "
-         "ua g0 ub n0 rk f4 roff pos0 o2a pof0 o2b g4 er0 n4 e40 pos1 zof0 pof1 Z30 Z10 e41 Z00 zof1 Z20 Z01 Z11 Z31 Z21 qz0 qz1 "
-         "qz2 qz3 pre FT qF zi ziu hf QH ews hof EQ0 EQ4 EQ3 EQ7 EQ6 EQ1 EQ2 EQ5 st e2 e3 xof X",
-    "S": "Xh Rr1 a19 a18 b19 Rr0 a17 Rr3 b17 Rr2 b18 a15 a16 b15 b16 a13 a14 b13 b14 f1 f2 n1 n2 f3 n3 f6 f5 n6 n5 f7 n7 Yh er1 "
-         "ec10 ec30 ec11 ec31 ec01 ec00 okc ec20 ec21 ew SH e11 e10 e12 e13 Hp",
-    "P": "mH m0 m1 mW1 mE0 mE1 mW3 mW0 mW2 mE3 mE2 mS mC0 mC3 mC4 mC2 mC1 mZ0 mZ1 mZ2 mZ3 mF",
-    "G": "sendQ sendS", "Y": "ok", "A": "land<"}
+    "V": "qx1 qx0 dH WH dL c12 WL c1 c10 c4 dg c8 c2 rd c6 c9 c7 c3 Y1 Y0 s3 t1 c5 Y3 Y2 q3 qy c11 s1 s0 d3 s2 Wm q0 ua q2 q1 ub "
+         "f0 f4 W2 g0 roff n0 o2a pos0 o2b pof0 g4 er0 n4 e40 pos1 zof0 pof1 Z20 Z10 e41 Z00 zof1 Z30 Z21 Z01 Z31 Z11 qz3 qz2 "
+         "qz0 qz1 pre Fb Fa qF ziu hof1 QH hof3 ews hof2 hof0 EQ7 EQ4 EQ6 EQ5 EQ0 EQ1 EQ3 EQ2 st1 st0 e21 e20 xo01 xo31 xo11 "
+         "xo21 xo10 xo00 xo20 xo30 XA X",
+    "S": "Xh a14 a17 a18 b17 a15 a19 Rr1 Rr0 b14 Rr3 Rr2 b18 a16 b15 b19 a13 b16 b13 f7 f1 f3 f2 n1 f5 n2 n3 f6 n5 n7 n6 Yh er1 "
+         "ec31 ec10 ec21 ec01 ec11 ec30 oka okb ec00 ec20 ew e11 e10 SH Hp1 okc Hp0",
+    "P": "mH m0 m1 mW1 mW0 mE0 mE1 mW3 mW2 mE3 mE2 mS mC0 mC3 mC4 mC2 mC1 mZ3 mZ2 mZ0 mZ1 mF",
+    "G": "sendQ sendS", "Y": "ok", "A": "land"}
 LAST = {
-    "V": "qx0 qx1 Y3 Y0 Y1 Y2 qy", "S": "Rr3 Rr0 Rr1 Rr2 ysx oyx ysy oyy", "P": "mE1 mW3 mW0 mE3 mW1 mE2 mE0 mW2 mvx mvy",
-    "G": "os3", "Y": "ocx os0 os1 os2 ocy", "A": "land<"}
-ORDER = [FIRST, STEADY, STEADY, LAST]
+    "V": "qx1 qx0 dH dL WH WL c12 Y1 c6 c4 c2 dg Y0 c3 c1 c11 c10 c7 rd Y2 c5 t1 Y3 c9 c8 qy s0 s3 s1 d3 s2 q2 Wm q0 ua q3 q1 ub "
+         "f4 f0 W2 g0 roff n0 o2a pos0 o2b pof0 g4 er0 n4 e40 pos1 zof0 pof1 Z20 Z00 e41 Z10 zof1 Z30 Z21 Z11 qz2 Z31 Z01 qz3 "
+         "qz1 qz0 pre Fa Fb qF ziu QH hof1 hof2 ews hof3 EQ7 EQ6 EQ2 EQ4 EQ5 EQ0 EQ1 EQ3 st1 hof0 st0 e21 e20 xo21 xo11 xo31 "
+         "xo30 xo01 xo10 xo00 xo20 XA X qx0! Y0! Y1! Y3! Y2! qx1! qy!",
+    "S": "Xh Rr1 Rr0 a14 a16 Rr2 a18 a13 a17 b13 Rr3 a15 a19 b18 b19 b14 b17 b16 b15 f1 f3 n1 f2 f6 f5 n3 n2 f7 n6 n7 n5 Yh ec00 "
+         "er1 ec21 ec20 ec30 ec10 ec01 ec11 ec31 okb ew SH e11 oka e10 Hp1 Hp0 okc Rr0! Rr1! Rr3! Rr2! ysX0! oyX0! ysX1! ysY! "
+         "oyX1! oyY!",
+    "P": "mH m0 m1 mW1 mW0 mE1 mE0 mW2 mE2 mW3 mE3 mS mC0 mC3 mC4 mC2 mC1 mZ2 mZ3 mZ1 mZ0 mF mW0! mW1! mE0! mW3! mW2! mE1! mE3! "
+         "mE2! mvX0! mvX1! mvY!",
+    "G": "sendQ sendS os3!", "Y": "ok ocX! os2! ocY! os1! os0!", "A": "land land!"}
+ORDER = [FIRST, STEADY, LAST]
 
 
 def build(g, core, T, topo):
@@ -76,10 +88,10 @@ def build(g, core, T, topo):
     ne = len(topo.engines(core, nxt))
     ops = []
     V, S, P, G, Y = g.vector, g.scalar, g.tensor, g, g.sync
-    at = [0]
+    at = [0, ""]
 
-    def add(name, eng, fn, r, w, sem=None, n=16, late=0):
-        ops.append({"name": name + "<" * late, "at": at[0] + late, "e": eng, "f": fn, "r": list(r), "w": list(w), "sem": sem, "n": n})
+    def add(name, eng, fn, r, w, sem=None, n=16):
+        ops.append({"name": name + at[1], "at": at[0], "e": eng, "f": fn, "r": list(r), "w": list(w), "sem": sem, "n": n})
 
     def ps(b, a, z):
         return T.ps[:, 512 * b + a:512 * b + z]
@@ -122,7 +134,6 @@ def build(g, core, T, topo):
         add(name, q, lambda: e.dma_start(out, in_), r, w, sem)
 
     ID = Act.Identity
-    VR = PAR["vrows"]
 
     dma("lu", "Y", T.ut[:], T.u[:], [], ["ut"], "lu")
     dma("lx1", "S", T.Xt[:, 4 * HI + GAP:XE], T.x[:, 4 * HI:4 * C], [], ["X1"], "lx1")
@@ -136,10 +147,10 @@ def build(g, core, T, topo):
     iota("uI", T.pI[:, 8:16], [[16, 8]], 0, 0, ["uI"], flt=False)
     cp("uL", T.uL[:], T.pI[:, 8:16], ["uI"], ["uL"])
     iota("pI", T.pI[:, 0:8], [[0, 8]], 0, 1, ["pI"], flt=False)
-    for a, z, sh, an in [(0, 1, 0, 15), (1, 2, 4, 7), (2, 3, 2, 3), (3, 4, 0, 3), (4, 6, 0, 7), (6, 8, 3, 1)]:
-        ts("cI%d" % a, T.cI[:, a:z], T.pI[:, a:z], sh, an, Alu.logical_shift_right, Alu.bitwise_and, ["pI"], ["cI%d" % a])
-    cp("cF", T.cF[:], T.cI[:], ["cI%d" % c for c in (0, 1, 2, 3, 4, 6)], ["cF"])
-    rc, gc_, r4, t4 = [T.cF[:, c:c + 1] for c in range(4)]
+    for a, sh, an in [(0, 0, 15), (1, 4, 7), (2, 2, 3), (3, 0, 3), (4, 1, 7), (5, 0, 1)]:
+        ts("cI%d" % a, T.cI[:, a:a + 1], T.pI[:, a:a + 1], sh, an, Alu.logical_shift_right, Alu.bitwise_and, ["pI"], ["cI%d" % a])
+    cp("cF", T.cF[:, 0:6], T.cI[:, 0:6], ["cI%d" % c for c in range(6)], ["cF"])
+    rc, gc_, r4, t4, h2, b2 = [T.cF[:, c:c + 1] for c in range(6)]
     act("neg", T.cG[:, 0:2], T.cF[:, 0:2], Act.Copy, ["cF"], ["neg"], scale=-1.0)
     nr, ng = T.cG[:, 0:1], T.cG[:, 1:2]
     iota("j16", T.j16[:], [[0, NI], [1, 16]], 0, 0, ["j16"])
@@ -147,11 +158,18 @@ def build(g, core, T, topo):
     ts("Mk", T.Mk[:], T.Mk[:], 2 * BIG, None, Alu.mult, None, ["Mk"], ["Mk"])
     act("keep", T.keep[:], T.j16[:], Act.Sign, ["j16"], ["keep"])
     act("K16", T.K16[:], T.keep[:], ID, ["keep"], ["K16"], scale=2 * BIG, bias=-BIG)
-    act("a0", T.a1[:], T.j16[:], Act.Abs, ["j16", "neg"], ["a1"], bias=nr)
+    act("a0", T.a1[:], T.j16[:, 0:M], Act.Abs, ["j16", "neg"], ["a1"], bias=nr)
+    act("ab", T.ab[:], T.a1[:, 0:16], Act.Copy, ["a1"], ["ab"])
     act("a1", T.a1[:], T.a1[:], Act.Sign, ["a1"], ["a1"])
     act("rc1", T.cG[:, 11:12], rc, ID, ["cF"], ["rc1"], bias=1.0)
-    ts("a2", T.a2[:], T.j16[:], T.cG[:, 11:12], K16W, Alu.is_equal, Alu.mult, ["j16", "rc1"], ["a2"])
+    ts("a2", T.a2[:], T.j16[:, 0:M], T.cG[:, 11:12], K16W, Alu.is_equal, Alu.mult, ["j16", "rc1"], ["a2"])
     tt("A16", T.A16[:], T.a1[:], T.a2[:], Alu.max, ["a1", "a2"], ["A16"])
+    act("mM", T.mM[:], T.Mk[:], Act.Relu, ["Mk"], ["mM"], scale=HOLD / BIG)
+    tt("D1", T.D1[:, 0:C - 1], T.mM[:, 1:C], T.mM[:, 0:C - 1], Alu.subtract, ["mM"], ["uu"])
+    ts("z0", T.cG[:, 13:14], rc, 0.0, HOLD, Alu.is_equal, Alu.mult, ["cF"], ["z0"])
+    ts("z1", T.cG[:, 14:15], rc, 15.0, HOLD, Alu.is_lt, Alu.mult, ["cF"], ["z1"])
+    act("z2", T.cG[:, 15:16], T.cG[:, 13:14], ID, ["z0"], ["z2"], scale=-1.0, bias=0.25)
+    act("z3", T.cG[:, 16:17], T.cG[:, 13:14], ID, ["z0", "z1"], ["z3"], bias=T.cG[:, 14:15])
     up16 = T.w4[:, 14:15]
     ts("wb", up16, rc, 15.0, K16W, Alu.is_lt, Alu.mult, ["cF"], ["wb"])
     ts("up16", up16, up16, 1.0, None, Alu.max, None, ["wb"], ["wb"])
@@ -165,16 +183,12 @@ def build(g, core, T, topo):
     iota("Gi", T.Gi[:], [[1, 8], [0, 64]], 0, 0, ["Gi"])
     add("kI", "G", lambda: G.dma_start(T.kI[0:1, :], T.kap[:], allow_slow_non_contiguous=True), ["Gi"], ["kI"], "lk")
     act("Gt0", T.Gt[:], T.Gi[:], Act.Abs, ["Gi", "neg"], ["Gt"], bias=ng)
-    act("Gt1", T.Gt[:], T.Gt[:], Act.Relu, ["Gt"], ["Gt"], bias=1.0 / K16W, scale=-1.0)
-    for c in range(4):
-        act("Gu%d" % c, T.Gt[:, 60 + c:512:64], T.Gt[:, 60 + c:512:64], Act.Copy, ["Gt"], ["Gu%d" % c], scale=K16W)
-    quant("qG", T.QG[:], T.SG[:], T.Gt[:], ["Gt"] + ["Gu%d" % c for c in range(4)], ["QG"])
+    act("Gt1", T.Gt[:], T.Gt[:], Act.Relu, ["Gt"], ["Gt"], bias=1.0, scale=-1.0)
+    quant("qG", T.QG[:], T.SG[:], T.Gt[:], ["Gt"], ["QG"])
     iota("i16", T.i16[:], [[16, 32]], 0, 0, ["i16"])
     act("cG2", T.cG[:, 2:3], rc, ID, ["cF"], ["cG2"], scale=-1.0, bias=15.0)
-    act("RC", T.RC[:], T.i16[:, 0:NI], ID, ["i16", "cG2"], ["RC"], bias=T.cG[:, 2:3])
-    act("jc", T.jc[:], T.i16[:, 0:8], ID, ["i16", "cF"], ["jc"], bias=rc)
-    act("cG3", T.cG[:, 3:4], rc, ID, ["cF"], ["cG3"], bias=float(XE))
-    act("dum", T.dum[:], T.i16[:], ID, ["i16", "cG3"], ["dum"], bias=T.cG[:, 3:4])
+    act("cG3", T.cG[:, 3:4], T.cG[:, 2:3], ID, ["cG2", "z3"], ["cG3"], bias=T.cG[:, 16:17])
+    act("RC", T.RC[:], T.i16[:, 0:NI], ID, ["i16", "cG3"], ["RC"], bias=T.cG[:, 3:4])
     n4 = 256
     iota("j4", T.j4[:], [[0, n4 // 4], [1, 4]], 0, 0, ["j4"])
     ts("A4", T.A4[:], T.j4[:], r4, K4W, Alu.not_equal, Alu.mult, ["j4", "cF"], ["A4"])
@@ -186,7 +200,7 @@ def build(g, core, T, topo):
     iota("iP0", T.iP[:, 0:HI], [[4, HI]], -MID, 0, ["iP0"])
     iota("iP1", T.iP[:, HI:C], [[4, C - HI]], 4 * HI + GAP - MID, 0, ["iP1"])
     act("iO", T.iO[:], T.iP[:], ID, ["iP0", "iP1", "down"], ["iO"], scale=down)
-    LS, L32, LEND, LF = T.L[:, 0:1], T.L[:, 4:6], T.L[:, 8:10], T.L[:, 10:12]
+    LS, LEND, LFa, LFb = T.L[:, 0:1], T.L[:, 2:3], T.L[:, 4:5], T.L[:, 6:7]
     mset("Lf0", T.Lf[:], 0.0, ["Lf"])
     mset("kq0", T.kq[:], 1.0, ["kq"])
     mset("kq1", T.kq[:, 0:SW:192], 0.0, ["kq"])
@@ -211,36 +225,42 @@ def build(g, core, T, topo):
     for c, r in enumerate(CH):
         act("Lr%d" % c, T.Lf[:, 14 + 4 * c:15 + 4 * c], T.Lf[:, 12 + 4 * c:13 + 4 * c], ID, ["Lq", "qg%d" % c], ["Lr%d" % c],
             scale=-float(r), bias=T.qf[:, 4 + c:5 + c])
-    act("Lf4", T.Lf[:, 4:6], T.cF[:, 4:6], Act.Copy, ["cF", "Lf"], ["Lf4"])
-    act("cG4", T.cG[:, 4:6], T.cF[:, 4:6], Act.Square, ["cF"], ["cG4"], bias=1.5)
-    act("Lf8", T.Lf[:, 8:10], T.cG[:, 4:6], ID, ["cG4", "Lf"], ["Lf8"], scale=8.0, bias=-3.0)
-    ts("cG10", T.cG[:, 10:11], t4, 3.0, None, Alu.is_lt, None, ["cF"], ["cG10"])
-    ts("cG6", T.cG[:, 6:7], t4, 5.0, T.cG[:, 10:11], Alu.add, Alu.mult, ["cF", "cG10"], ["cG6"])
-    for c in range(2):
-        ts("cG8%d" % c, T.cG[:, 8 + c:9 + c], r4, 4.0 * c, gc_, Alu.add, Alu.is_equal, ["cF"], ["cG8%d" % c])
-    ts("Lf10", T.Lf[:, 10:12], T.cG[:, 8:10], T.cG[:, 6:7], None, Alu.mult, None, ["cG80", "cG81", "cG6", "Lf"], ["Lf10"])
-    cp("L", T.L[:], T.Lf[:], ["Ls", "Lf4", "Lf8", "Lf10", "Lq"] + ["Lr%d" % c for c in range(NC)], ["L"])
+    act("cG4", T.cG[:, 4:5], r4, Act.Square, ["cF"], ["cG4"], bias=1.5)
+    act("Le", T.Lf[:, 2:3], T.cG[:, 4:5], ID, ["cG4", "Lf"], ["Le"], scale=8.0, bias=-3.0)
+    ts("own", T.cG[:, 5:6], h2, gc_, None, Alu.is_equal, None, ["cF"], ["own"])
+    ts("La", T.Lf[:, 4:5], b2, 6.0, T.cG[:, 5:6], Alu.add, Alu.mult, ["cF", "own", "Lf"], ["La"])
+    act("b5", T.cG[:, 6:7], b2, ID, ["cF"], ["b5"], scale=2.0, bias=5.0)
+    act("Lb", T.Lf[:, 6:7], T.cG[:, 6:7], ID, ["b5", "own", "Lf"], ["Lb"], scale=T.cG[:, 5:6])
+    cp("L", T.L[:], T.Lf[:], ["Ls", "Le", "La", "Lb", "Lq"] + ["Lr%d" % c for c in range(NC)], ["L"])
     act("t640", T.cG[:, 7:8], t4, ID, ["cF"], ["t640"], bias=MID + 0.25)
     t640 = T.cG[:, 7:8]
     cp("kF", T.kF[0:1, :], T.kI[0:1, :], ["kI"], ["kF"])
     add("dk", "G", lambda: G.partition_broadcast(T.dk[:], T.kF[0:1, :], 128), ["kF"], ["dk"])
     for c in range(NC):
         act("D%d" % c, T.D16[:, 16 * c:16 * c + 16], T.dk[:].indirect(T.L[:, 12 + 4 * c:13 + 4 * c]), Act.Copy, ["dk", "L"], ["D%d" % c])
-    iota("ti", T.ti[:], [[1, 4], [0, 8]], 0, 0, ["ti"])
-    act("tq", T.tq[:], T.ti[:], Act.Copy, ["ti"], ["tq"], scale=0.25)
+    act("p256", T.cG[:, 8:9], rc, ID, ["cF"], ["p256"], bias=2.0 * M)
+    for c in range(4):
+        act("h4%d" % c, T.h4[:, c:c + 1], rc, ID, ["cF"], ["h4%d" % c], scale=4.0, bias=8.0 * M + c)
     mset("nb", T.nb[:], -BIG, ["nb"])
     mset("pre0", T.pre[:], BIG, ["pre"])
     mset("FT0", T.FT[:], 0.0, ["FT"])
     iota("Ri", T.Ri[:], [[0, 8], [1, 16], [0, 4]], 0, 0, ["Ri"])
     act("Rt0", T.Rt[:], T.Ri[:], Act.Abs, ["Ri", "neg"], ["Rt"], bias=nr)
-    act("Rt1", T.Rt[:], T.Rt[:], Act.Relu, ["Rt"], ["Rt"], bias=float(M), scale=-float(M))
-    quant("qR", T.QR[:], T.SR[:], T.Rt[:], ["Rt"], ["QR"])
+    act("Rt1", T.Rt[:], T.Rt[:], Act.Relu, ["Rt"], ["Rt"], bias=1.0, scale=-1.0)
+    act("w2", T.cG[:, 9:10], gc_, Act.Copy, ["cF"], ["w2"], scale=16.0)
+    act("w3", T.cG[:, 10:11], gc_, ID, ["cF"], ["w3"], scale=16.0, bias=-float(M))
+    for c, w in enumerate((float(M), -float(M), T.cG[:, 9:10], T.cG[:, 10:11])):
+        act("Ru%d" % c, T.Rt[:, c:512:4], T.Rt[:, c:512:4], ID, ["Rt", "w2", "w3"], ["Ru%d" % c], scale=w)
+    quant("qR", T.QR[:], T.SR[:], T.Rt[:], ["Rt"] + ["Ru%d" % c for c in range(4)], ["QR"])
+    act("p16", T.cG[:, 17:18], rc, ID, ["cF"], ["p16"], scale=16.0, bias=float(SPARE))
+    act("Dc", T.Dc[:, 0:8], T.i16[:, 0:8], ID, ["i16", "p16"], ["Dc"], scale=16.0, bias=T.cG[:, 17:18])
+    act("Dn", T.Dc[:, 8:16], T.Dc[:, 0:8], Act.Copy, ["Dc"], ["Dn"], scale=-1.0)
+    iota("A0", T.A[:], [[0, SEG[8]]], 0, 0, ["A"])
     for i in range(8):
-        iota("Ai%d" % i, T.Ai[:, SEG[i]:SEG[i + 1]], [[1, 16 * (i + 1)]], -16 * i, 0, ["Ai%d" % i])
-    act("A0", T.A[:], T.Ai[:], Act.Abs, ["Ai%d" % i for i in range(8)] + ["neg"], ["A"], bias=nr)
-    act("A1", T.A[:], T.A[:], Act.Relu, ["A"], ["A"], bias=4096.0, scale=-4096.0)
-    act("A2", T.A[:], T.A[:], ID, ["A"], ["A"], bias=1.0)
-    for i in range(1, 8):
+        act("Ad%d" % i, T.A[:, SEG[i + 1] - 16:SEG[i + 1]], T.ab[:], Act.Relu, ["A", "ab", "Dc", "Dn"], ["Ad%d" % i],
+            scale=T.Dc[:, 8 + i:9 + i], bias=T.Dc[:, i:i + 1])
+    act("A2", T.A[:], T.A[:], ID, ["A"] + ["Ad%d" % i for i in range(8)], ["A"], bias=1.0)
+    for i in (1, 2, 3, 5, 6, 7):
         iota("Az%d" % i, T.A[:, SEG[i]:SEG[i] + 1], [[0, 1]], 0, 0, ["A"])
     iota("Et0", T.Et[:], [[0, 2048]], 1, 0, ["Et"])
     add("Et1", "G", lambda: G.affine_select(T.Et[:], T.Et[:], [[-1, 4], [-16, 128], [1, 4]], Alu.is_equal, 0.0, 0, 16),
@@ -254,7 +274,6 @@ def build(g, core, T, topo):
 
     kX, kY = ["X0", "X1"], ["Y0", "Y1", "Y2", "Y3"]
     kG = ["Qg", "Sg"]
-    t1, rk, uu = T.tr[:, 0:NI], T.tr[:, NI:2 * NI], T.tr[:, 2 * NI:3 * NI]
 
     def quant_x():
         quant("qx1", T.QA[:, HI:C], T.SA[:, HI:C], T.Xt[:, 4 * HI + GAP:XE], ["X1"], ["QX1"])
@@ -265,6 +284,7 @@ def build(g, core, T, topo):
 
     def new_y(t, rb, db):
         q, s, k = T["QL%d" % t][:], T["SL%d" % t][:], "land%d" % t
+        add("land", "A", None, ["sentS%d" % t, "sentQ%d" % t], [k], "arr%d" % t, 2 * ne)
         for b in range(4):
             mm("mW%d" % b, ps(rb[b], 0, M), T.QW[:, M * b:M * b + M], T.SW[:, M * b:M * b + M], q, s, ["QW", "SW", k], ["B%d" % rb[b]])
             mm("mE%d" % b, ps(db[b], 0, M), T.QE[:, M * b:M * b + M], T.SE[:, M * b:M * b + M], q, s, ["QE%d" % b, k], ["B%d" % db[b]])
@@ -286,7 +306,7 @@ def build(g, core, T, topo):
         diag = T.CT[:, 0:4 * C:4]
         tt("dg", diag, T.W[:], ps(0, 0, C), Alu.is_ge, ["WH", "WL", "B0"], ["CTd"])
         scan("rd", T.rd[:], T.keep[:], diag, 0.0, Alu.mult, Alu.add, ["keep", "CTd"], ["rd"])
-        tt("t1", t1, T.rd[:, 15:C:16], T.RC[:], Alu.subtract, ["RC", "rd"], ["t1"])
+        tt("t1", T.tr[:], T.RC[:], T.rd[:, 15:C:16], Alu.subtract, ["RC", "rd"], ["t1"])
         for rows, width, first in TILES:
             for slot, i in enumerate(rows):
                 if i == "d":
@@ -296,17 +316,17 @@ def build(g, core, T, topo):
                 key, kw = "CT%d" % i, "WH" if w >= HI else "WL"
                 own = T.W[:, w + 15:w + 16]
                 if i > VR:
-                    sk = "sg%d" % (i % 2)
-                    act("a%d" % i, T[sk][:, 0:w], ps(1, 0, w), Act.Sign, ["B1", kw], [sk], bias=own, scale=-1.0)
-                    act("b%d" % i, out, T[sk][:, 0:w], Act.Relu, [sk], [key, "RS%d" % i], accum_out=T.RS[:, i:i + 1])
+                    sk, sg = "sg%d" % i, T.sg[:, C * (i - VR - 1):C * (i - VR - 1) + w]
+                    act("a%d" % i, sg, ps(1, 0, w), Act.Sign, ["B1", kw], [sk], bias=own, scale=-1.0)
+                    act("b%d" % i, out, sg, Act.Relu, [sk], [key, "RS%d" % i], accum_out=T.RS[:, i:i + 1])
                 else:
                     ts("c%d" % i, out, ps(0, 0, w), own, None, Alu.is_lt, None, ["B0", kw], [key])
         for c in range(4):
-            scan("s%d" % c, T.rs[:, SW * c:SW * c + SW], T.kq[:], T.CT[:, 4 * 576 + c:4 * 960:4], 0.0, Alu.mult, Alu.add,
+            scan("s%d" % c, T.rs[:, SW * c:SW * c + SW], T.kq[:], T.CT[:, 4 * 576 + c:4 * 960:4], 0.0, Alu.mult, Alu.subtract,
                  ["kq"] + ["CT%d" % (c + 1 + 4 * a) for a in range(3)], ["rs%d" % c])
-        tt("ua", T.tr[:, 2 * NI:2 * NI + 16], T.rs[:].indirect(LS), T.tr[:, 0:16], Alu.add,
+        tt("ua", T.D1[:, 15:256:16], T.rs[:].indirect(LS), T.tr[:, 0:16], Alu.add,
            ["t1", "L", "rsz"] + ["rs%d" % c for c in range(4)], ["uu"])
-        tt("ub", T.tr[:, 2 * NI + VR + 1:3 * NI], T.tr[:, VR + 1:NI], T.RS[:, VR + 1:NI], Alu.add,
+        tt("ub", T.D1[:, 16 * VR + 31:C:16], T.tr[:, VR + 1:NI], T.RS[:, VR + 1:NI], Alu.subtract,
            ["t1"] + ["RS%d" % i for i in range(VR + 1, NI)], ["uu"])
         for u in range(3):
             rows, width, first = TILES[u]
@@ -324,21 +344,20 @@ def build(g, core, T, topo):
         mm("mS", ps(3, 0, M), T.Qg[:], T.Sg[:], T.QA[:, C:C + M], T.SA[:, C:C + M], kG + ["QY"], ["B3"])
         tt("d3", T.d3[:], ps(3, 0, M), T.Mk[:, 0:M], Alu.min, ["B3", "Mk"], ["d3"])
         scan("Wm", T.Wm[:], T.K16[:, 0:M], T.d3[:], -BIG, Alu.min, Alu.max, ["K16", "d3"], ["Wm"])
-        scan("W2", T.W2[:], T.A16[:], ps(2, 0, C), 0.0, Alu.mult, Alu.add, ["A16", "B2"], ["W2"])
-        tt("rk", rk, T.W2[:, 15:C:16], uu, Alu.subtract, ["W2", "uu"], ["rk"])
-        ts("roff", T.roff[:], rk, 0.25, None, Alu.add, None, ["rk"], ["roff"])
+        scan("W2", T.W2[:], ps(2, 0, C), T.D1[:], HOLD, Alu.min, Alu.add, ["uu", "B2"], ["W2"])
+        ts("roff", T.roff[:], T.W2[:, 15:C:16], T.cG[:, 15:16], None, Alu.add, None, ["W2", "z2"], ["roff"])
         cp("o2a", T.o2[:, 0:C].indirect(T.roff[:]), T.iO[:], ["roff", "iO"], ["o2a"])
         cp("o2b", T.o2[:, C:2 * C], T.o2[:, 0:C], ["o2a"], ["o2b"])
         for i in range(8):
             own = T.Wm[:, 16 * i + 15:16 * i + 16]
+            sk, sg = "sm%d" % i, T.sm[:, C * i:C * i + C]
             if i in PAR["vmsg"]:
-                ts("f%d" % i, T.vg[:], ps(0, 0, C), own, None, Alu.is_gt, None, ["B0", "Wm"], ["vg"])
-                scan("g%d" % i, T.vb[:, C * i:C * i + C], T.vg[:], T.big[:], -128.0, Alu.add, Alu.min, ["vg", "big"], ["vb%d" % i])
+                ts("f%d" % i, sg, ps(0, 0, C), own, None, Alu.is_gt, None, ["B0", "Wm"], [sk])
+                scan("g%d" % i, T.vb[:, C * i:C * i + C], sg, T.big[:], -128.0, Alu.add, Alu.min, [sk, "big"], ["vb%d" % i])
                 ts("n%d" % i, T.n[:, i:i + 1], T.vb[:, C * i + C - 1:C * i + C], 128.0, None, Alu.add, None, ["vb%d" % i], ["n%d" % i])
             else:
-                sk = "sg%d" % (i % 2)
-                act("f%d" % i, T[sk][:], ps(1, 0, C), Act.Sign, ["B1", "Wm"], [sk], bias=own, scale=-1.0)
-                act("n%d" % i, T[sk][:], T[sk][:], Act.Relu, [sk], ["n%d" % i, sk], scale=-1.0, accum_out=T.n[:, i:i + 1])
+                act("f%d" % i, sg, ps(1, 0, C), Act.Sign, ["B1", "Wm"], [sk], bias=own, scale=-1.0)
+                act("n%d" % i, sg, sg, Act.Relu, [sk], ["n%d" % i, sk], scale=-1.0, accum_out=T.n[:, i:i + 1])
         for h, r in enumerate(CH):
             i0, n = sum(CH[:h]), 64 * r
             z0, pos, pk = 16 * i0, T.pos[:, 16 * h:16 * h + 16], "pof%d" % h
@@ -350,12 +369,13 @@ def build(g, core, T, topo):
                 cp("er%d" % h, er, T.o2[:].indirect(pof), ["o2a", "o2b", pk], ["er%d" % h])
             else:
                 act("er%d" % h, er, T.o2[:].indirect(pof), Act.Copy, ["o2a", "o2b", pk], ["er%d" % h])
-            scan("e4%d" % h, T.e4[:, 0:n], T.A4[:, 0:n], er, 0.0, Alu.mult, Alu.add, ["A4", "er%d" % h], ["e4"])
-            ts("zof%d" % h, T.zof[:, z0:z0 + n // 4], T.e4[:, 3:n:4], t640, None, Alu.add, None, ["e4", "t640"], ["zof%d" % h])
+            scan("e4%d" % h, T.e4[:, 4 * z0:4 * z0 + n], T.A4[:, 0:n], er, 0.0, Alu.mult, Alu.add, ["A4", "er%d" % h], ["e4%d" % h])
+            ts("zof%d" % h, T.zof[:, z0:z0 + n // 4], T.e4[:, 4 * z0 + 3:4 * z0 + n:4], t640, None, Alu.add, None,
+               ["e4%d" % h, "t640"], ["zof%d" % h])
             for k in range(F):
                 a, b = 512 * k + 64 * i0, 64 * i0 + 16 * r * k
-                tt("Z%d%d" % (k, h), T.Z[:, a:a + n], T.Xh[:].indirect(T.zof[:, z0 + 4 * r * k:z0 + 4 * r * (k + 1)]), T.Yh[:, 64 * i0:64 * i0 + n],
-                   Alu.add, ["Xh", "Yh", "zof%d" % h], ["Z%d%d" % (k, h)])
+                tt("Z%d%d" % (k, h), T.Z[:, a:a + n], T.Xh[:].indirect(T.zof[:, z0 + 4 * r * k:z0 + 4 * r * (k + 1)]),
+                   T.Yh[:, 64 * i0:64 * i0 + n], Alu.add, ["Xh", "Yh", "zof%d" % h], ["Z%d%d" % (k, h)])
                 act("ec%d%d" % (k, h), T.erep[:, M * k + 16 * i0:M * k + 16 * (i0 + r)], T.er[:, b:b + 16 * r], ID,
                     ["er%d" % h, "up"], ["ec%d%d" % (k, h)], scale=up)
         for k in range(F):
@@ -367,11 +387,13 @@ def build(g, core, T, topo):
         kZ = ["Z%d%d" % (k, h) for k in range(F) for h in range(NC)]
         kE = ["ec%d%d" % (k, h) for k in range(F) for h in range(NC)]
         scan("pre", T.pre[:, 5:9], T.ps[:, 2049:4096:512], T.nb[:], -BIG, Alu.max, Alu.max, ["B4", "B5", "B6", "B7", "nb"], ["pre"])
-        ts("FT", T.FT[:, 0:32], T.pre[:, 0:8].indirect(LF), T.pre[:, 8:9], None, Alu.is_lt, None, ["pre", "L"], ["FT"])
-        quant("qF", T.QF[:], T.SF[:], T.FT[:], ["FT"], ["QF"])
+        ts("Fa", T.FT[:, 0:32:2], T.pre[:, 0:8].indirect(LFa), T.pre[:, 8:9], None, Alu.is_lt, None, ["pre", "L", "FT"], ["Fa"])
+        ts("Fb", T.FT[:, 1:32:2], T.pre[:, 0:8].indirect(LFb), T.pre[:, 8:9], None, Alu.is_equal, None, ["pre", "L", "FT"], ["Fb"])
+        quant("qF", T.QF[:], T.SF[:], T.FT[:], ["Fa", "Fb"], ["QF"])
         mm("mF", ps(3, 0, M), T.QR[:], T.SR[:], T.QF[:], T.SF[:], ["QR", "QF"], ["B3"])
-        tt("zi", T.zi[:], ps(3, 0, 8), T.jc[:], Alu.add, ["B3", "jc"], ["zi"])
-        cp("ziu", T.ziu[:], T.zi[:], ["zi"], ["ziu"])
+        ts("ziu", T.ziu[:], ps(3, 0, 8), T.cG[:, 8:9], None, Alu.add, None, ["B3", "p256"], ["ziu"])
+        for c in range(4):
+            ts("hof%d" % c, T.hof[:, c:32:4], ps(3, 0, 8), 4.0, T.h4[:, c:c + 1], Alu.mult, Alu.add, ["B3", "h4%d" % c], ["hof%d" % c])
         cp("QH", QH[:].bitcast(dt.uint32), QZ[:].bitcast(dt.uint32).indirect(T.ziu[:]), kQZ + ["ziu"], ["QH%d" % t])
         act("SH", SH[:], SZ[:].indirect(T.ziu[:]), Act.Copy, kQZ + ["ziu"], ["SH%d" % t])
         arr = T.sem["arr%d" % t]
@@ -379,35 +401,39 @@ def build(g, core, T, topo):
             ["SH%d" % t], ["sentS%d" % t], "remote")
         add("sendQ", "G", lambda a=T["QL%d" % t][:].bitcast(dt.uint8), b=QH[:].bitcast(dt.uint8), s=arr:
             G.remote_dma(a, b, s, T.sem.sent, pid, rid, mask), ["QH%d" % t], ["sentQ%d" % t], "remote")
-        add("land", "A", None, ["sentS%d" % t, "sentQ%d" % t], ["land%d" % t], "arr%d" % t, 2 * ne, late=1)
-        act("okc", T.a2[:, 0:32], T.FT[:, 0:32], Act.Copy, ["FT"], ["okc%d" % t, "a2"], accum_out=T.okc[:, t:t + 1])
+        act("oka", T.jk[:, 0:16], T.FT[:, 0:32:2], Act.Copy, ["Fa"], ["oka"], accum_out=T.okc[:, 4:5])
+        act("okb", T.jk[:, 16:24], T.FT[:, 1:32:4], ID, ["Fb"], ["okb"], scale=-1.0, bias=0.125, accum_out=T.okc[:, 5:6])
+        act("okc", T.okc[:, t:t + 1], T.okc[:, 4:5], ID, ["oka", "okb"], ["okc%d" % t], bias=T.okc[:, 5:6])
         dma("ok", "Y", T.ok[t], T.okc[:, t:t + 1], ["okc%d" % t], [], "outh")
         act("ew", T.ew[:], T.erep[:].indirect(T.ziu[:]), ID, kE + ["ziu", "dn16"], ["ew"], scale=T.cG[:, 12:13])
-        tt("hf", T.hf[:], T.zi[:].indirect(L32), T.tq[:], Alu.add, ["zi", "tq", "L"], ["hf"])
-        ts("hof", T.hof[:], T.hf[:], 4.0, None, Alu.mult, None, ["hf"], ["hof"])
-        act("Hp", T.Hp[:], T.Z[:].indirect(T.hof[:]), Act.Copy, kZ + ["hof"], ["Hp"])
         scan("ews", T.ews[:], T.A16[:, 0:M], T.ew[:], 0.0, Alu.mult, Alu.add, ["A16", "ew"], ["ews"])
-        for i in range(8):
-            w = 16 * (i + 1)
-            ts("EQ%d" % i, T.EQ[:, SEG[i]:SEG[i + 1]], T.ew[:, 0:w], up16, T.ews[:, w - 1:w], Alu.mult, Alu.is_equal,
-               ["ew", "ews", "wb"], ["EQ%d" % i])
-        for c in range(4):
-            act("e1%d" % c, T.e[:, 8 * c:8 * c + 8], T.ews[:, 15:M:16], ID, ["ews"], ["e1%d" % c], bias=float(MID - 1 + c))
-        scan("st", T.st[:], T.A[:], T.EQ[:], 0.0, Alu.mult, Alu.max, ["A"] + ["EQ%d" % i for i in range(8)], ["st"])
-        tt("e2", T.e[:, 32:64], T.st[:].indirect(LEND), T.e[:, 0:32], Alu.add, ["st", "L"] + ["e1%d" % c for c in range(4)], ["e2"])
-        tt("e3", T.e[:, 64:96], T.e[:, 32:64], T.dum[:], Alu.min, ["e2", "dum"], ["e3"])
-        cp("xof", T.xof[:], T.e[:, 64:96], ["e3"], ["xof"])
-        cp("X", T.Xt[:].indirect(T.xof[:]), T.Hp[:], ["xof", "Hp", "gap"] + kX, kX)
+        for h in (1, 0):
+            act("Hp%d" % h, T.Hp[:, 256 * h:256 * h + 256], T.Z[:].indirect(T.hof[:, 16 * h:16 * h + 16]), Act.Copy,
+                kZ + ["hof%d" % c for c in range(4)], ["Hp%d" % h])
+            for i in range(4 * h, 4 * h + 4):
+                ts("EQ%d" % i, T.EQ[:, SEG[i]:SEG[i + 1]], T.ew[:, 64 * h:16 * i + 16], up16, T.ews[:, 16 * i + 15:16 * i + 16],
+                   Alu.mult, Alu.is_equal, ["ew", "ews", "wb"], ["EQ%d" % i])
+            a, e1, e2 = 160 * h, T.e[:, 32 * h:32 * h + 16], T.e[:, 32 * h + 16:32 * h + 32]
+            act("e1%d" % h, e1, T.ews[:, 64 * h + 3:64 * h + 64:4], ID, ["ews"], ["e1%d" % h], bias=MID + 4.0)
+            scan("st%d" % h, T.st[:, a:a + 160], T.A[:, a:a + 160], T.EQ[:, a:a + 160], 0.0, Alu.mult, Alu.max,
+                 ["A"] + ["EQ%d" % i for i in range(4 * h, 4 * h + 4)], ["st%d" % h])
+            tt("e2%d" % h, e2, T.st[:, a:a + 160].indirect(LEND), e1, Alu.max, ["st%d" % h, "L", "e1%d" % h], ["e2%d" % h])
+            for c in range(4):
+                ts("xo%d%d" % (c, h), T.xof[:, 16 * h + c:16 * h + 16:4], T.e[:, 32 * h + 19:32 * h + 32:4], c - 4.0, None, Alu.add, None,
+                   ["e2%d" % h], ["xo%d%d" % (c, h)])
+            cp("X" if h == 0 else "XA", T.Xt[:].indirect(T.xof[:, 16 * h:16 * h + 16]), T.Hp[:, 256 * h:256 * h + 256],
+               ["xo%d%d" % (c, h) for c in range(4)] + ["Hp%d" % h, "gap"], kX)
 
-    at[0] = R
+    at[1] = "!"
     new_y(R - 1, [4, 5, 6, 7], [0, 1, 2, 3])
     quant_y()
     quant_x()
-    for key, a, z, b, k in (("y", C, C + M, 4, ["QY"]), ("x", 0, C, 5, ["QX0", "QX1"])):
-        mm("mv" + key, ps(b, 0, z - a), T.Qv[:], T.Sv[:], T.QA[:, a:z], T.SA[:, a:z], ["Qv"] + k, ["B%d" % b])
-        dma("oc" + key, "Y", T.oc[:, 4 * a:4 * z], T.QA[:, a:z].bitcast(dt.uint8), k, [], "outh")
+    for key, a, z, b in (("Y", C, C + M, 4), ("X1", HI, C, 5), ("X0", 0, HI, 6)):
+        mm("mv" + key, ps(b, 0, z - a), T.Qv[:], T.Sv[:], T.QA[:, a:z], T.SA[:, a:z], ["Qv", "Q" + key], ["B%d" % b])
         act("ys" + key, T.ysb[:, a:z], ps(b, 0, z - a), Act.Copy, ["B%d" % b], ["ysb" + key])
         dma("oy" + key, "S", T.y[:, a:z], T.ysb[:, a:z], ["ysb" + key], [], "outh")
+    for key, a, z, k in (("Y", C, C + M, ["QY"]), ("X", 0, C, ["QX0", "QX1"])):
+        dma("oc" + key, "Y", T.oc[:, 4 * a:4 * z], T.QA[:, a:z].bitcast(dt.uint8), k, [], "outh")
     for k in range(4):
         dma("os%d" % k, "G" if k == 3 else "Y", T.osc[4 * k:4 * k + 4, :], T.SA[32 * k:32 * k + 4, :], ["QX0", "QX1", "QY"], [],
             "outg" if k == 3 else "outh")

@@ -4,13 +4,14 @@ C, M, F, R = 320, 128, 4, 3
 NI = C // 16
 BIG = 2.0 ** 96
 K16W, K4W = 2.0 ** 30, 2.0 ** 13
-SEG = [160 * (i // 4) + 8 * (i % 4) * (i % 4 + 1) for i in range(9)]
+SEG = [8 * q * (q + 1) + 4 * q for q in range(5)]
 HI = 192
 GAP = 8
 XE = 4 * C + GAP
 MID = 4 * HI + 4
 HOLD = 1024.0
-SPARE = XE + 24
+SPARE = 1552
+LIFT = 8192.0
 SW = 384
 VR = 12
 
@@ -20,17 +21,18 @@ PAR = {
     "vmsg": (0, 4),
     "chunks": (4, 4),
     "eg": "VS",
+    "cut": 1,
     "pe": (0, 3, 4, 2, 1),
 }
 
 Q4, U8, BF, F32, I32, U16 = "float8_e4m3fn_x4", "uint8", "bfloat16", "float32", "int32", "uint16"
 SCRATCH = {"ps": ("psum", [128, 4096], F32)}
 for _d, _l in (
-        (BF, "Xt:3344 Xh:1288 Yt:512 Yh:512 Z:2048 ut:512 vt:512 CT:4096 FT:512 Et:2048 Gi:512 Gt:512 Ri:512 Rt:512 j16:320 Mk:320 "
-             "K16:320 keep:320 A16:128 a1:128 a2:128 mM:320 ab:16 big:320 j4:256 A4:256 w4:16 A:320 iO:320 iP:320 sg:2240 sm:2560 "
-             "vb:2560 rs:1538 kq:384 rd:320 o2:640 er:512 e4:512 jk:32 erep:512 Hp:512 ew:128 ews:128 EQ:320 st:320"),
-        (F32, "cF:8 cG:24 Lf:24 i16:32 RC:20 D1:320 Dc:16 h4:4 nb:4 kF:16 dk:16 D16:48 qf:16 d1:320 W:320 s4:16 "
-              "W2:320 d3:128 Wm:128 RS:20 tr:20 n:8 pos:48 pre:16 okc:8 e:64 Rr:512 ysb:448"),
+        (BF, "Xt:3344 Xh:1288 Yt:512 Yh:512 Z:2048 ut:512 vt:512 CT:4096 FT:512 Et:2048 Zt:512 Gi:512 Gt:512 Ri:512 Rt:512 j16:320 "
+             "Mk:320 K16:320 keep:320 A16:128 a1:128 a2:128 cB:8 ab:16 j4:256 A4:256 w4:16 A:176 Dc:8 EW:512 OW:32 iO:320 iP:320 "
+             "sg:2240 sm:2560 vb:2560 rs:1538 kq:384 rd:320 o2:640 er:512 e4:512 jk:32 erep:512 Hp:512 ew:128 EQ:352"),
+        (F32, "cF:8 cG:24 Lf:24 i16:32 RC:20 D1:320 st:352 HD:32 HG:32 h4:4 nb:4 kF:16 dk:16 D16:48 qf:16 d1:320 W:320 s4:16 "
+              "W2:320 d3:128 Wm:128 RS:20 tr:20 n:8 pos:48 pre:16 okc:8 Rr:512 ysb:448"),
         (I32, "pI:16 cI:8 kI:16 qI:8"),
         (U16, "uL:8 L:24 roff:20 pof:48 zof:128 ziu:8 hof:32 xof:32")):
     for _e in _l.split():
@@ -44,38 +46,39 @@ SEMAPHORES = ["cV", "cS", "cP", "cG", "lu", "lx0", "lx1", "lm", "lv", "lwc", "lw
               "arr0", "arr1", "arr2"]
 
 FIRST = {
-    "V": "kq0 CT3 CT0 cI5 cI0 cI4 cI2 cI1 cI3 pm CT2 cF pmb kq1 dn16 pma CT1 pmf kq2 rs0 z1 z0 CT4 big uL qpad Lf0 Mk0 gap qu qI "
-         "Mk own qx1 Qg qy qx0 sz Lq dH FT0 WH wb w4b dL D1 WL c12 c6 c1 dg c2 d3 c8 qG c4 c10 c9 A4 w4a kF c3 Ls Wm s3 c5 qv c7 "
-         "c11 rd q0 t1 s1 La s0 s2 q3 down q2 L q1 ua f4 ub f0 W2 nb g0 roff a2 n0 o2a pos0 g4 o2b pof0 n4 er0 pos1 e40 pof1 up "
-         "zof0 Z20 Z30 e41 Z00 zof1 Z10 Z11 Z01 Z21 Z31 qz2 qz0 qz1 qz3 pre0 qR A16 pre Fa Fb qE0 qF ziu hof2 hof3 hof0 up16 QH "
-         "hof1 ews EQ7 EQ4 EQ6 EQ5 EQ1 EQ3 EQ2 EQ0 st1 st0 e21 qE3 e20 xo21 xo31 xo11 xo01 xo00 xo10 xo20 xo30 XA qE2 X qE1",
-    "S": "lm lx1 qg0 neg t640 qg1 qf0 cG4 b5 qf1 keep cG2 rc1 sq a0 z3 z2 se K16 Yh Sg Gt0 Lb mM sp Gt1 a19 cG3 a15 a18 a13 a14 "
-         "Le b18 a17 b19 RC b17 Lr0 Lr1 a16 f2 b13 b14 b16 f5 b15 f1 f3 f7 n2 iO D0 n1 n3 f6 n7 n6 D1 n5 Xh h41 p16 er1 h43 ec00 "
-         "h40 ec10 Dc ec20 Dn w2 ab Ad5 w3 Rt0 ec30 a1 Rt1 Ad0 Ad1 ec11 Ad4 Ru1 Ru3 Ad6 Ru2 ec01 h42 Ru0 ec31 Ad7 Ad2 Ad3 p256 "
-         "ec21 A2 oka ew okb SH e11 Hp0 e10 Hp1 okc",
-    "P": "mH m0 mS m1 mC0 mC3 mC4 mC2 mC1 mZ2 mZ0 mZ1 mZ3 mF",
-    "G": "pI j16 uI Gi j4 A0 kI i16 Ri iP1 iP0 dk Et0 Et1 Az1 Az2 Az3 Az5 Az6 Az7 sendQ sendS",
-    "Y": "lu lx0 lv lwc lws ok"}
+    "V": "CT4 CT2 cI5 cI4 cI2 cI0 cI3 cI1 pm Lf0 cF pmb pma CT0 own z0 rs0 cB nb CT1 pmf K16 gap pre0 keep uL qI dn16 La wb Mk "
+         "qu CT3 qx1 Qg up16 qx0 sz Gt Lq Ls dH qpad WH dL c12 WL qG A4 c10 w4a c11 c7 c9 c8 c6 qy w4b dg c5 L c1 kq1 d3 c3 kq2 "
+         "c2 c4 down rd s0 s2 Wm q0 kF s3 s1 q3 q2 t1 q1 ua f0 ub f4 W2 g0 roff g4 n0 o2a pos0 n4 o2b pof0 up a2 er0b er0a e40b "
+         "e40a pos1 zof0b zof0a pof1 Z10 Z20 e41 Z30 zof1 Z00 Z01 Z11 Z21 Z31 qz0 qz2 qz1 qz3 A16 qR pre EW0 EW1 Fa Fb qv H1 qF "
+         "EW2 EW3 qE3 H0 H2 H3 ziu G2 G1 G3 QH OW hof1 hof0 hof2 hof3 EQ5 EQ7 EQ6 EQ4 EQ3 EQ0 EQ2 EQ1 st1 st0 xo1 qE2 xo0 XA qE0 "
+         "X qE1",
+    "S": "lx1 z1 t85 neg t640 qf1 b5 qf0 cG2 qg1 cG4 z3 a0 qg0 sq dp Le Lb rc1 ab se cG3 D1 h40 sp Sg Xh Lr1 z2 a18 a19 Lr0 a16 "
+         "a17 b19 b17 RC a14 b18 a13 a15 b13 b14 b16 f3 b15 f6 f1 dk0 f2 n1 iO n3 f5 n2 f7 n6 n7 n5 dk1 Yh h41 ud p256 h42 er1 "
+         "w2 Rt0 ec30 Ad3 Rt1 w3 Az3 As3 As1 Ad2 At1 At0 ec00 At3 ec20 Ru3 p16 Ru0 ec11 As2 a1 Az2 At2 Ru1 h43 ec31 Dc As0 Ru2 "
+         "ec21 Az1 ec01 ec10 okb Ad1 oka Ad0 ew SH sl6 sl4 sl7 sl5 sl3 sl0 sl1 sl2 Hp1 okc Hp0",
+    "P": "mH m1 m0 mS mC0 mC3 mC4 mC2 mC1 mZ0 mZ2 mZ1 mZ3 mF",
+    "G": "pI j16 uI Gi iP1 j4 i16 kq0 kI A0 dk iP0 Zt Eq Et1 Ri Et3 FT0 Et2 HG Et0 sendQ sendS",
+    "Y": "lu lx0 lm lwc lv lws ok"}
 STEADY = {
-    "V": "qx1 qx0 dH WH dL c12 WL c1 c10 c4 dg c8 c2 rd c6 c9 c7 c3 Y1 Y0 s3 t1 c5 Y3 Y2 q3 qy c11 s1 s0 d3 s2 Wm q0 ua q2 q1 ub "
-         "f0 f4 W2 g0 roff n0 o2a pos0 o2b pof0 g4 er0 n4 e40 pos1 zof0 pof1 Z20 Z10 e41 Z00 zof1 Z30 Z21 Z01 Z31 Z11 qz3 qz2 "
-         "qz0 qz1 pre Fb Fa qF ziu hof1 QH hof3 ews hof2 hof0 EQ7 EQ4 EQ6 EQ5 EQ0 EQ1 EQ3 EQ2 st1 st0 e21 e20 xo01 xo31 xo11 "
-         "xo21 xo10 xo00 xo20 xo30 XA X",
-    "S": "Xh a14 a17 a18 b17 a15 a19 Rr1 Rr0 b14 Rr3 Rr2 b18 a16 b15 b19 a13 b16 b13 f7 f1 f3 f2 n1 f5 n2 n3 f6 n5 n7 n6 Yh er1 "
-         "ec31 ec10 ec21 ec01 ec11 ec30 oka okb ec00 ec20 ew e11 e10 SH Hp1 okc Hp0",
-    "P": "mH m0 m1 mW1 mW0 mE0 mE1 mW3 mW2 mE3 mE2 mS mC0 mC3 mC4 mC2 mC1 mZ3 mZ2 mZ0 mZ1 mF",
+    "V": "qx1 qx0 dH WH dL WL c12 c4 c8 c5 c9 dg s3 c1 c6 Y1 c7 Y0 c3 c2 s0 c11 Y2 Y3 s2 qy q3 c10 rd d3 s1 t1 Wm q2 q0 ua q1 f0 "
+         "ub f4 W2 g0 roff g4 n0 o2a n4 pos0 o2b pof0 er0a er0b e40a pos1 e40b zof0a pof1 zof0b Z00 Z10 e41 Z20 zof1 Z30 Z01 Z21 "
+         "Z31 Z11 qz2 qz3 qz0 qz1 EW0 EW3 EW1 pre H0 Fb Fa H1 qF EW2 H3 H2 ziu G1 G3 G2 hof1 hof3 hof2 OW QH hof0 EQ4 EQ5 EQ7 "
+         "EQ6 EQ2 EQ0 EQ3 EQ1 st1 st0 xo1 xo0 XA X",
+    "S": "Xh a18 a19 a14 a13 a16 Rr1 Rr0 b18 a17 Rr2 Rr3 a15 b19 b15 b16 b13 b17 b14 f3 f1 f2 n1 f6 n3 n2 n6 f5 f7 n5 n7 Yh er1 "
+         "ec30 ec00 ec31 ec21 ec01 ec20 ec10 ec11 oka okb ew SH sl4 sl6 sl5 sl7 sl1 sl0 sl3 sl2 Hp1 Hp0 okc",
+    "P": "mH m0 m1 mW1 mW0 mE0 mE1 mW3 mW2 mE2 mE3 mS mC0 mC3 mC4 mC2 mC1 mZ2 mZ3 mZ0 mZ1 mF",
     "G": "sendQ sendS", "Y": "ok", "A": "land"}
 LAST = {
-    "V": "qx1 qx0 dH dL WH WL c12 Y1 c6 c4 c2 dg Y0 c3 c1 c11 c10 c7 rd Y2 c5 t1 Y3 c9 c8 qy s0 s3 s1 d3 s2 q2 Wm q0 ua q3 q1 ub "
-         "f4 f0 W2 g0 roff n0 o2a pos0 o2b pof0 g4 er0 n4 e40 pos1 zof0 pof1 Z20 Z00 e41 Z10 zof1 Z30 Z21 Z11 qz2 Z31 Z01 qz3 "
-         "qz1 qz0 pre Fa Fb qF ziu QH hof1 hof2 ews hof3 EQ7 EQ6 EQ2 EQ4 EQ5 EQ0 EQ1 EQ3 st1 hof0 st0 e21 e20 xo21 xo11 xo31 "
-         "xo30 xo01 xo10 xo00 xo20 XA X qx0! Y0! Y1! Y3! Y2! qx1! qy!",
-    "S": "Xh Rr1 Rr0 a14 a16 Rr2 a18 a13 a17 b13 Rr3 a15 a19 b18 b19 b14 b17 b16 b15 f1 f3 n1 f2 f6 f5 n3 n2 f7 n6 n7 n5 Yh ec00 "
-         "er1 ec21 ec20 ec30 ec10 ec01 ec11 ec31 okb ew SH e11 oka e10 Hp1 Hp0 okc Rr0! Rr1! Rr3! Rr2! ysX0! oyX0! ysX1! ysY! "
-         "oyX1! oyY!",
-    "P": "mH m0 m1 mW1 mW0 mE1 mE0 mW2 mE2 mW3 mE3 mS mC0 mC3 mC4 mC2 mC1 mZ2 mZ3 mZ1 mZ0 mF mW0! mW1! mE0! mW3! mW2! mE1! mE3! "
-         "mE2! mvX0! mvX1! mvY!",
-    "G": "sendQ sendS os3!", "Y": "ok ocX! os2! ocY! os1! os0!", "A": "land land!"}
+    "V": "qx1 qx0 dH WH dL c12 WL c1 dg c4 c3 c8 c11 c7 Y1 c10 Y0 c2 c9 rd Y3 Y2 c6 c5 t1 qy q2 s3 s0 d3 s1 q3 Wm q0 s2 q1 ua f0 "
+         "ub f4 W2 g0 roff g4 n0 o2a n4 pos0 o2b pof0 er0a er0b e40a pos1 e40b zof0a pof1 zof0b Z00 Z10 e41 Z20 zof1 Z30 Z01 Z31 "
+         "Z21 Z11 qz2 qz0 qz3 qz1 EW2 EW1 EW0 EW3 pre H3 Fb Fa qF H0 H2 H1 ziu G2 G3 G1 QH OW hof1 hof3 hof2 EQ6 EQ7 hof0 EQ4 "
+         "EQ5 EQ0 EQ2 EQ1 EQ3 st1 st0 xo1 xo0 XA X qx0! Y1! Y0! Y2! Y3! qx1! qy!",
+    "S": "Xh a17 a16 a13 b17 Rr1 Rr0 a15 a18 Rr3 Rr2 a14 b13 b18 a19 b15 b19 b14 b16 f1 f3 f7 f2 f6 n3 n1 n2 n6 f5 n7 n5 Yh ec30 "
+         "er1 ec20 ec31 ec21 ec01 ec10 ec11 ec00 ew SH sl6 sl4 sl7 sl0 sl5 sl1 sl3 sl2 Hp1 Hp0 okb oka okc Rr1! Rr0! Rr2! Rr3! "
+         "ysX0! oyX0! ysX1! ysY! oyX1! oyY!",
+    "P": "mH m0 m1 mW1 mE0 mW0 mE1 mW3 mW2 mE3 mE2 mS mC0 mC3 mC4 mC2 mC1 mZ2 mZ0 mZ3 mZ1 mF mW1! mW0! mW2! mE1! mW3! mE0! mE2! "
+         "mE3! mvX0! mvX1! mvY!",
+    "G": "sendQ sendS os3!", "Y": "ok ocX! os0! ocY! os2! os1!", "A": "land land!"}
 ORDER = [FIRST, STEADY, LAST]
 
 
@@ -138,7 +141,7 @@ def build(g, core, T, topo):
     dma("lu", "Y", T.ut[:], T.u[:], [], ["ut"], "lu")
     dma("lx1", "S", T.Xt[:, 4 * HI + GAP:XE], T.x[:, 4 * HI:4 * C], [], ["X1"], "lx1")
     dma("lx0", "Y", T.Xt[:, 0:4 * HI], T.x[:, 0:4 * HI], [], ["X0"], "lx0")
-    dma("lm", "S", T.Yt[:], T.m[:], [], ["Y0", "Y1", "Y2", "Y3"], "lm")
+    dma("lm", "Y", T.Yt[:], T.m[:], ["ut"], ["Y0", "Y1", "Y2", "Y3"], "lm")
     quant("qu", T.Qu[:], T.Su[:], T.ut[:], ["ut"], ["Qu"])
     dma("lwc", "Y", T.QW[:].bitcast(dt.uint8), T.wc[:], ["Qu"], ["QW"], "lwc")
     dma("lws", "Y", T.SW[:], T.ws[:], ["Qu"], ["SW"], "lws")
@@ -151,39 +154,37 @@ def build(g, core, T, topo):
         ts("cI%d" % a, T.cI[:, a:a + 1], T.pI[:, a:a + 1], sh, an, Alu.logical_shift_right, Alu.bitwise_and, ["pI"], ["cI%d" % a])
     cp("cF", T.cF[:, 0:6], T.cI[:, 0:6], ["cI%d" % c for c in range(6)], ["cF"])
     rc, gc_, r4, t4, h2, b2 = [T.cF[:, c:c + 1] for c in range(6)]
-    act("neg", T.cG[:, 0:2], T.cF[:, 0:2], Act.Copy, ["cF"], ["neg"], scale=-1.0)
-    nr, ng = T.cG[:, 0:1], T.cG[:, 1:2]
+    cp("cB", T.cB[:, 0:6], T.cI[:, 0:6], ["cI%d" % c for c in range(6)], ["cB"])
+    rb, gb, r4b = [T.cB[:, c:c + 1] for c in range(3)]
+    act("neg", T.cG[:, 0:1], rc, Act.Copy, ["cF"], ["neg"], scale=-1.0)
+    nr = T.cG[:, 0:1]
     iota("j16", T.j16[:], [[0, NI], [1, 16]], 0, 0, ["j16"])
-    ts("Mk0", T.Mk[:], T.j16[:], rc, 0.5, Alu.is_equal, Alu.subtract, ["j16", "cF"], ["Mk"])
-    ts("Mk", T.Mk[:], T.Mk[:], 2 * BIG, None, Alu.mult, None, ["Mk"], ["Mk"])
-    act("keep", T.keep[:], T.j16[:], Act.Sign, ["j16"], ["keep"])
-    act("K16", T.K16[:], T.keep[:], ID, ["keep"], ["K16"], scale=2 * BIG, bias=-BIG)
+    ts("Mk", T.Mk[:], T.j16[:], rb, -BIG, Alu.not_equal, Alu.mult, ["j16", "cB"], ["Mk"])
+    ts("K16", T.K16[:], T.j16[:], 0.5, 2 * BIG, Alu.subtract, Alu.mult, ["j16"], ["K16"])
+    ts("keep", T.keep[:], T.j16[:], 0.0, None, Alu.not_equal, None, ["j16"], ["keep"])
     act("a0", T.a1[:], T.j16[:, 0:M], Act.Abs, ["j16", "neg"], ["a1"], bias=nr)
     act("ab", T.ab[:], T.a1[:, 0:16], Act.Copy, ["a1"], ["ab"])
     act("a1", T.a1[:], T.a1[:], Act.Sign, ["a1"], ["a1"])
     act("rc1", T.cG[:, 11:12], rc, ID, ["cF"], ["rc1"], bias=1.0)
     ts("a2", T.a2[:], T.j16[:, 0:M], T.cG[:, 11:12], K16W, Alu.is_equal, Alu.mult, ["j16", "rc1"], ["a2"])
     tt("A16", T.A16[:], T.a1[:], T.a2[:], Alu.max, ["a1", "a2"], ["A16"])
-    act("mM", T.mM[:], T.Mk[:], Act.Relu, ["Mk"], ["mM"], scale=HOLD / BIG)
-    tt("D1", T.D1[:, 0:C - 1], T.mM[:, 1:C], T.mM[:, 0:C - 1], Alu.subtract, ["mM"], ["uu"])
+    act("dp", T.cG[:, 14:15], rc, ID, ["cF"], ["dp"], scale=2 * HOLD, bias=-HOLD)
+    act("D1", T.D1[:], T.j16[:], ID, ["j16", "dp"], ["uu"], scale=-2 * HOLD, bias=T.cG[:, 14:15])
     ts("z0", T.cG[:, 13:14], rc, 0.0, HOLD, Alu.is_equal, Alu.mult, ["cF"], ["z0"])
-    ts("z1", T.cG[:, 14:15], rc, 15.0, HOLD, Alu.is_lt, Alu.mult, ["cF"], ["z1"])
+    act("z1", T.cG[:, 21:22], rc, Act.Square, ["cF"], ["z1"], scale=-HOLD ** 0.5, bias=15 * HOLD ** 0.5)
     act("z2", T.cG[:, 15:16], T.cG[:, 13:14], ID, ["z0"], ["z2"], scale=-1.0, bias=0.25)
-    act("z3", T.cG[:, 16:17], T.cG[:, 13:14], ID, ["z0", "z1"], ["z3"], bias=T.cG[:, 14:15])
-    up16 = T.w4[:, 14:15]
-    ts("wb", up16, rc, 15.0, K16W, Alu.is_lt, Alu.mult, ["cF"], ["wb"])
-    ts("up16", up16, up16, 1.0, None, Alu.max, None, ["wb"], ["wb"])
+    act("z3", T.cG[:, 16:17], T.cG[:, 13:14], ID, ["z0", "z1"], ["z3"], bias=T.cG[:, 21:22])
+    ts("wb", T.cG[:, 18:19], rc, 15.0, K16W, Alu.is_lt, Alu.mult, ["cF"], ["wb"])
+    ts("up16", T.cG[:, 18:19], T.cG[:, 18:19], 1.0, None, Alu.max, None, ["wb"], ["wb"])
     ts("dn16", T.cG[:, 12:13], rc, 15.0, 1.0 / K16W, Alu.is_equal, Alu.max, ["cF"], ["dn16"])
     mset("gap", T.Xt[:, 4 * HI:4 * HI + GAP], 0.0, ["gap"])
-    mset("big", T.big[:], 512.0, ["big"])
     for u, (rows, width, first) in enumerate(TILES):
         a, z = (4 * (first + 16 * min(i for i in rows if i != "d")), 4 * (first + width)) if u < 4 else (4 * first, 4096)
         mset("CT%d" % u, T.CT[:, a:z], 0.0, ["CT%s" % str(i) for i in rows])
     quant("qpad", T.QC[:, 896:1024], T.SC[:, 896:1024], T.CT[:, 4 * 896:4096], ["CT1", "CT2", "CT3", "CT4"], ["QC4"])
     iota("Gi", T.Gi[:], [[1, 8], [0, 64]], 0, 0, ["Gi"])
     add("kI", "G", lambda: G.dma_start(T.kI[0:1, :], T.kap[:], allow_slow_non_contiguous=True), ["Gi"], ["kI"], "lk")
-    act("Gt0", T.Gt[:], T.Gi[:], Act.Abs, ["Gi", "neg"], ["Gt"], bias=ng)
-    act("Gt1", T.Gt[:], T.Gt[:], Act.Relu, ["Gt"], ["Gt"], bias=1.0, scale=-1.0)
+    ts("Gt", T.Gt[:], T.Gi[:], gb, None, Alu.is_equal, None, ["Gi", "cB"], ["Gt"])
     quant("qG", T.QG[:], T.SG[:], T.Gt[:], ["Gt"], ["QG"])
     iota("i16", T.i16[:], [[16, 32]], 0, 0, ["i16"])
     act("cG2", T.cG[:, 2:3], rc, ID, ["cF"], ["cG2"], scale=-1.0, bias=15.0)
@@ -191,18 +192,19 @@ def build(g, core, T, topo):
     act("RC", T.RC[:], T.i16[:, 0:NI], ID, ["i16", "cG3"], ["RC"], bias=T.cG[:, 3:4])
     n4 = 256
     iota("j4", T.j4[:], [[0, n4 // 4], [1, 4]], 0, 0, ["j4"])
-    ts("A4", T.A4[:], T.j4[:], r4, K4W, Alu.not_equal, Alu.mult, ["j4", "cF"], ["A4"])
+    ts("A4", T.A4[:], T.j4[:], r4b, K4W, Alu.not_equal, Alu.mult, ["j4", "cB"], ["A4"])
     ts("w4a", T.w4[:, 0:4], T.j4[:, 0:4], r4, 1.0 / K4W, Alu.not_equal, Alu.mult, ["j4", "cF"], ["w4a"])
     ts("w4b", T.w4[:, 8:12], T.j4[:, 0:4], r4, None, Alu.is_equal, None, ["j4", "cF"], ["w4b"])
     scan("up", T.s4[:, 0:4], T.A4[:, 0:4], T.w4[:, 8:12], 0.0, Alu.mult, Alu.add, ["A4", "w4b"], ["up"])
     scan("down", T.s4[:, 8:12], T.w4[:, 0:4], T.w4[:, 8:12], 0.0, Alu.mult, Alu.add, ["w4a", "w4b"], ["down"])
-    up, down = T.s4[:, 3:4], T.s4[:, 11:12]
+    act("ud", T.cG[:, 19:20], T.s4[:, 3:4], ID, ["up", "dn16"], ["ud"], scale=T.cG[:, 12:13])
+    ud, down = T.cG[:, 19:20], T.s4[:, 11:12]
     iota("iP0", T.iP[:, 0:HI], [[4, HI]], -MID, 0, ["iP0"])
     iota("iP1", T.iP[:, HI:C], [[4, C - HI]], 4 * HI + GAP - MID, 0, ["iP1"])
     act("iO", T.iO[:], T.iP[:], ID, ["iP0", "iP1", "down"], ["iO"], scale=down)
     LS, LEND, LFa, LFb = T.L[:, 0:1], T.L[:, 2:3], T.L[:, 4:5], T.L[:, 6:7]
     mset("Lf0", T.Lf[:], 0.0, ["Lf"])
-    mset("kq0", T.kq[:], 1.0, ["kq"])
+    iota("kq0", T.kq[:], [[0, SW]], 1, 0, ["kq"])
     mset("kq1", T.kq[:, 0:SW:192], 0.0, ["kq"])
     mset("kq2", T.kq[:, 320:321], 0.0, ["kq"])
     mset("rs0", T.rs[:, 4 * SW:4 * SW + 2], 0.0, ["rsz"])
@@ -225,8 +227,9 @@ def build(g, core, T, topo):
     for c, r in enumerate(CH):
         act("Lr%d" % c, T.Lf[:, 14 + 4 * c:15 + 4 * c], T.Lf[:, 12 + 4 * c:13 + 4 * c], ID, ["Lq", "qg%d" % c], ["Lr%d" % c],
             scale=-float(r), bias=T.qf[:, 4 + c:5 + c])
-    act("cG4", T.cG[:, 4:5], r4, Act.Square, ["cF"], ["cG4"], bias=1.5)
-    act("Le", T.Lf[:, 2:3], T.cG[:, 4:5], ID, ["cG4", "Lf"], ["Le"], scale=8.0, bias=-3.0)
+    act("cG4", T.cG[:, 4:5], r4, Act.Square, ["cF"], ["cG4"], bias=1.75)
+    act("t85", T.cG[:, 20:21], t4, ID, ["cF"], ["t85"], bias=-8.5)
+    act("Le", T.Lf[:, 2:3], T.cG[:, 4:5], ID, ["cG4", "t85", "Lf"], ["Le"], scale=8.0, bias=T.cG[:, 20:21])
     ts("own", T.cG[:, 5:6], h2, gc_, None, Alu.is_equal, None, ["cF"], ["own"])
     ts("La", T.Lf[:, 4:5], b2, 6.0, T.cG[:, 5:6], Alu.add, Alu.mult, ["cF", "own", "Lf"], ["La"])
     act("b5", T.cG[:, 6:7], b2, ID, ["cF"], ["b5"], scale=2.0, bias=5.0)
@@ -237,13 +240,13 @@ def build(g, core, T, topo):
     cp("kF", T.kF[0:1, :], T.kI[0:1, :], ["kI"], ["kF"])
     add("dk", "G", lambda: G.partition_broadcast(T.dk[:], T.kF[0:1, :], 128), ["kF"], ["dk"])
     for c in range(NC):
-        act("D%d" % c, T.D16[:, 16 * c:16 * c + 16], T.dk[:].indirect(T.L[:, 12 + 4 * c:13 + 4 * c]), Act.Copy, ["dk", "L"], ["D%d" % c])
+        act("dk%d" % c, T.D16[:, 16 * c:16 * c + 16], T.dk[:].indirect(T.L[:, 12 + 4 * c:13 + 4 * c]), Act.Copy, ["dk", "L"], ["D%d" % c])
     act("p256", T.cG[:, 8:9], rc, ID, ["cF"], ["p256"], bias=2.0 * M)
     for c in range(4):
         act("h4%d" % c, T.h4[:, c:c + 1], rc, ID, ["cF"], ["h4%d" % c], scale=4.0, bias=8.0 * M + c)
     mset("nb", T.nb[:], -BIG, ["nb"])
     mset("pre0", T.pre[:], BIG, ["pre"])
-    mset("FT0", T.FT[:], 0.0, ["FT"])
+    iota("FT0", T.FT[:], [[0, 512]], 0, 0, ["FT"])
     iota("Ri", T.Ri[:], [[0, 8], [1, 16], [0, 4]], 0, 0, ["Ri"])
     act("Rt0", T.Rt[:], T.Ri[:], Act.Abs, ["Ri", "neg"], ["Rt"], bias=nr)
     act("Rt1", T.Rt[:], T.Rt[:], Act.Relu, ["Rt"], ["Rt"], bias=1.0, scale=-1.0)
@@ -253,20 +256,23 @@ def build(g, core, T, topo):
         act("Ru%d" % c, T.Rt[:, c:512:4], T.Rt[:, c:512:4], ID, ["Rt", "w2", "w3"], ["Ru%d" % c], scale=w)
     quant("qR", T.QR[:], T.SR[:], T.Rt[:], ["Rt"] + ["Ru%d" % c for c in range(4)], ["QR"])
     act("p16", T.cG[:, 17:18], rc, ID, ["cF"], ["p16"], scale=16.0, bias=float(SPARE))
-    act("Dc", T.Dc[:, 0:8], T.i16[:, 0:8], ID, ["i16", "p16"], ["Dc"], scale=16.0, bias=T.cG[:, 17:18])
-    act("Dn", T.Dc[:, 8:16], T.Dc[:, 0:8], Act.Copy, ["Dc"], ["Dn"], scale=-1.0)
-    iota("A0", T.A[:], [[0, SEG[8]]], 0, 0, ["A"])
-    for i in range(8):
-        act("Ad%d" % i, T.A[:, SEG[i + 1] - 16:SEG[i + 1]], T.ab[:], Act.Relu, ["A", "ab", "Dc", "Dn"], ["Ad%d" % i],
-            scale=T.Dc[:, 8 + i:9 + i], bias=T.Dc[:, i:i + 1])
-    act("A2", T.A[:], T.A[:], ID, ["A"] + ["Ad%d" % i for i in range(8)], ["A"], bias=1.0)
-    for i in (1, 2, 3, 5, 6, 7):
-        iota("Az%d" % i, T.A[:, SEG[i]:SEG[i] + 1], [[0, 1]], 0, 0, ["A"])
-    iota("Et0", T.Et[:], [[0, 2048]], 1, 0, ["Et"])
-    add("Et1", "G", lambda: G.affine_select(T.Et[:], T.Et[:], [[-1, 4], [-16, 128], [1, 4]], Alu.is_equal, 0.0, 0, 16),
-        ["Et"], ["Et"])
+    act("Dc", T.Dc[:], T.i16[:, 0:8], ID, ["i16", "p16"], ["Dc"], scale=16.0, bias=T.cG[:, 17:18])
+    iota("A0", T.A[:], [[0, SEG[4]]], 0, 0, ["A"])
+    for q in range(4):
+        z = SEG[q + 1]
+        act("Ad%d" % q, T.A[:, z - 20:z - 4], T.ab[:], Act.Relu, ["A", "ab"], ["Ad%d" % q], scale=-LIFT, bias=LIFT)
+        act("As%d" % q, T.A[:, z - 4:z - 3], T.ab[:, 0:1], ID, ["A", "ab"], ["As%d" % q], scale=0.0, bias=-LIFT - HOLD)
+        act("At%d" % q, T.A[:, z - 3:z], T.ab[:, 0:3], ID, ["A", "ab"], ["At%d" % q], scale=0.0, bias=1.0)
+        if q:
+            act("Az%d" % q, T.A[:, SEG[q]:SEG[q] + 1], T.ab[:, 0:1], ID, ["A", "ab"], ["Az%d" % q], scale=0.0, bias=-2 * LIFT)
+    kA = ["A"] + [n + str(q) for q in range(4) for n in ("Ad", "As", "At", "Az")]
+    iota("Eq", T.EQ[:], [[0, 2 * SEG[4]]], -4 * int(HOLD), 0, ["EQ%d" % i for i in range(8)] + ["sl%d" % i for i in range(8)])
+    iota("HG", T.HG[:], [[0, 32]], 0, 0, ["g1", "g2", "g3"])
+    iota("Zt", T.Zt[:], [[0, 512]], 0, 0, ["Zt"])
     for b in range(4):
-        quant("qE%d" % b, T.QE[:, M * b:M * b + M], T.SE[:, M * b:M * b + M], T.Et[:, 512 * b:512 * b + 512], ["Et"], ["QE%d" % b])
+        add("Et%d" % b, "G", lambda b=b: G.affine_select(T.Et[:, 512 * b:512 * b + 512], T.Zt[:], [[-4, 128], [-1, 4]], Alu.not_equal,
+                                                         1.0, b, 4), ["Zt"], ["Et%d" % b])
+        quant("qE%d" % b, T.QE[:, M * b:M * b + M], T.SE[:, M * b:M * b + M], T.Et[:, 512 * b:512 * b + 512], ["Et%d" % b], ["QE%d" % b])
 
     cp("Qg", T.Qg[:].bitcast(dt.uint32), T.Qu[:].bitcast(dt.uint32).indirect(T.uL[:]), ["Qu", "uL"], ["Qg"])
     act("Sg", T.Sg[:], T.Su[:].indirect(T.uL[:]), Act.Copy, ["Qu", "uL"], ["Sg"])
@@ -299,9 +305,9 @@ def build(g, core, T, topo):
         mm("m1", ps(1, 0, C), T.Qg[:], T.Sg[:], T.QA[:, 0:C], T.SA[:, 0:C], kG + ["QX0", "QX1"], ["B1"])
         mm("m0", ps(0, 0, C), T.Qg[:], T.Sg[:], T.QA[:, 0:C], T.SA[:, 0:C], kG + ["QX0", "QX1"], ["B0"])
         act("Xh", T.Xh[:], T.Xt[:, 0:XE], Act.Copy, kX + ["gap"], ["Xh"], scale=0.5)
-        tt("dH", T.d1[:, HI:C], ps(3, 0, C - HI), T.Mk[:, HI:C], Alu.min, ["B3", "Mk"], ["dH"])
+        tt("dH", T.d1[:, HI:C], ps(3, 0, C - HI), T.Mk[:, HI:C], Alu.add, ["B3", "Mk"], ["dH"])
         scan("WH", T.W[:, HI:C], T.K16[:, HI:C], T.d1[:, HI:C], -BIG, Alu.min, Alu.max, ["K16", "dH"], ["WH"])
-        tt("dL", T.d1[:, 0:HI], ps(0, 0, HI), T.Mk[:, 0:HI], Alu.min, ["B0", "Mk"], ["dL"])
+        tt("dL", T.d1[:, 0:HI], ps(0, 0, HI), T.Mk[:, 0:HI], Alu.add, ["B0", "Mk"], ["dL"])
         scan("WL", T.W[:, 0:HI], T.K16[:, 0:HI], T.d1[:, 0:HI], -BIG, Alu.min, Alu.max, ["K16", "dL"], ["WL"])
         diag = T.CT[:, 0:4 * C:4]
         tt("dg", diag, T.W[:], ps(0, 0, C), Alu.is_ge, ["WH", "WL", "B0"], ["CTd"])
@@ -342,7 +348,7 @@ def build(g, core, T, topo):
         quant_y()
         act("Yh", T.Yh[:], T.Yt[:], Act.Copy, kY, ["Yh"], scale=0.5)
         mm("mS", ps(3, 0, M), T.Qg[:], T.Sg[:], T.QA[:, C:C + M], T.SA[:, C:C + M], kG + ["QY"], ["B3"])
-        tt("d3", T.d3[:], ps(3, 0, M), T.Mk[:, 0:M], Alu.min, ["B3", "Mk"], ["d3"])
+        tt("d3", T.d3[:], ps(3, 0, M), T.Mk[:, 0:M], Alu.add, ["B3", "Mk"], ["d3"])
         scan("Wm", T.Wm[:], T.K16[:, 0:M], T.d3[:], -BIG, Alu.min, Alu.max, ["K16", "d3"], ["Wm"])
         scan("W2", T.W2[:], ps(2, 0, C), T.D1[:], HOLD, Alu.min, Alu.add, ["uu", "B2"], ["W2"])
         ts("roff", T.roff[:], T.W2[:, 15:C:16], T.cG[:, 15:16], None, Alu.add, None, ["W2", "z2"], ["roff"])
@@ -353,36 +359,47 @@ def build(g, core, T, topo):
             sk, sg = "sm%d" % i, T.sm[:, C * i:C * i + C]
             if i in PAR["vmsg"]:
                 ts("f%d" % i, sg, ps(0, 0, C), own, None, Alu.is_gt, None, ["B0", "Wm"], [sk])
-                scan("g%d" % i, T.vb[:, C * i:C * i + C], sg, T.big[:], -128.0, Alu.add, Alu.min, [sk, "big"], ["vb%d" % i])
-                ts("n%d" % i, T.n[:, i:i + 1], T.vb[:, C * i + C - 1:C * i + C], 128.0, None, Alu.add, None, ["vb%d" % i], ["n%d" % i])
+                scan("g%d" % i, T.vb[:, C * i:C * i + C], T.kq[:, 0:C], sg, 0.0, Alu.mult, Alu.add, [sk, "kq"], ["vb%d" % i])
+                tt("n%d" % i, T.n[:, i:i + 1], T.vb[:, C * i + 191:C * i + 192], T.vb[:, C * i + C - 1:C * i + C], Alu.add,
+                   ["vb%d" % i], ["n%d" % i])
             else:
                 act("f%d" % i, sg, ps(1, 0, C), Act.Sign, ["B1", "Wm"], [sk], bias=own, scale=-1.0)
                 act("n%d" % i, sg, sg, Act.Relu, [sk], ["n%d" % i, sk], scale=-1.0, accum_out=T.n[:, i:i + 1])
         for h, r in enumerate(CH):
             i0, n = sum(CH[:h]), 64 * r
             z0, pos, pk = 16 * i0, T.pos[:, 16 * h:16 * h + 16], "pof%d" % h
-            pof, er = T.pof[:, 16 * h:16 * h + 4 * r], T.er[:, 64 * i0:64 * i0 + n]
             tt("pos%d" % h, pos, T.n[:, 0:i0 + r].indirect(T.L[:, 14 + 4 * h:15 + 4 * h]), T.D16[:, 16 * h:16 * h + 16], Alu.add,
                ["n%d" % i for i in range(i0 + r)] + ["L", "D%d" % h], ["pos%d" % h])
-            cp(pk, pof, T.pos[:, 16 * h:16 * h + 4 * r], ["pos%d" % h], [pk])
-            if PAR["eg"][h] == "V":
-                cp("er%d" % h, er, T.o2[:].indirect(pof), ["o2a", "o2b", pk], ["er%d" % h])
-            else:
-                act("er%d" % h, er, T.o2[:].indirect(pof), Act.Copy, ["o2a", "o2b", pk], ["er%d" % h])
-            scan("e4%d" % h, T.e4[:, 4 * z0:4 * z0 + n], T.A4[:, 0:n], er, 0.0, Alu.mult, Alu.add, ["A4", "er%d" % h], ["e4%d" % h])
-            ts("zof%d" % h, T.zof[:, z0:z0 + n // 4], T.e4[:, 4 * z0 + 3:4 * z0 + n:4], t640, None, Alu.add, None,
-               ["e4%d" % h, "t640"], ["zof%d" % h])
+            cp(pk, T.pof[:, 16 * h:16 * h + 4 * r], T.pos[:, 16 * h:16 * h + 4 * r], ["pos%d" % h], [pk])
+            for name, ka, kz in ((("a", 0, 1), ("b", 1, F)) if h < PAR["cut"] else (("", 0, F),)):
+                a, z, u = 16 * r * ka, 16 * r * kz, "%d%s" % (h, name)
+                of, er = T.pof[:, 16 * h + r * ka:16 * h + r * kz], T.er[:, 4 * z0 + a:4 * z0 + z]
+                if PAR["eg"][h] == "V":
+                    cp("er" + u, er, T.o2[:].indirect(of), ["o2a", "o2b", pk], ["er" + u])
+                else:
+                    act("er" + u, er, T.o2[:].indirect(of), Act.Copy, ["o2a", "o2b", pk], ["er" + u])
+                scan("e4" + u, T.e4[:, 4 * z0 + a:4 * z0 + z], T.A4[:, a:z], er, 0.0, Alu.mult, Alu.add, ["A4", "er" + u], ["e4" + u])
+                ts("zof" + u, T.zof[:, z0 + a // 4:z0 + z // 4], T.e4[:, 4 * z0 + a + 3:4 * z0 + z:4], t640, None, Alu.add, None,
+                   ["e4" + u, "t640"], ["zof" + u])
             for k in range(F):
                 a, b = 512 * k + 64 * i0, 64 * i0 + 16 * r * k
+                u = "%d%s" % (h, "ab"[min(k, 1)] if h < PAR["cut"] else "")
                 tt("Z%d%d" % (k, h), T.Z[:, a:a + n], T.Xh[:].indirect(T.zof[:, z0 + 4 * r * k:z0 + 4 * r * (k + 1)]),
-                   T.Yh[:, 64 * i0:64 * i0 + n], Alu.add, ["Xh", "Yh", "zof%d" % h], ["Z%d%d" % (k, h)])
+                   T.Yh[:, 64 * i0:64 * i0 + n], Alu.add, ["Xh", "Yh", "zof" + u], ["Z%d%d" % (k, h)])
                 act("ec%d%d" % (k, h), T.erep[:, M * k + 16 * i0:M * k + 16 * (i0 + r)], T.er[:, b:b + 16 * r], ID,
-                    ["er%d" % h, "up"], ["ec%d%d" % (k, h)], scale=up)
+                    ["er" + u, "ud"], ["ec%d%d" % (k, h)], scale=ud)
         for k in range(F):
             quant("qz%d" % k, QZ[:, M * k:M * k + M], SZ[:, M * k:M * k + M], T.Z[:, 512 * k:512 * k + 512],
                   ["Z%d%d" % (k, h) for h in range(NC)], ["QZ%d_%d" % (t, k)])
             mm("mZ%d" % k, ps(4 + k, 0, M), QZ[:, M * k:M * k + M], SZ[:, M * k:M * k + M], T.Qu[:], T.Su[:],
                ["QZ%d_%d" % (t, k), "Qu"], ["B%d" % (4 + k)])
+        for k in range(F):
+            scan("EW%d" % k, T.EW[:, M * k:M * k + M], T.A16[:], T.erep[:, M * k:M * k + M], 0.0, Alu.mult, Alu.add,
+                 ["A16"] + ["ec%d%d" % (k, h) for h in range(NC)], ["EW%d" % k])
+        cp("H0", T.HD[:, 3:32:4], T.EW[:, 15:M:16], ["EW0"], ["H0"])
+        for k in range(1, F):
+            tt("H%d" % k, T.HD[:, 3 - k:32:4], T.EW[:, M * k + 15:M * k + M:16], T.EW[:, M * k - M + 15:M * k:16], Alu.subtract,
+               ["EW%d" % k, "EW%d" % (k - 1)], ["H%d" % k])
         kQZ = ["QZ%d_%d" % (t, k) for k in range(F)]
         kZ = ["Z%d%d" % (k, h) for k in range(F) for h in range(NC)]
         kE = ["ec%d%d" % (k, h) for k in range(F) for h in range(NC)]
@@ -405,24 +422,25 @@ def build(g, core, T, topo):
         act("okb", T.jk[:, 16:24], T.FT[:, 1:32:4], ID, ["Fb"], ["okb"], scale=-1.0, bias=0.125, accum_out=T.okc[:, 5:6])
         act("okc", T.okc[:, t:t + 1], T.okc[:, 4:5], ID, ["oka", "okb"], ["okc%d" % t], bias=T.okc[:, 5:6])
         dma("ok", "Y", T.ok[t], T.okc[:, t:t + 1], ["okc%d" % t], [], "outh")
-        act("ew", T.ew[:], T.erep[:].indirect(T.ziu[:]), ID, kE + ["ziu", "dn16"], ["ew"], scale=T.cG[:, 12:13])
-        scan("ews", T.ews[:], T.A16[:, 0:M], T.ew[:], 0.0, Alu.mult, Alu.add, ["A16", "ew"], ["ews"])
+        act("ew", T.ew[:], T.erep[:].indirect(T.ziu[:]), ID, kE + ["ziu", "wb"], ["ew"], scale=T.cG[:, 18:19])
+        for k in range(1, F):
+            ts("G%d" % k, T.HG[:, 4 - k:32:4], ps(3, 0, 8), float(M * k - 2 * M), None, Alu.is_ge, None, ["B3"], ["g%d" % k])
+        scan("OW", T.OW[:], T.HG[:], T.HD[:], 0.0, Alu.mult, Alu.add, ["g1", "g2", "g3", "H0", "H1", "H2", "H3"], ["OW"])
         for h in (1, 0):
             act("Hp%d" % h, T.Hp[:, 256 * h:256 * h + 256], T.Z[:].indirect(T.hof[:, 16 * h:16 * h + 16]), Act.Copy,
                 kZ + ["hof%d" % c for c in range(4)], ["Hp%d" % h])
-            for i in range(4 * h, 4 * h + 4):
-                ts("EQ%d" % i, T.EQ[:, SEG[i]:SEG[i + 1]], T.ew[:, 64 * h:16 * i + 16], up16, T.ews[:, 16 * i + 15:16 * i + 16],
-                   Alu.mult, Alu.is_equal, ["ew", "ews", "wb"], ["EQ%d" % i])
-            a, e1, e2 = 160 * h, T.e[:, 32 * h:32 * h + 16], T.e[:, 32 * h + 16:32 * h + 32]
-            act("e1%d" % h, e1, T.ews[:, 64 * h + 3:64 * h + 64:4], ID, ["ews"], ["e1%d" % h], bias=MID + 4.0)
-            scan("st%d" % h, T.st[:, a:a + 160], T.A[:, a:a + 160], T.EQ[:, a:a + 160], 0.0, Alu.mult, Alu.max,
-                 ["A"] + ["EQ%d" % i for i in range(4 * h, 4 * h + 4)], ["st%d" % h])
-            tt("e2%d" % h, e2, T.st[:, a:a + 160].indirect(LEND), e1, Alu.max, ["st%d" % h, "L", "e1%d" % h], ["e2%d" % h])
-            for c in range(4):
-                ts("xo%d%d" % (c, h), T.xof[:, 16 * h + c:16 * h + 16:4], T.e[:, 32 * h + 19:32 * h + 32:4], c - 4.0, None, Alu.add, None,
-                   ["e2%d" % h], ["xo%d%d" % (c, h)])
+            a, rows = SEG[4] * h, range(4 * h, 4 * h + 4)
+            for i in rows:
+                b, z, own = a + SEG[i % 4], a + SEG[i % 4 + 1] - 4, T.OW[:, 4 * i + 3:4 * i + 4]
+                ts("EQ%d" % i, T.EQ[:, b:z], T.ew[:, 64 * h:16 * i + 16], own, T.Dc[:, i:i + 1], Alu.is_equal, Alu.mult,
+                   ["ew", "OW", "Dc"], ["EQ%d" % i])
+                act("sl%d" % i, T.EQ[:, z:z + 1], own, Act.Copy, ["OW"], ["sl%d" % i])
+            scan("st%d" % h, T.st[:, a:a + SEG[4]], T.A[:], T.EQ[:, a:a + SEG[4]], 0.0, Alu.add, Alu.max,
+                 kA + ["EQ%d" % i for i in rows] + ["sl%d" % i for i in rows], ["st%d" % h])
+            ts("xo%d" % h, T.xof[:, 16 * h:16 * h + 16], T.st[:, a:a + SEG[4]].indirect(LEND), float(MID), None, Alu.add, None,
+               ["st%d" % h, "L"], ["xo%d" % h])
             cp("X" if h == 0 else "XA", T.Xt[:].indirect(T.xof[:, 16 * h:16 * h + 16]), T.Hp[:, 256 * h:256 * h + 256],
-               ["xo%d%d" % (c, h) for c in range(4)] + ["Hp%d" % h, "gap"], kX)
+               ["xo%d" % h, "Hp%d" % h, "gap"], kX)
 
     at[1] = "!"
     new_y(R - 1, [4, 5, 6, 7], [0, 1, 2, 3])

from concourse.mybir import dt, AluOpType, ActivationFunctionType

C, M, F, R = 320, 128, 4, 3
NI = C // 16
BIG = 2.0 ** 96
K16W, K4W = 2.0 ** 30, 2.0 ** 13
SEG = [8 * q * (q + 1) + 4 * q for q in range(5)]
HI = 192
GAP = 8
XE = 4 * C + GAP
MID = 4 * HI + 4
HOLD = 1024.0
SPARE = 1552
LIFT = 8192.0
SW = 384
VR = 12

TILES = [(("d", 19, 18, 17), 320, 0), ((16, 15, 14, 13), 256, 320), ((9, 10, 11, 12), 192, 576),
         ((5, 6, 7, 8), 128, 768), ((1, 2, 3, 4), 64, 896)]
PAR = {
    "vmsg": (0, 4),
    "chunks": (4, 4),
    "eg": "VS",
    "cut": 1,
    "pe": (0, 3, 4, 2, 1),
}

Q4, U8, BF, F32, I32, U16 = "float8_e4m3fn_x4", "uint8", "bfloat16", "float32", "int32", "uint16"
SCRATCH = {"ps": ("psum", [128, 4096], F32)}
for _d, _l in (
        (BF, "Xt:3344 Xh:1288 Yt:512 Yh:512 Z:2048 ut:512 vt:512 CT:4096 FT:512 Et:2048 Zt:512 Gi:512 Gt:512 Ri:512 Rt:512 j16:320 "
             "Mk:320 K16:320 keep:320 A16:128 a1:128 a2:128 cB:8 ab:16 j4:256 A4:256 w4:16 A:176 Dc:8 EW:512 OW:32 iO:320 iP:320 "
             "sg:2240 sm:2560 vb:2560 rs:1538 kq:384 rd:320 o2:640 er:512 e4:512 jk:32 erep:512 Hp:512 ew:128 EQ:352"),
        (F32, "cF:8 cG:24 Lf:24 i16:32 RC:20 D1:320 st:352 HD:32 HG:32 h4:4 nb:4 kF:16 dk:16 D16:48 qf:16 d1:320 W:320 s4:16 "
              "W2:320 d3:128 Wm:128 RS:20 tr:20 n:8 pos:48 pre:16 okc:8 Rr:512 ysb:448"),
        (I32, "pI:16 cI:8 kI:16 qI:8"),
        (U16, "uL:8 L:24 roff:20 pof:48 zof:128 ziu:8 hof:32 xof:32")):
    for _e in _l.split():
        SCRATCH[_e.split(":")[0]] = ("sbuf", [128, int(_e.split(":")[1])], _d)
for _e in ("A:448 u:128 v:128 g:128 W:512 C:1024 F:128 E:512 G:128 R:128 Z0:512 Z1:512 Z2:512 H0:128 H1:128 H2:128 "
           "L0:128 L1:128 L2:128").split():
    SCRATCH["Q" + _e.split(":")[0]] = ("sbuf", [128, int(_e.split(":")[1])], Q4)
    SCRATCH["S" + _e.split(":")[0]] = ("sbuf", [128, int(_e.split(":")[1])], U8)

SEMAPHORES = ["cV", "cS", "cP", "cG", "lu", "lx0", "lx1", "lm", "lv", "lwc", "lws", "lk", "outh", "outg", "sent",
              "arr0", "arr1", "arr2"]

FIRST = {
    "V": "CT4 CT2 cI5 cI4 cI2 cI0 cI3 cI1 pm Lf0 cF pmb pma CT0 own z0 rs0 cB nb CT1 pmf K16 gap pre0 keep uL qI dn16 La wb Mk "
         "qu CT3 qx1 Qg up16 qx0 sz Gt Lq Ls dH qpad WH dL c12 WL qG A4 c10 w4a c11 c7 c9 c8 c6 qy w4b dg c5 L c1 kq1 d3 c3 kq2 "
         "c2 c4 down rd s0 s2 Wm q0 kF s3 s1 q3 q2 t1 q1 ua f0 ub f4 W2 g0 roff g4 n0 o2a pos0 n4 o2b pof0 up a2 er0b er0a e40b "
         "e40a pos1 zof0b zof0a pof1 Z10 Z20 e41 Z30 zof1 Z00 Z01 Z11 Z21 Z31 qz0 qz2 qz1 qz3 A16 qR pre EW0 EW1 Fa Fb qv H1 qF "
         "EW2 EW3 qE3 H0 H2 H3 ziu G2 G1 G3 QH OW hof1 hof0 hof2 hof3 EQ5 EQ7 EQ6 EQ4 EQ3 EQ0 EQ2 EQ1 st1 st0 xo1 qE2 xo0 XA qE0 "
         "X qE1",
    "S": "lx1 z1 t85 neg t640 qf1 b5 qf0 cG2 qg1 cG4 z3 a0 qg0 sq dp Le Lb rc1 ab se cG3 D1 h40 sp Sg Xh Lr1 z2 a18 a19 Lr0 a16 "
         "a17 b19 b17 RC a14 b18 a13 a15 b13 b14 b16 f3 b15 f6 f1 dk0 f2 n1 iO n3 f5 n2 f7 n6 n7 n5 dk1 Yh h41 ud p256 h42 er1 "
         "w2 Rt0 ec30 Ad3 Rt1 w3 Az3 As3 As1 Ad2 At1 At0 ec00 At3 ec20 Ru3 p16 Ru0 ec11 As2 a1 Az2 At2 Ru1 h43 ec31 Dc As0 Ru2 "
         "ec21 Az1 ec01 ec10 okb Ad1 oka Ad0 ew SH sl6 sl4 sl7 sl5 sl3 sl0 sl1 sl2 Hp1 okc Hp0",
    "P": "mH m1 m0 mS mC0 mC3 mC4 mC2 mC1 mZ0 mZ2 mZ1 mZ3 mF",
    "G": "pI j16 uI Gi iP1 j4 i16 kq0 kI A0 dk iP0 Zt Eq Et1 Ri Et3 FT0 Et2 HG Et0 sendQ sendS",
    "Y": "lu lx0 lm lwc lv lws ok"}
STEADY = {
    "V": "qx1 qx0 dH WH dL WL c12 c4 c8 c5 c9 dg s3 c1 c6 Y1 c7 Y0 c3 c2 s0 c11 Y2 Y3 s2 qy q3 c10 rd d3 s1 t1 Wm q2 q0 ua q1 f0 "
         "ub f4 W2 g0 roff g4 n0 o2a n4 pos0 o2b pof0 er0a er0b e40a pos1 e40b zof0a pof1 zof0b Z00 Z10 e41 Z20 zof1 Z30 Z01 Z21 "
         "Z31 Z11 qz2 qz3 qz0 qz1 EW0 EW3 EW1 pre H0 Fb Fa H1 qF EW2 H3 H2 ziu G1 G3 G2 hof1 hof3 hof2 OW QH hof0 EQ4 EQ5 EQ7 "
         "EQ6 EQ2 EQ0 EQ3 EQ1 st1 st0 xo1 xo0 XA X",
    "S": "Xh a18 a19 a14 a13 a16 Rr1 Rr0 b18 a17 Rr2 Rr3 a15 b19 b15 b16 b13 b17 b14 f3 f1 f2 n1 f6 n3 n2 n6 f5 f7 n5 n7 Yh er1 "
         "ec30 ec00 ec31 ec21 ec01 ec20 ec10 ec11 oka okb ew SH sl4 sl6 sl5 sl7 sl1 sl0 sl3 sl2 Hp1 Hp0 okc",
    "P": "mH m0 m1 mW1 mW0 mE0 mE1 mW3 mW2 mE2 mE3 mS mC0 mC3 mC4 mC2 mC1 mZ2 mZ3 mZ0 mZ1 mF",
    "G": "sendQ sendS", "Y": "ok", "A": "land"}
LAST = {
    "V": "qx1 qx0 dH WH dL c12 WL c1 dg c4 c3 c8 c11 c7 Y1 c10 Y0 c2 c9 rd Y3 Y2 c6 c5 t1 qy q2 s3 s0 d3 s1 q3 Wm q0 s2 q1 ua f0 "
         "ub f4 W2 g0 roff g4 n0 o2a n4 pos0 o2b pof0 er0a er0b e40a pos1 e40b zof0a pof1 zof0b Z00 Z10 e41 Z20 zof1 Z30 Z01 Z31 "
         "Z21 Z11 qz2 qz0 qz3 qz1 EW2 EW1 EW0 EW3 pre H3 Fb Fa qF H0 H2 H1 ziu G2 G3 G1 QH OW hof1 hof3 hof2 EQ6 EQ7 hof0 EQ4 "
         "EQ5 EQ0 EQ2 EQ1 EQ3 st1 st0 xo1 xo0 XA X qx0! Y1! Y0! Y2! Y3! qx1! qy!",
    "S": "Xh a17 a16 a13 b17 Rr1 Rr0 a15 a18 Rr3 Rr2 a14 b13 b18 a19 b15 b19 b14 b16 f1 f3 f7 f2 f6 n3 n1 n2 n6 f5 n7 n5 Yh ec30 "
         "er1 ec20 ec31 ec21 ec01 ec10 ec11 ec00 ew SH sl6 sl4 sl7 sl0 sl5 sl1 sl3 sl2 Hp1 Hp0 okb oka okc Rr1! Rr0! Rr2! Rr3! "
         "ysX0! oyX0! ysX1! ysY! oyX1! oyY!",
    "P": "mH m0 m1 mW1 mE0 mW0 mE1 mW3 mW2 mE3 mE2 mS mC0 mC3 mC4 mC2 mC1 mZ2 mZ0 mZ3 mZ1 mF mW1! mW0! mW2! mE1! mW3! mE0! mE2! "
         "mE3! mvX0! mvX1! mvY!",
    "G": "sendQ sendS os3!", "Y": "ok ocX! os0! ocY! os2! os1!", "A": "land land!"}
ORDER = [FIRST, STEADY, LAST]


def build(g, core, T, topo):
    Alu, Act = AluOpType, ActivationFunctionType
    rank = T.rank_of(core)
    nxt = T.cores[(rank + 1) % len(T.cores)]
    rid, pid = topo.addr(nxt)[0], topo.addr(nxt)[1]
    mask = topo.mask(core, nxt)
    ne = len(topo.engines(core, nxt))
    ops = []
    V, S, P, G, Y = g.vector, g.scalar, g.tensor, g, g.sync
    at = [0, ""]

    def add(name, eng, fn, r, w, sem=None, n=16):
        ops.append({"name": name + at[1], "at": at[0], "e": eng, "f": fn, "r": list(r), "w": list(w), "sem": sem, "n": n})

    def ps(b, a, z):
        return T.ps[:, 512 * b + a:512 * b + z]

    def ts(name, out, in0, s1, s2, op0, op1, r, w):
        if op1 is None:
            add(name, "V", lambda: V.tensor_scalar(out, in0, s1, None, op0), r, w)
        else:
            add(name, "V", lambda: V.tensor_scalar(out, in0, s1, s2, op0, op1), r, w)

    def tt(name, out, in0, in1, op, r, w):
        add(name, "V", lambda: V.tensor_tensor(out, in0, in1, op), r, w)

    def cp(name, out, in_, r, w):
        add(name, "V", lambda: V.tensor_copy(out, in_), r, w)

    def scan(name, out, a, b, init, op0, op1, r, w):
        add(name, "V", lambda: V.tensor_tensor_scan(out, a, b, init, op0, op1), r, w)

    def mset(name, ap, val, w):
        add(name, "V", lambda: V.memset(ap, val), [], w)

    def quant(name, q, s, t, r, w):
        add(name, "V", lambda: V.quantize_mx(q, s, t), r, w)

    def act(name, out, in_, fn, r, w, **kw):
        add(name, "S", lambda: S.activation(out, in_, fn, **kw), r, w)

    def mm(name, out, a, sa, b, sb, r, w, start=True, stop=True):
        add(name, "P", lambda: P.matmul_mx(out, a, sa, b, sb, start, stop), r, w)

    def iota(name, out, pat, base, cm, w, flt=True):
        if flt:
            add(name, "G", lambda: G.iota(out, pat, base, cm, allow_small_or_imprecise_dtypes=True), [], w)
        else:
            add(name, "G", lambda: G.iota(out, pat, base, cm), [], w)

    def dma(name, q, out, in_, r, w, sem):
        e = {"Y": Y, "S": S, "G": G}[q]
        add(name, q, lambda: e.dma_start(out, in_), r, w, sem)

    ID = Act.Identity

    dma("lu", "Y", T.ut[:], T.u[:], [], ["ut"], "lu")
    dma("lx1", "S", T.Xt[:, 4 * HI + GAP:XE], T.x[:, 4 * HI:4 * C], [], ["X1"], "lx1")
    dma("lx0", "Y", T.Xt[:, 0:4 * HI], T.x[:, 0:4 * HI], [], ["X0"], "lx0")
    dma("lm", "Y", T.Yt[:], T.m[:], ["ut"], ["Y0", "Y1", "Y2", "Y3"], "lm")
    quant("qu", T.Qu[:], T.Su[:], T.ut[:], ["ut"], ["Qu"])
    dma("lwc", "Y", T.QW[:].bitcast(dt.uint8), T.wc[:], ["Qu"], ["QW"], "lwc")
    dma("lws", "Y", T.SW[:], T.ws[:], ["Qu"], ["SW"], "lws")
    dma("lv", "Y", T.vt[:], T.v[:], ["Qu"], ["vt"], "lv")

    iota("uI", T.pI[:, 8:16], [[16, 8]], 0, 0, ["uI"], flt=False)
    cp("uL", T.uL[:], T.pI[:, 8:16], ["uI"], ["uL"])
    iota("pI", T.pI[:, 0:8], [[0, 8]], 0, 1, ["pI"], flt=False)
    for a, sh, an in [(0, 0, 15), (1, 4, 7), (2, 2, 3), (3, 0, 3), (4, 1, 7), (5, 0, 1)]:
        ts("cI%d" % a, T.cI[:, a:a + 1], T.pI[:, a:a + 1], sh, an, Alu.logical_shift_right, Alu.bitwise_and, ["pI"], ["cI%d" % a])
    cp("cF", T.cF[:, 0:6], T.cI[:, 0:6], ["cI%d" % c for c in range(6)], ["cF"])
    rc, gc_, r4, t4, h2, b2 = [T.cF[:, c:c + 1] for c in range(6)]
    cp("cB", T.cB[:, 0:6], T.cI[:, 0:6], ["cI%d" % c for c in range(6)], ["cB"])
    rb, gb, r4b = [T.cB[:, c:c + 1] for c in range(3)]
    act("neg", T.cG[:, 0:1], rc, Act.Copy, ["cF"], ["neg"], scale=-1.0)
    nr = T.cG[:, 0:1]
    iota("j16", T.j16[:], [[0, NI], [1, 16]], 0, 0, ["j16"])
    ts("Mk", T.Mk[:], T.j16[:], rb, -BIG, Alu.not_equal, Alu.mult, ["j16", "cB"], ["Mk"])
    ts("K16", T.K16[:], T.j16[:], 0.5, 2 * BIG, Alu.subtract, Alu.mult, ["j16"], ["K16"])
    ts("keep", T.keep[:], T.j16[:], 0.0, None, Alu.not_equal, None, ["j16"], ["keep"])
    act("a0", T.a1[:], T.j16[:, 0:M], Act.Abs, ["j16", "neg"], ["a1"], bias=nr)
    act("ab", T.ab[:], T.a1[:, 0:16], Act.Copy, ["a1"], ["ab"])
    act("a1", T.a1[:], T.a1[:], Act.Sign, ["a1"], ["a1"])
    act("rc1", T.cG[:, 11:12], rc, ID, ["cF"], ["rc1"], bias=1.0)
    ts("a2", T.a2[:], T.j16[:, 0:M], T.cG[:, 11:12], K16W, Alu.is_equal, Alu.mult, ["j16", "rc1"], ["a2"])
    tt("A16", T.A16[:], T.a1[:], T.a2[:], Alu.max, ["a1", "a2"], ["A16"])
    act("dp", T.cG[:, 14:15], rc, ID, ["cF"], ["dp"], scale=2 * HOLD, bias=-HOLD)
    act("D1", T.D1[:], T.j16[:], ID, ["j16", "dp"], ["uu"], scale=-2 * HOLD, bias=T.cG[:, 14:15])
    ts("z0", T.cG[:, 13:14], rc, 0.0, HOLD, Alu.is_equal, Alu.mult, ["cF"], ["z0"])
    act("z1", T.cG[:, 21:22], rc, Act.Square, ["cF"], ["z1"], scale=-HOLD ** 0.5, bias=15 * HOLD ** 0.5)
    act("z2", T.cG[:, 15:16], T.cG[:, 13:14], ID, ["z0"], ["z2"], scale=-1.0, bias=0.25)
    act("z3", T.cG[:, 16:17], T.cG[:, 13:14], ID, ["z0", "z1"], ["z3"], bias=T.cG[:, 21:22])
    ts("wb", T.cG[:, 18:19], rc, 15.0, K16W, Alu.is_lt, Alu.mult, ["cF"], ["wb"])
    ts("up16", T.cG[:, 18:19], T.cG[:, 18:19], 1.0, None, Alu.max, None, ["wb"], ["wb"])
    ts("dn16", T.cG[:, 12:13], rc, 15.0, 1.0 / K16W, Alu.is_equal, Alu.max, ["cF"], ["dn16"])
    mset("gap", T.Xt[:, 4 * HI:4 * HI + GAP], 0.0, ["gap"])
    for u, (rows, width, first) in enumerate(TILES):
        a, z = (4 * (first + 16 * min(i for i in rows if i != "d")), 4 * (first + width)) if u < 4 else (4 * first, 4096)
        mset("CT%d" % u, T.CT[:, a:z], 0.0, ["CT%s" % str(i) for i in rows])
    quant("qpad", T.QC[:, 896:1024], T.SC[:, 896:1024], T.CT[:, 4 * 896:4096], ["CT1", "CT2", "CT3", "CT4"], ["QC4"])
    iota("Gi", T.Gi[:], [[1, 8], [0, 64]], 0, 0, ["Gi"])
    add("kI", "G", lambda: G.dma_start(T.kI[0:1, :], T.kap[:], allow_slow_non_contiguous=True), ["Gi"], ["kI"], "lk")
    ts("Gt", T.Gt[:], T.Gi[:], gb, None, Alu.is_equal, None, ["Gi", "cB"], ["Gt"])
    quant("qG", T.QG[:], T.SG[:], T.Gt[:], ["Gt"], ["QG"])
    iota("i16", T.i16[:], [[16, 32]], 0, 0, ["i16"])
    act("cG2", T.cG[:, 2:3], rc, ID, ["cF"], ["cG2"], scale=-1.0, bias=15.0)
    act("cG3", T.cG[:, 3:4], T.cG[:, 2:3], ID, ["cG2", "z3"], ["cG3"], bias=T.cG[:, 16:17])
    act("RC", T.RC[:], T.i16[:, 0:NI], ID, ["i16", "cG3"], ["RC"], bias=T.cG[:, 3:4])
    n4 = 256
    iota("j4", T.j4[:], [[0, n4 // 4], [1, 4]], 0, 0, ["j4"])
    ts("A4", T.A4[:], T.j4[:], r4b, K4W, Alu.not_equal, Alu.mult, ["j4", "cB"], ["A4"])
    ts("w4a", T.w4[:, 0:4], T.j4[:, 0:4], r4, 1.0 / K4W, Alu.not_equal, Alu.mult, ["j4", "cF"], ["w4a"])
    ts("w4b", T.w4[:, 8:12], T.j4[:, 0:4], r4, None, Alu.is_equal, None, ["j4", "cF"], ["w4b"])
    scan("up", T.s4[:, 0:4], T.A4[:, 0:4], T.w4[:, 8:12], 0.0, Alu.mult, Alu.add, ["A4", "w4b"], ["up"])
    scan("down", T.s4[:, 8:12], T.w4[:, 0:4], T.w4[:, 8:12], 0.0, Alu.mult, Alu.add, ["w4a", "w4b"], ["down"])
    act("ud", T.cG[:, 19:20], T.s4[:, 3:4], ID, ["up", "dn16"], ["ud"], scale=T.cG[:, 12:13])
    ud, down = T.cG[:, 19:20], T.s4[:, 11:12]
    iota("iP0", T.iP[:, 0:HI], [[4, HI]], -MID, 0, ["iP0"])
    iota("iP1", T.iP[:, HI:C], [[4, C - HI]], 4 * HI + GAP - MID, 0, ["iP1"])
    act("iO", T.iO[:], T.iP[:], ID, ["iP0", "iP1", "down"], ["iO"], scale=down)
    LS, LEND, LFa, LFb = T.L[:, 0:1], T.L[:, 2:3], T.L[:, 4:5], T.L[:, 6:7]
    mset("Lf0", T.Lf[:], 0.0, ["Lf"])
    iota("kq0", T.kq[:], [[0, SW]], 1, 0, ["kq"])
    mset("kq1", T.kq[:, 0:SW:192], 0.0, ["kq"])
    mset("kq2", T.kq[:, 320:321], 0.0, ["kq"])
    mset("rs0", T.rs[:, 4 * SW:4 * SW + 2], 0.0, ["rsz"])
    ts("pm", T.qI[:, 4:6], T.pI[:, 0:2], 15.0, None, Alu.add, None, ["pI"], ["pm"])
    ts("pma", T.qI[:, 6:7], T.qI[:, 4:5], 0, 3, Alu.logical_shift_right, Alu.bitwise_and, ["pm"], ["pma"])
    ts("pmb", T.qI[:, 7:8], T.qI[:, 5:6], 2, 3, Alu.logical_shift_right, Alu.bitwise_and, ["pm"], ["pmb"])
    cp("pmf", T.qf[:, 8:10], T.qI[:, 6:8], ["pma", "pmb"], ["pmf"])
    act("sq", T.qf[:, 10:11], T.qf[:, 9:10], Act.Square, ["pmf"], ["sq"], bias=0.5)
    act("se", T.qf[:, 11:12], T.qf[:, 10:11], ID, ["sq"], ["se"], scale=-32.0, bias=SW + 7.0)
    act("sp", T.qf[:, 12:13], T.qf[:, 8:9], ID, ["pmf", "se"], ["sp"], scale=float(SW), bias=T.qf[:, 11:12])
    ts("sz", T.qf[:, 13:14], rc, 0.0, 4.0 * SW, Alu.is_equal, Alu.mult, ["cF"], ["sz"])
    ts("Ls", T.Lf[:, 0:1], T.qf[:, 12:13], T.qf[:, 13:14], None, Alu.max, None, ["sp", "sz", "Lf"], ["Ls"])
    CH = PAR["chunks"]
    NC = len(CH)
    for c, r in enumerate(CH):
        act("qf%d" % c, T.qf[:, c:c + 1], rc, ID, ["cF"], ["qf%d" % c], scale=1.0 / r, bias=-(r - 1) / (2.0 * r))
        act("qg%d" % c, T.qf[:, 4 + c:5 + c], rc, ID, ["cF"], ["qg%d" % c], bias=float(sum(CH[:c])))
    cp("qI", T.qI[:, 0:NC], T.qf[:, 0:NC], ["qf%d" % c for c in range(NC)], ["qI"])
    cp("Lq", T.Lf[:, 12:12 + 4 * NC:4], T.qI[:, 0:NC], ["qI", "Lf"], ["Lq"])
    for c, r in enumerate(CH):
        act("Lr%d" % c, T.Lf[:, 14 + 4 * c:15 + 4 * c], T.Lf[:, 12 + 4 * c:13 + 4 * c], ID, ["Lq", "qg%d" % c], ["Lr%d" % c],
            scale=-float(r), bias=T.qf[:, 4 + c:5 + c])
    act("cG4", T.cG[:, 4:5], r4, Act.Square, ["cF"], ["cG4"], bias=1.75)
    act("t85", T.cG[:, 20:21], t4, ID, ["cF"], ["t85"], bias=-8.5)
    act("Le", T.Lf[:, 2:3], T.cG[:, 4:5], ID, ["cG4", "t85", "Lf"], ["Le"], scale=8.0, bias=T.cG[:, 20:21])
    ts("own", T.cG[:, 5:6], h2, gc_, None, Alu.is_equal, None, ["cF"], ["own"])
    ts("La", T.Lf[:, 4:5], b2, 6.0, T.cG[:, 5:6], Alu.add, Alu.mult, ["cF", "own", "Lf"], ["La"])
    act("b5", T.cG[:, 6:7], b2, ID, ["cF"], ["b5"], scale=2.0, bias=5.0)
    act("Lb", T.Lf[:, 6:7], T.cG[:, 6:7], ID, ["b5", "own", "Lf"], ["Lb"], scale=T.cG[:, 5:6])
    cp("L", T.L[:], T.Lf[:], ["Ls", "Le", "La", "Lb", "Lq"] + ["Lr%d" % c for c in range(NC)], ["L"])
    act("t640", T.cG[:, 7:8], t4, ID, ["cF"], ["t640"], bias=MID + 0.25)
    t640 = T.cG[:, 7:8]
    cp("kF", T.kF[0:1, :], T.kI[0:1, :], ["kI"], ["kF"])
    add("dk", "G", lambda: G.partition_broadcast(T.dk[:], T.kF[0:1, :], 128), ["kF"], ["dk"])
    for c in range(NC):
        act("dk%d" % c, T.D16[:, 16 * c:16 * c + 16], T.dk[:].indirect(T.L[:, 12 + 4 * c:13 + 4 * c]), Act.Copy, ["dk", "L"], ["D%d" % c])
    act("p256", T.cG[:, 8:9], rc, ID, ["cF"], ["p256"], bias=2.0 * M)
    for c in range(4):
        act("h4%d" % c, T.h4[:, c:c + 1], rc, ID, ["cF"], ["h4%d" % c], scale=4.0, bias=8.0 * M + c)
    mset("nb", T.nb[:], -BIG, ["nb"])
    mset("pre0", T.pre[:], BIG, ["pre"])
    iota("FT0", T.FT[:], [[0, 512]], 0, 0, ["FT"])
    iota("Ri", T.Ri[:], [[0, 8], [1, 16], [0, 4]], 0, 0, ["Ri"])
    act("Rt0", T.Rt[:], T.Ri[:], Act.Abs, ["Ri", "neg"], ["Rt"], bias=nr)
    act("Rt1", T.Rt[:], T.Rt[:], Act.Relu, ["Rt"], ["Rt"], bias=1.0, scale=-1.0)
    act("w2", T.cG[:, 9:10], gc_, Act.Copy, ["cF"], ["w2"], scale=16.0)
    act("w3", T.cG[:, 10:11], gc_, ID, ["cF"], ["w3"], scale=16.0, bias=-float(M))
    for c, w in enumerate((float(M), -float(M), T.cG[:, 9:10], T.cG[:, 10:11])):
        act("Ru%d" % c, T.Rt[:, c:512:4], T.Rt[:, c:512:4], ID, ["Rt", "w2", "w3"], ["Ru%d" % c], scale=w)
    quant("qR", T.QR[:], T.SR[:], T.Rt[:], ["Rt"] + ["Ru%d" % c for c in range(4)], ["QR"])
    act("p16", T.cG[:, 17:18], rc, ID, ["cF"], ["p16"], scale=16.0, bias=float(SPARE))
    act("Dc", T.Dc[:], T.i16[:, 0:8], ID, ["i16", "p16"], ["Dc"], scale=16.0, bias=T.cG[:, 17:18])
    iota("A0", T.A[:], [[0, SEG[4]]], 0, 0, ["A"])
    for q in range(4):
        z = SEG[q + 1]
        act("Ad%d" % q, T.A[:, z - 20:z - 4], T.ab[:], Act.Relu, ["A", "ab"], ["Ad%d" % q], scale=-LIFT, bias=LIFT)
        act("As%d" % q, T.A[:, z - 4:z - 3], T.ab[:, 0:1], ID, ["A", "ab"], ["As%d" % q], scale=0.0, bias=-LIFT - HOLD)
        act("At%d" % q, T.A[:, z - 3:z], T.ab[:, 0:3], ID, ["A", "ab"], ["At%d" % q], scale=0.0, bias=1.0)
        if q:
            act("Az%d" % q, T.A[:, SEG[q]:SEG[q] + 1], T.ab[:, 0:1], ID, ["A", "ab"], ["Az%d" % q], scale=0.0, bias=-2 * LIFT)
    kA = ["A"] + [n + str(q) for q in range(4) for n in ("Ad", "As", "At", "Az")]
    iota("Eq", T.EQ[:], [[0, 2 * SEG[4]]], -4 * int(HOLD), 0, ["EQ%d" % i for i in range(8)] + ["sl%d" % i for i in range(8)])
    iota("HG", T.HG[:], [[0, 32]], 0, 0, ["g1", "g2", "g3"])
    iota("Zt", T.Zt[:], [[0, 512]], 0, 0, ["Zt"])
    for b in range(4):
        add("Et%d" % b, "G", lambda b=b: G.affine_select(T.Et[:, 512 * b:512 * b + 512], T.Zt[:], [[-4, 128], [-1, 4]], Alu.not_equal,
                                                         1.0, b, 4), ["Zt"], ["Et%d" % b])
        quant("qE%d" % b, T.QE[:, M * b:M * b + M], T.SE[:, M * b:M * b + M], T.Et[:, 512 * b:512 * b + 512], ["Et%d" % b], ["QE%d" % b])

    cp("Qg", T.Qg[:].bitcast(dt.uint32), T.Qu[:].bitcast(dt.uint32).indirect(T.uL[:]), ["Qu", "uL"], ["Qg"])
    act("Sg", T.Sg[:], T.Su[:].indirect(T.uL[:]), Act.Copy, ["Qu", "uL"], ["Sg"])
    quant("qv", T.Qv[:], T.Sv[:], T.vt[:], ["vt"], ["Qv"])

    kX, kY = ["X0", "X1"], ["Y0", "Y1", "Y2", "Y3"]
    kG = ["Qg", "Sg"]

    def quant_x():
        quant("qx1", T.QA[:, HI:C], T.SA[:, HI:C], T.Xt[:, 4 * HI + GAP:XE], ["X1"], ["QX1"])
        quant("qx0", T.QA[:, 0:HI], T.SA[:, 0:HI], T.Xt[:, 0:4 * HI], ["X0"], ["QX0"])

    def quant_y():
        quant("qy", T.QA[:, C:C + M], T.SA[:, C:C + M], T.Yt[:], kY, ["QY"])

    def new_y(t, rb, db):
        q, s, k = T["QL%d" % t][:], T["SL%d" % t][:], "land%d" % t
        add("land", "A", None, ["sentS%d" % t, "sentQ%d" % t], [k], "arr%d" % t, 2 * ne)
        for b in range(4):
            mm("mW%d" % b, ps(rb[b], 0, M), T.QW[:, M * b:M * b + M], T.SW[:, M * b:M * b + M], q, s, ["QW", "SW", k], ["B%d" % rb[b]])
            mm("mE%d" % b, ps(db[b], 0, M), T.QE[:, M * b:M * b + M], T.SE[:, M * b:M * b + M], q, s, ["QE%d" % b, k], ["B%d" % db[b]])
            act("Rr%d" % b, T.Rr[:, M * b:M * b + M], ps(rb[b], 0, M), Act.Relu, ["B%d" % rb[b]], ["Rr%d" % b], scale=0.03125)
            tt("Y%d" % b, T.Yt[:, b:512:4], T.Rr[:, M * b:M * b + M], ps(db[b], 0, M), Alu.add, ["Rr%d" % b, "B%d" % db[b]], ["Y%d" % b])

    for t in range(R):
        at[0] = t
        QZ, SZ, QH, SH = T["QZ%d" % t], T["SZ%d" % t], T["QH%d" % t], T["SH%d" % t]
        quant_x()
        mm("mH", ps(3, 0, C - HI), T.Qg[:], T.Sg[:], T.QA[:, HI:C], T.SA[:, HI:C], kG + ["QX1"], ["B3"])
        mm("m1", ps(1, 0, C), T.Qg[:], T.Sg[:], T.QA[:, 0:C], T.SA[:, 0:C], kG + ["QX0", "QX1"], ["B1"])
        mm("m0", ps(0, 0, C), T.Qg[:], T.Sg[:], T.QA[:, 0:C], T.SA[:, 0:C], kG + ["QX0", "QX1"], ["B0"])
        act("Xh", T.Xh[:], T.Xt[:, 0:XE], Act.Copy, kX + ["gap"], ["Xh"], scale=0.5)
        tt("dH", T.d1[:, HI:C], ps(3, 0, C - HI), T.Mk[:, HI:C], Alu.add, ["B3", "Mk"], ["dH"])
        scan("WH", T.W[:, HI:C], T.K16[:, HI:C], T.d1[:, HI:C], -BIG, Alu.min, Alu.max, ["K16", "dH"], ["WH"])
        tt("dL", T.d1[:, 0:HI], ps(0, 0, HI), T.Mk[:, 0:HI], Alu.add, ["B0", "Mk"], ["dL"])
        scan("WL", T.W[:, 0:HI], T.K16[:, 0:HI], T.d1[:, 0:HI], -BIG, Alu.min, Alu.max, ["K16", "dL"], ["WL"])
        diag = T.CT[:, 0:4 * C:4]
        tt("dg", diag, T.W[:], ps(0, 0, C), Alu.is_ge, ["WH", "WL", "B0"], ["CTd"])
        scan("rd", T.rd[:], T.keep[:], diag, 0.0, Alu.mult, Alu.add, ["keep", "CTd"], ["rd"])
        tt("t1", T.tr[:], T.RC[:], T.rd[:, 15:C:16], Alu.subtract, ["RC", "rd"], ["t1"])
        for rows, width, first in TILES:
            for slot, i in enumerate(rows):
                if i == "d":
                    continue
                w = 16 * i
                out = T.CT[:, 4 * first + slot:4 * (first + w):4]
                key, kw = "CT%d" % i, "WH" if w >= HI else "WL"
                own = T.W[:, w + 15:w + 16]
                if i > VR:
                    sk, sg = "sg%d" % i, T.sg[:, C * (i - VR - 1):C * (i - VR - 1) + w]
                    act("a%d" % i, sg, ps(1, 0, w), Act.Sign, ["B1", kw], [sk], bias=own, scale=-1.0)
                    act("b%d" % i, out, sg, Act.Relu, [sk], [key, "RS%d" % i], accum_out=T.RS[:, i:i + 1])
                else:
                    ts("c%d" % i, out, ps(0, 0, w), own, None, Alu.is_lt, None, ["B0", kw], [key])
        for c in range(4):
            scan("s%d" % c, T.rs[:, SW * c:SW * c + SW], T.kq[:], T.CT[:, 4 * 576 + c:4 * 960:4], 0.0, Alu.mult, Alu.subtract,
                 ["kq"] + ["CT%d" % (c + 1 + 4 * a) for a in range(3)], ["rs%d" % c])
        tt("ua", T.D1[:, 15:256:16], T.rs[:].indirect(LS), T.tr[:, 0:16], Alu.add,
           ["t1", "L", "rsz"] + ["rs%d" % c for c in range(4)], ["uu"])
        tt("ub", T.D1[:, 16 * VR + 31:C:16], T.tr[:, VR + 1:NI], T.RS[:, VR + 1:NI], Alu.subtract,
           ["t1"] + ["RS%d" % i for i in range(VR + 1, NI)], ["uu"])
        for u in range(3):
            rows, width, first = TILES[u]
            quant("q%d" % u, T.QC[:, first:first + width], T.SC[:, first:first + width], T.CT[:, 4 * first:4 * (first + width)],
                  ["CT%s" % str(i) for i in rows], ["QC%d" % u])
        quant("q3", T.QC[:, 768:960], T.SC[:, 768:960], T.CT[:, 4 * 768:4 * 960], ["CT%d" % i for i in range(1, 9)], ["QC3", "QC4"])
        for z, u in enumerate(PAR["pe"]):
            first, width = TILES[u][2], max(TILES[u][1], M)
            mm("mC%d" % u, ps(2, 0, width), T.QG[:], T.SG[:], T.QC[:, first:first + width], T.SC[:, first:first + width],
               ["QG", "QC%d" % u], ["B2"], start=(z == 0), stop=(z == 4))
        if t > 0:
            new_y(t - 1, [4, 6, 4, 6], [5, 7, 5, 7])
        quant_y()
        act("Yh", T.Yh[:], T.Yt[:], Act.Copy, kY, ["Yh"], scale=0.5)
        mm("mS", ps(3, 0, M), T.Qg[:], T.Sg[:], T.QA[:, C:C + M], T.SA[:, C:C + M], kG + ["QY"], ["B3"])
        tt("d3", T.d3[:], ps(3, 0, M), T.Mk[:, 0:M], Alu.add, ["B3", "Mk"], ["d3"])
        scan("Wm", T.Wm[:], T.K16[:, 0:M], T.d3[:], -BIG, Alu.min, Alu.max, ["K16", "d3"], ["Wm"])
        scan("W2", T.W2[:], ps(2, 0, C), T.D1[:], HOLD, Alu.min, Alu.add, ["uu", "B2"], ["W2"])
        ts("roff", T.roff[:], T.W2[:, 15:C:16], T.cG[:, 15:16], None, Alu.add, None, ["W2", "z2"], ["roff"])
        cp("o2a", T.o2[:, 0:C].indirect(T.roff[:]), T.iO[:], ["roff", "iO"], ["o2a"])
        cp("o2b", T.o2[:, C:2 * C], T.o2[:, 0:C], ["o2a"], ["o2b"])
        for i in range(8):
            own = T.Wm[:, 16 * i + 15:16 * i + 16]
            sk, sg = "sm%d" % i, T.sm[:, C * i:C * i + C]
            if i in PAR["vmsg"]:
                ts("f%d" % i, sg, ps(0, 0, C), own, None, Alu.is_gt, None, ["B0", "Wm"], [sk])
                scan("g%d" % i, T.vb[:, C * i:C * i + C], T.kq[:, 0:C], sg, 0.0, Alu.mult, Alu.add, [sk, "kq"], ["vb%d" % i])
                tt("n%d" % i, T.n[:, i:i + 1], T.vb[:, C * i + 191:C * i + 192], T.vb[:, C * i + C - 1:C * i + C], Alu.add,
                   ["vb%d" % i], ["n%d" % i])
            else:
                act("f%d" % i, sg, ps(1, 0, C), Act.Sign, ["B1", "Wm"], [sk], bias=own, scale=-1.0)
                act("n%d" % i, sg, sg, Act.Relu, [sk], ["n%d" % i, sk], scale=-1.0, accum_out=T.n[:, i:i + 1])
        for h, r in enumerate(CH):
            i0, n = sum(CH[:h]), 64 * r
            z0, pos, pk = 16 * i0, T.pos[:, 16 * h:16 * h + 16], "pof%d" % h
            tt("pos%d" % h, pos, T.n[:, 0:i0 + r].indirect(T.L[:, 14 + 4 * h:15 + 4 * h]), T.D16[:, 16 * h:16 * h + 16], Alu.add,
               ["n%d" % i for i in range(i0 + r)] + ["L", "D%d" % h], ["pos%d" % h])
            cp(pk, T.pof[:, 16 * h:16 * h + 4 * r], T.pos[:, 16 * h:16 * h + 4 * r], ["pos%d" % h], [pk])
            for name, ka, kz in ((("a", 0, 1), ("b", 1, F)) if h < PAR["cut"] else (("", 0, F),)):
                a, z, u = 16 * r * ka, 16 * r * kz, "%d%s" % (h, name)
                of, er = T.pof[:, 16 * h + r * ka:16 * h + r * kz], T.er[:, 4 * z0 + a:4 * z0 + z]
                if PAR["eg"][h] == "V":
                    cp("er" + u, er, T.o2[:].indirect(of), ["o2a", "o2b", pk], ["er" + u])
                else:
                    act("er" + u, er, T.o2[:].indirect(of), Act.Copy, ["o2a", "o2b", pk], ["er" + u])
                scan("e4" + u, T.e4[:, 4 * z0 + a:4 * z0 + z], T.A4[:, a:z], er, 0.0, Alu.mult, Alu.add, ["A4", "er" + u], ["e4" + u])
                ts("zof" + u, T.zof[:, z0 + a // 4:z0 + z // 4], T.e4[:, 4 * z0 + a + 3:4 * z0 + z:4], t640, None, Alu.add, None,
                   ["e4" + u, "t640"], ["zof" + u])
            for k in range(F):
                a, b = 512 * k + 64 * i0, 64 * i0 + 16 * r * k
                u = "%d%s" % (h, "ab"[min(k, 1)] if h < PAR["cut"] else "")
                tt("Z%d%d" % (k, h), T.Z[:, a:a + n], T.Xh[:].indirect(T.zof[:, z0 + 4 * r * k:z0 + 4 * r * (k + 1)]),
                   T.Yh[:, 64 * i0:64 * i0 + n], Alu.add, ["Xh", "Yh", "zof" + u], ["Z%d%d" % (k, h)])
                act("ec%d%d" % (k, h), T.erep[:, M * k + 16 * i0:M * k + 16 * (i0 + r)], T.er[:, b:b + 16 * r], ID,
                    ["er" + u, "ud"], ["ec%d%d" % (k, h)], scale=ud)
        for k in range(F):
            quant("qz%d" % k, QZ[:, M * k:M * k + M], SZ[:, M * k:M * k + M], T.Z[:, 512 * k:512 * k + 512],
                  ["Z%d%d" % (k, h) for h in range(NC)], ["QZ%d_%d" % (t, k)])
            mm("mZ%d" % k, ps(4 + k, 0, M), QZ[:, M * k:M * k + M], SZ[:, M * k:M * k + M], T.Qu[:], T.Su[:],
               ["QZ%d_%d" % (t, k), "Qu"], ["B%d" % (4 + k)])
        for k in range(F):
            scan("EW%d" % k, T.EW[:, M * k:M * k + M], T.A16[:], T.erep[:, M * k:M * k + M], 0.0, Alu.mult, Alu.add,
                 ["A16"] + ["ec%d%d" % (k, h) for h in range(NC)], ["EW%d" % k])
        cp("H0", T.HD[:, 3:32:4], T.EW[:, 15:M:16], ["EW0"], ["H0"])
        for k in range(1, F):
            tt("H%d" % k, T.HD[:, 3 - k:32:4], T.EW[:, M * k + 15:M * k + M:16], T.EW[:, M * k - M + 15:M * k:16], Alu.subtract,
               ["EW%d" % k, "EW%d" % (k - 1)], ["H%d" % k])
        kQZ = ["QZ%d_%d" % (t, k) for k in range(F)]
        kZ = ["Z%d%d" % (k, h) for k in range(F) for h in range(NC)]
        kE = ["ec%d%d" % (k, h) for k in range(F) for h in range(NC)]
        scan("pre", T.pre[:, 5:9], T.ps[:, 2049:4096:512], T.nb[:], -BIG, Alu.max, Alu.max, ["B4", "B5", "B6", "B7", "nb"], ["pre"])
        ts("Fa", T.FT[:, 0:32:2], T.pre[:, 0:8].indirect(LFa), T.pre[:, 8:9], None, Alu.is_lt, None, ["pre", "L", "FT"], ["Fa"])
        ts("Fb", T.FT[:, 1:32:2], T.pre[:, 0:8].indirect(LFb), T.pre[:, 8:9], None, Alu.is_equal, None, ["pre", "L", "FT"], ["Fb"])
        quant("qF", T.QF[:], T.SF[:], T.FT[:], ["Fa", "Fb"], ["QF"])
        mm("mF", ps(3, 0, M), T.QR[:], T.SR[:], T.QF[:], T.SF[:], ["QR", "QF"], ["B3"])
        ts("ziu", T.ziu[:], ps(3, 0, 8), T.cG[:, 8:9], None, Alu.add, None, ["B3", "p256"], ["ziu"])
        for c in range(4):
            ts("hof%d" % c, T.hof[:, c:32:4], ps(3, 0, 8), 4.0, T.h4[:, c:c + 1], Alu.mult, Alu.add, ["B3", "h4%d" % c], ["hof%d" % c])
        cp("QH", QH[:].bitcast(dt.uint32), QZ[:].bitcast(dt.uint32).indirect(T.ziu[:]), kQZ + ["ziu"], ["QH%d" % t])
        act("SH", SH[:], SZ[:].indirect(T.ziu[:]), Act.Copy, kQZ + ["ziu"], ["SH%d" % t])
        arr = T.sem["arr%d" % t]
        add("sendS", "G", lambda a=T["SL%d" % t][:], b=SH[:], s=arr: G.remote_dma(a, b, s, T.sem.sent, pid, rid, mask),
            ["SH%d" % t], ["sentS%d" % t], "remote")
        add("sendQ", "G", lambda a=T["QL%d" % t][:].bitcast(dt.uint8), b=QH[:].bitcast(dt.uint8), s=arr:
            G.remote_dma(a, b, s, T.sem.sent, pid, rid, mask), ["QH%d" % t], ["sentQ%d" % t], "remote")
        act("oka", T.jk[:, 0:16], T.FT[:, 0:32:2], Act.Copy, ["Fa"], ["oka"], accum_out=T.okc[:, 4:5])
        act("okb", T.jk[:, 16:24], T.FT[:, 1:32:4], ID, ["Fb"], ["okb"], scale=-1.0, bias=0.125, accum_out=T.okc[:, 5:6])
        act("okc", T.okc[:, t:t + 1], T.okc[:, 4:5], ID, ["oka", "okb"], ["okc%d" % t], bias=T.okc[:, 5:6])
        dma("ok", "Y", T.ok[t], T.okc[:, t:t + 1], ["okc%d" % t], [], "outh")
        act("ew", T.ew[:], T.erep[:].indirect(T.ziu[:]), ID, kE + ["ziu", "wb"], ["ew"], scale=T.cG[:, 18:19])
        for k in range(1, F):
            ts("G%d" % k, T.HG[:, 4 - k:32:4], ps(3, 0, 8), float(M * k - 2 * M), None, Alu.is_ge, None, ["B3"], ["g%d" % k])
        scan("OW", T.OW[:], T.HG[:], T.HD[:], 0.0, Alu.mult, Alu.add, ["g1", "g2", "g3", "H0", "H1", "H2", "H3"], ["OW"])
        for h in (1, 0):
            act("Hp%d" % h, T.Hp[:, 256 * h:256 * h + 256], T.Z[:].indirect(T.hof[:, 16 * h:16 * h + 16]), Act.Copy,
                kZ + ["hof%d" % c for c in range(4)], ["Hp%d" % h])
            a, rows = SEG[4] * h, range(4 * h, 4 * h + 4)
            for i in rows:
                b, z, own = a + SEG[i % 4], a + SEG[i % 4 + 1] - 4, T.OW[:, 4 * i + 3:4 * i + 4]
                ts("EQ%d" % i, T.EQ[:, b:z], T.ew[:, 64 * h:16 * i + 16], own, T.Dc[:, i:i + 1], Alu.is_equal, Alu.mult,
                   ["ew", "OW", "Dc"], ["EQ%d" % i])
                act("sl%d" % i, T.EQ[:, z:z + 1], own, Act.Copy, ["OW"], ["sl%d" % i])
            scan("st%d" % h, T.st[:, a:a + SEG[4]], T.A[:], T.EQ[:, a:a + SEG[4]], 0.0, Alu.add, Alu.max,
                 kA + ["EQ%d" % i for i in rows] + ["sl%d" % i for i in rows], ["st%d" % h])
            ts("xo%d" % h, T.xof[:, 16 * h:16 * h + 16], T.st[:, a:a + SEG[4]].indirect(LEND), float(MID), None, Alu.add, None,
               ["st%d" % h, "L"], ["xo%d" % h])
            cp("X" if h == 0 else "XA", T.Xt[:].indirect(T.xof[:, 16 * h:16 * h + 16]), T.Hp[:, 256 * h:256 * h + 256],
               ["xo%d" % h, "Hp%d" % h, "gap"], kX)

    at[1] = "!"
    new_y(R - 1, [4, 5, 6, 7], [0, 1, 2, 3])
    quant_y()
    quant_x()
    for key, a, z, b in (("Y", C, C + M, 4), ("X1", HI, C, 5), ("X0", 0, HI, 6)):
        mm("mv" + key, ps(b, 0, z - a), T.Qv[:], T.Sv[:], T.QA[:, a:z], T.SA[:, a:z], ["Qv", "Q" + key], ["B%d" % b])
        act("ys" + key, T.ysb[:, a:z], ps(b, 0, z - a), Act.Copy, ["B%d" % b], ["ysb" + key])
        dma("oy" + key, "S", T.y[:, a:z], T.ysb[:, a:z], ["ysb" + key], [], "outh")
    for key, a, z, k in (("Y", C, C + M, ["QY"]), ("X", 0, C, ["QX0", "QX1"])):
        dma("oc" + key, "Y", T.oc[:, 4 * a:4 * z], T.QA[:, a:z].bitcast(dt.uint8), k, [], "outh")
    for k in range(4):
        dma("os%d" % k, "G" if k == 3 else "Y", T.osc[4 * k:4 * k + 4, :], T.SA[32 * k:32 * k + 4, :], ["QX0", "QX1", "QY"], [],
            "outg" if k == 3 else "outh")
    return ops, ne


def depend(ops):
    writer, readers = {}, {}
    for i, o in enumerate(ops):
        d = set()
        for k in o["r"]:
            if k in writer:
                d.add(writer[k])
            if k[0] == "B" and len(k) == 2:
                d.update(j for j in readers.get(k, []) if ops[j]["e"] != o["e"])
        for k in o["w"]:
            if k in writer:
                d.add(writer[k])
            d.update(readers.get(k, []))
        d.discard(i)
        o["d"] = sorted(d)
        for k in o["r"]:
            readers.setdefault(k, []).append(i)
        for k in o["w"]:
            writer[k] = i
            readers[k] = []


def merge(ops):
    q = {}
    for i, o in enumerate(ops):
        q.setdefault(o["e"], []).append(i)
    for e in q:
        q[e].sort(key=lambda i: (ops[i]["at"], ORDER[ops[i]["at"]][e].split().index(ops[i]["name"])))
    head, done, order = {e: 0 for e in q}, set(), []
    while len(order) < len(ops):
        moved = False
        for e in q:
            while head[e] < len(q[e]) and all(j in done for j in ops[q[e][head[e]]]["d"]):
                done.add(q[e][head[e]])
                order.append(q[e][head[e]])
                head[e] += 1
                moved = True
        assert moved
    return order


def emit(g, T, ops, order, ne):
    queue = {"V": g.vector, "S": g.scalar, "P": g.tensor, "G": g, "Y": g.sync}
    seq, cnt = {}, {}
    place = {i: k for k, i in enumerate(order)}
    for i in order:
        o = ops[i]
        if o["sem"] is None:
            cnt[o["e"]] = cnt.get(o["e"], 0) + 1
            seq[i] = cnt[o["e"]]
    known = {e: {} for e in queue}
    clock, waits, wanted = {}, {}, set()
    for i in order:
        o = ops[i]
        e = o["e"]
        if e == "A":
            clock[i] = {o["sem"]: 1}
            continue
        kn, ws = known[e], []
        for j in sorted(o["d"], key=lambda j: -place[j]):
            p = ops[j]
            if p["e"] == "P" and e == "P":
                continue
            key, val = (p["e"], seq[j]) if p["sem"] is None else (p["sem"], 1)
            if kn.get(key, 0) >= val:
                continue
            ws.append(j)
            wanted.add(j)
            for k, v in clock[j].items():
                if kn.get(k, 0) < v:
                    kn[k] = v
        waits[i] = ws
        c = dict(kn)
        if o["sem"] is None:
            c[e] = seq[i]
        else:
            c[o["sem"]] = 1
        clock[i] = c
    last = {}
    for i in order:
        if ops[i]["sem"] is None:
            last[ops[i]["e"]] = i
    wanted.update(last.values())
    num, cnt, total = {}, {}, {}
    for i in order:
        if ops[i]["sem"] is None and i in wanted:
            cnt[ops[i]["e"]] = cnt.get(ops[i]["e"], 0) + 1
            num[i] = cnt[ops[i]["e"]]
    for i in order:
        o = ops[i]
        if o["e"] == "A":
            total[o["sem"]] = o["n"]
            continue
        q = queue[o["e"]]
        for j in waits[i]:
            p = ops[j]
            if p["sem"] is None:
                q.wait_ge(T.sem["c" + p["e"]], num[j])
            else:
                q.wait_ge(T.sem[p["sem"]], p["n"])
        ins = o["f"]()
        if o["sem"] is None:
            if i in wanted:
                ins.then_inc(T.sem["c" + o["e"]], 1)
        elif o["sem"] == "remote":
            total["sent"] = total.get("sent", 0) + ne
        else:
            ins.then_inc(T.sem[o["sem"]], 16)
            total[o["sem"]] = total.get(o["sem"], 0) + 16
    for e, v in cnt.items():
        total["c" + e] = v
    for k in sorted(total, key=lambda k: k.startswith("out")):
        g.wait_ge(T.sem[k], total[k])


def rank_program(g, core, T, topo):
    if T.rank_of(core) is None:
        return
    ops, ne = build(g, core, T, topo)
    depend(ops)
    emit(g, T, ops, merge(ops), ne)
